import numpy as np, ml_dtypes
CORES = [16,17,18,19,32,33,34,35]
N = 8
BF = ml_dtypes.bfloat16
def gentries(a):
    return np.ascontiguousarray(a.reshape(8, 16, -1).transpose(0, 2, 1)).reshape(8, -1)
def gtable(e):
    e = np.asarray(e); return np.ascontiguousarray(e.reshape(8, -1, 16).transpose(0, 2, 1)).reshape(128, -1).astype(np.int32)
W, P, RO = 2560, 128, 3
def parts(rng):
    X = rng.integers(0, 128, (N, 8, 16, W)); G = rng.integers(-127, 128, (N, 8, 16, W)); E = rng.integers(0, 2 ** 20, (N, 8, W)); B = rng.integers(0, W, (N, 8, 16, W))
    return X, G, E, B, rng.integers(0, W, (N, 8, P, 16)), rng.integers(0, W, (N, 8, P, 16)), rng.integers(0, 9, (N, 8, P, 16))
def pack(X, G, E, B, a, b, l):
    return {"xrec": np.ascontiguousarray(X.reshape(N, 128, W)).astype(np.float32).astype(BF), "grec": np.ascontiguousarray(G.reshape(N, 128, W)).astype(np.float32).astype(BF),
            "erec": np.ascontiguousarray(E.reshape(N, 8, W)).astype(np.int32), "nbr": np.ascontiguousarray(B.reshape(N, 128, W)).astype(np.int32),
            "pa": np.stack([gtable(t.reshape(8, -1)) for t in a]), "pb": np.stack([gtable(t.reshape(8, -1)) for t in b]), "lam": np.stack([gtable(t.reshape(8, -1)) for t in l])}
def setup_inputs(rng):
    X, G, E, B, a, b, l = parts(rng)
    X[:, 1::2] = (X[:, 1::2] * rng.choice(np.array([1, 4, 16, 16]), (N, 4, 1, W))) >> 4
    E[:, 2::3] &= 2 ** 20 - 2 ** 18
    r = rng.integers(0, W, (N, 8, 1)); a[:, :, 5] = r; b[:, :, 5] = r
    return pack(X, G, E, B, a, b, l)
def setup_inputs_corners(rng):
    X, G, E, B, a, b, l = parts(rng); h = P // 2; sh = int(rng.integers(0, 8)); J = np.arange(16)
    for q in range(N):
        for g in range(8):
            c = (g + q + sh) % 8
            if c == 0:
                z = h // 2; r = rng.integers(0, W, (z, 1)); a[q, g, :z] = r; b[q, g, :z] = r
                rec = rng.permutation(W)[:16]; X[q, g][:, rec] = X[q, g][:, rec[:1]]
                a[q, g, z:h] = rec[rng.integers(0, 16, (h - z, 16))]; b[q, g, z:h] = rec[rng.integers(0, 16, (h - z, 16))]
            elif c == 1:
                B[q, g] = np.arange(W); l[q, g] = 8 * rng.integers(0, 2, (P, 16))
            elif c == 2:
                B[q, g] = (W - 1) * rng.integers(0, 2, (16, W)); l[q, g] = 8 * rng.integers(0, 2, (P, 16))
                a[q, g, :, ::3] = (W - 1) * rng.integers(0, 2, (P, 6)); b[q, g, :, 1::3] = (W - 1) * rng.integers(0, 2, (P, 5))
            elif c == 3:
                l[q, g] = rng.integers(3, 6, (P, 16))
                rec = rng.permutation(W)[:48].reshape(3, 16); o = rng.permutation(16)
                v = 2 * rng.integers(51, 62, (16, 16)); v[o[1]] = v[o[0]]; v[o[2]] = v[o[0]] + 4 * rng.integers(0, 2, 16) - 2
                s = v.copy(); s[o[0]] += 1; s[o[1]] -= 1; u = v >> 1; u[o[0]] += 1; u[o[2]] -= 1
                X[q, g][:, rec[0]] = 0; X[q, g][:, rec[1]] = v; X[q, g][:, rec[2]] = s; G[q, g][:, rec[0]] = u; E[q, g, rec[2]] = 2 ** 20 - 1
                i = np.arange(h) % 16; a[q, g, :h, 0] = rec[0][i]; b[q, g, :h, 0] = rec[1][i]; l[q, g, :h, 0] = 0
                a[q, g, :h, 1] = rec[2][i]; b[q, g, :h, 1] = rec[2][i]
            elif c == 4:
                if q % 2 == 0: E[q, g] = rng.integers(0, 2 ** 20)
                else: E[q, g] = 4096 * int(rng.integers(128, 256)) + 1025 + 8 * int(rng.integers(0, 127)) + rng.integers(0, 2, W)
            elif c == 5:
                G[q, g] = 0; r = rng.integers(0, W, (h, 2))[:, J % 2]; a[q, g, :h] = r; b[q, g, :h] = r
                rec = rng.permutation(W)[:128].reshape(8, 16); inc = np.zeros((16, 16), np.int64); inc[:, 1] = 1; size = rng.permutation(20)[:8] + 1
                for i in range(2, 16): inc[i, i] = 3 if i == 15 else 2
                for i in range(8): X[q, g][:, rec[i]] = 40 + int(size[i]) * np.add.accumulate(inc, axis=1)
                k = rec[np.arange(P - h) % 8]; a[q, g, h:] = k; b[q, g, h:] = k
            elif c == 6:
                r = rng.integers(0, W, (P, 2)); a[q, g] = np.take_along_axis(r, rng.integers(0, 2, (P, 16)), 1); b[q, g] = np.take_along_axis(r, rng.integers(0, 2, (P, 16)), 1)
            else:
                u = rng.integers(0, W, (P, 2)); cut = rng.integers(0, 15, (P, 1)); r = np.where(J <= cut, u[:, :1], u[:, 1:]); a[q, g] = r; k = b[q, g].copy(); b[q, g] = r
                b[q, g, h:, 0] = k[h:, 0]; b[q, g, h:, 15] = k[h:, 15]; l[q, g, h:, 0] = 0; l[q, g, h:, 15] = 0
    return pack(X, G, E, B, a, b, l)
def setup_inputs_crowd(rng):
    X, G, E, B, a, b, l = parts(rng); sh = int(rng.integers(0, 8)); J = np.arange(16)
    for q in range(N):
        for g in range(8):
            c = (g + sh) % 8; one = int(rng.choice(np.array([0, W - 1, int(rng.integers(0, W))])))
            if c < 2:
                B[q, g] = one; l[q, g] = 8 * rng.integers(0, 2, (P, 16))
                if c == 1: B[q, g, int(rng.integers(0, 16)), a[q, g, P - 1, 15]] = (one + 1) % W
            elif c in (2, 3, 6):
                cut = 14 if c == 2 else 13 if c == 3 else 0
                u = rng.integers(0, W, (P, 2)); r = np.where(J <= cut, u[:, :1], u[:, 1:]); k = b[q, g].copy(); a[q, g] = r; b[q, g] = r
                b[q, g, 1::2, 0] = k[1::2, 0]; b[q, g, 1::2, 15] = k[1::2, 15]; l[q, g, 1::2, 0] = 0; l[q, g, 1::2, 15] = 0
            elif c == 4:
                a[q, g] = one; b[q, g] = one; i = int(rng.integers(0, 16)); a[q, g, P - 1, i] = (one + 1) % W; b[q, g, P - 1, i] = (one + 2) % W
            elif c == 5:
                r = rng.integers(0, W, 4); a[q, g] = r[rng.integers(0, 4, (P, 16))]; b[q, g] = r[rng.integers(0, 4, (P, 16))]; B[q, g] = r[rng.integers(0, 4, (16, W))]
            else:
                b[q, g] = one; l[q, g] = 8
    return pack(X, G, E, B, a, b, l)
def setup_inputs_ends(rng):
    X, G, E, B, a, b, l = parts(rng)
    X = 127 * rng.integers(0, 2, X.shape); G = 254 * rng.integers(0, 2, G.shape) - 127; E = (2 ** 20 - 1) * rng.integers(0, 2, E.shape)
    E[:, :, 0] = (2 ** 20 - 1) * rng.integers(0, 2, (N, 8)); E[:, ::2, W - 1] = 2 ** 20 - 1 - E[:, ::2, 0]
    B = np.where(rng.random(B.shape) < 0.3, B, (W - 1) * rng.integers(0, 2, B.shape))
    a = np.where(rng.random(a.shape) < 0.33, a, (W - 1) * rng.integers(0, 2, a.shape)); b = np.where(rng.random(b.shape) < 0.33, b, (W - 1) * rng.integers(0, 2, b.shape))
    l = np.where(rng.random(l.shape) < 0.2, l, 8 * rng.integers(0, 2, l.shape)); alt = (W - 1) * (np.arange(16) % 2)
    for g in (0, 2, 5, 7):
        o = rng.integers(0, 2, (N, 1)); X[:, g, :, 0] = 127 * o; X[:, g, :, W - 1] = 127 * (1 - o)
        s = 254 * rng.integers(0, 2, (N, 2)) - 127
        if g == 7: s[:] = 127
        if g == 0: s[:] = -127
        G[:, g, :, 0] = s[:, :1]; G[:, g, :, W - 1] = s[:, 1:]
        a[:, g, 7::8] = alt; b[:, g, 7::8] = alt
    return pack(X, G, E, B, a, b, l)
def setup_inputs_spread(rng):
    X, G, E, B, a, b, l = parts(rng)
    X = (np.exp2(7 * rng.random((N, 8, 1, W))) * rng.random(X.shape)).astype(np.int64); X[:, 1::2] = 127 - X[:, 1::2]
    G = np.minimum((np.exp2(7 * rng.random((N, 8, 1, W))) * rng.random(G.shape)).astype(np.int64), 127) * (2 * rng.integers(0, 2, G.shape) - 1)
    E = np.minimum(np.exp2(20 * rng.random(E.shape)).astype(np.int64) - 1, 2 ** 20 - 1)
    a = np.minimum((W * rng.random(a.shape) ** 3).astype(np.int64), W - 1); b = np.minimum((W * rng.random(b.shape) ** 2).astype(np.int64), W - 1)
    B = W - 1 - np.minimum((W * rng.random(B.shape) ** 3).astype(np.int64), W - 1)
    l = rng.choice(np.array([0, 0, 0, 1, 2, 3, 4, 4, 5, 6, 7, 8, 8, 8]), l.shape)
    return pack(np.minimum(np.maximum(X, 0), 127), G, E, B, a, b, l)
def check_inputs(d):
    bad = []
    for k, lo, hi in (("xrec", 0, 127), ("grec", -127, 127), ("erec", 0, 2 ** 20 - 1), ("nbr", 0, W - 1), ("pa", 0, W - 1), ("pb", 0, W - 1), ("lam", 0, 8)):
        v = np.asarray(d[k]).astype(np.float64)
        if not (np.min(v) >= lo and np.max(v) <= hi): bad.append("range of " + k)
        elif not np.all(v == np.rint(v)): bad.append("whole numbers in " + k)
    return bad
def pick(t, i):
    return np.take_along_axis(t, i.reshape(N, 8, 1, P * 16), 3).reshape(N, 8, 16, P, 16)
def dot(u, v):
    return np.add.reduce(u * v, axis=2)
def reference(xrec, grec, erec, nbr, pa, pb, lam):
    X = xrec.astype(np.float32).astype(np.int64).reshape(N, 8, 16, W); G = grec.astype(np.float32).astype(np.int64).reshape(N, 8, 16, W)
    E = erec.astype(np.int64); B = nbr.astype(np.int64).reshape(N, 8, 16, W); J = np.arange(16); mid = (J > 0) & (J < 15)
    a, b, l = [np.stack([gentries(t) for t in v]).astype(np.int64).reshape(N, 8, P, 16) for v in (pa, pb, lam)]
    for rnd in range(RO):
        w = l[:, :, None]; xa = pick(X, a); d = pick(X, b) - xa; R = 8 * xa + w * d
        g = (8 - w) * pick(G, a) + w * pick(G, b)
        ea = np.take_along_axis(E, a.reshape(N, 8, P * 16), 2).reshape(N, 8, P, 16); eb = np.take_along_axis(E, b.reshape(N, 8, P * 16), 2).reshape(N, 8, P, 16)
        e = (8 - l) * ea + l * eb
        Rx = np.concatenate([np.roll(R[..., 15:], 1, axis=0), R, np.roll(R[..., :1], -1, axis=0)], axis=4)
        ex = np.concatenate([np.roll(e[..., 15:], 1, axis=0), e, np.roll(e[..., :1], -1, axis=0)], axis=3)
        D = Rx[..., 1:] - Rx[..., :-1]; fwd = ex[..., 2:] >= ex[..., :-2]
        tau = np.where(fwd[:, :, None], D[..., 1:], D[..., :-1])
        p = dot(g, d).astype(np.float32) * dot(tau, tau).astype(np.float32)
        q = dot(g, tau).astype(np.float32) * dot(tau, d).astype(np.float32)
        l = l - (p > q).astype(np.int64) + (p < q).astype(np.int64)
        up = l > 8; dn = l < 0; z = np.where(up, b, a)
        n = np.take_along_axis(B, z.transpose(0, 1, 3, 2), 3).transpose(0, 1, 3, 2)
        a, b, l = np.where(up, b, np.where(dn, n, a)), np.where(up, n, np.where(dn, a, b)), np.where(up, 1, np.where(dn, 7, l))
        xa = pick(X, a); R = 8 * xa + l[:, :, None] * (pick(X, b) - xa)
        H = np.add.reduce(np.abs(R[..., 1:] - R[..., :-1]), axis=2)
        C = np.concatenate([np.zeros((N, 8, P, 1), np.int64), np.add.accumulate(H, axis=3)], axis=3); S = C[..., 15:]
        c = np.where(l <= 4, a, b)
        j = np.add.reduce((15 * C[..., None, :15] <= J[:, None] * S[..., None]).astype(np.int64), axis=4) - 1
        lo = np.take_along_axis(C, j, 3); gap = 15 * (np.take_along_axis(C, j + 1, 3) - lo); rest = 16 * (J * S - 15 * lo); m = np.zeros((N, 8, P, 16), np.int64)
        for i in range(1, 9): m = m + ((2 * i - 1) * gap <= rest)
        a, b, l = np.where(mid, np.take_along_axis(c, j, 3), a), np.where(mid, np.take_along_axis(c, j + 1, 3), b), np.where(mid, m, l)
    ya, yb, yl = [np.stack([gtable(t.reshape(8, -1)) for t in v]).astype(np.float32) for v in (a, b, l)]
    return {"ya": ya, "yb": yb, "yl": yl}

@@ -1,0 +1,681 @@
+import numpy as np
+from concourse.bass import DstId, RemoteDMATransfer
+from concourse.mybir import AluOpType, ActivationFunctionType
+A = AluOpType
+F = ActivationFunctionType
+W = 2560
+H = 136
+f32, f16, b16, i32, u16 = "float32", "float16", "bfloat16", "int32", "uint16"
+
+
+def _sb(shape, dt):
+    return ("sbuf", [128] + shape, dt)
+
+
+SCRATCH = {
+    "ps": ("psum", [128, 4096], f32),
+    "X": _sb([W], b16), "G": _sb([W], b16), "NB": _sb([W], i32), "WE": _sb([2048 + W], f32),
+    "RW0": _sb([2048 + 2 * H], f32), "RW1": _sb([2048 + 2 * H], f32), "RW2": _sb([2048 + 2 * H], f32),
+    "SN0": _sb([2 * H], f32), "SN1": _sb([2 * H], f32), "SN2": _sb([2 * H], f32),
+    "XA": _sb([2048], b16), "D": _sb([2048], b16), "L2": _sb([2048], f16), "LD": _sb([2048], f16), "GA": _sb([2048], b16), "GB": _sb([2048], b16),
+    "TT": _sb([2048], f16), "PR0": _sb([2048], f32), "PR1": _sb([2048], f32), "PR2": _sb([2048], f32), "PR3": _sb([2048], f32),
+    "NG": _sb([2048], f16), "XN": _sb([2048], b16), "RP": _sb([2048], f16), "MX": _sb([2048], f16),
+    "CZ": _sb([1792], f16), "WG": _sb([2048], f16), "AS": _sb([8, 16, 16], f16), "C2": _sb([64, 16], f16),
+    "LST": _sb([1024], u16), "PI": _sb([384], i32), "H16": _sb([384], f16), "EI": _sb([160], i32), "EF": _sb([480], f32),
+    "S4": _sb([4, 8, 16], f16), "SE": _sb([2, 8, 16], f32), "LL": _sb([3, 8, 16], f16), "MM": _sb([3, 8, 16], f16),
+    "EM": _sb([2, 8, 16], f32), "EE": _sb([8, 16], f32), "ZP": _sb([2, 128], f16), "DE": _sb([8, 2], f32),
+    "GM": _sb([2, 128], f32), "LW": _sb([2048], b16), "XN2": _sb([2048], f16), "AB": _sb([128], f32), "CM": _sb([2, 8, 16], f16),
+    "UD": _sb([2, 8, 16], f16), "SL": _sb([2, 8, 16], f16), "EC": _sb([8, 16], f32), "PH": _sb([2, 8, 16], f16), "PL": _sb([256], f16),
+    "ZB": _sb([5, 8, 16], f16), "PQ": _sb([2, 2, 8, 2], f16), "SS": _sb([8, 2], f16), "SQ": _sb([2, 8, 2], f16),
+    "EP": _sb([2, 8, 2], f32), "Q4": _sb([2, 8, 2], f32), "LE": _sb([2, 8, 2], f32), "Q5": _sb([2, 8, 2], f32), "YO": _sb([384], f32),
+    "I32": _sb([128], f32), "UP": _sb([2, 128], f32),
+    "ZERO": _sb([512], b16), "ONE": _sb([128], b16), "II": _sb([512], b16), "LT": _sb([16], b16), "PP": _sb([128], b16), "BO": _sb([8], f32),
+    "X3": _sb([32], b16), "X3E": _sb([32], b16), "XP": _sb([64], b16), "XH": _sb([64], b16), "KS": _sb([8, 16], b16),
+    "ZM": _sb([14, 128], b16), "SM": _sb([8, 32], b16), "S2": _sb([8, 32], b16), "S0": _sb([128], b16),
+}
+DIAG = ["I8", "I2", "IM1", "IM8", "IM2", "I7", "I16", "DMUL", "DADD", "DA", "DB", "DC", "DD", "IMID", "IEND", "E0", "ZK"]
+for _n in DIAG:
+    SCRATCH[_n] = _sb([128], b16)
+SEMAPHORES = ["v", "a", "p", "gq", "dx", "dg", "dn", "de", "dpa", "dpb", "dpl", "dw", "h0", "h1", "h2", "snt", "o1", "o2"]
+MAG32 = 402653184.0
+MAG64 = 805306368.0
+END = slice(0, 16, 15)
+
+
+LISTS = ("LA", "LB", "Ll", "LZ", "LN", "LU", "LX", "LW")
+CYC, GAM, PCYC, VFIX, AFIX, PFIX, WAKE = 0.83, 1.56, 0.417, 60.0, 90.0, 10.0, 120.0
+TRIES = [(300.0, 0, 0.0)]
+ORDER = {}
+PLAN = "2b02080004030g010h060a072c092h0x2e3p3k100z3u2g2f0y2j2i0w2d2k2n3f2q050i2m0b2s2t0l2p0c2v0j2r2u0m2w2y2l0k390n2x360o0q0p3g0r383l0s3h0u373m0t0v3n3a1c3i0d32113b3o0e1534333j0f3q2z16354k3v3r19313c173w3s443d123x453e3y1846401a413z42472o3t431b4r13498l4l1d14304o4s1e4p1v4y4v1s1w4b4z4a4w1n4c1o564d521p4m4g1j551k501l48594e1m4t1q4n1r1f574q5c1g1h5a5d1i581t4u5b1x531u4x1y515r225e1z54235f5s205h245t215g5u25285j5m26295i5n272a5l5o5k5p4f615q5w5x5v5y5z4h60624i634j7b64656766686f696a6b8a6c8b6d6g6e8d6h6i6k6y6j6l6s786m6t6n6p6o6u6z6r6q6x6w706v7a76739c74779d727c7d7j75717n798c7p7e7q8m7f7g7o7i7h7r7k808o828e818n7m8u8v8y837l7y7w7s7t7x7z7v7u8884868587898h8f8j8i8g8k8t8p938s8r8q8x8w92b290919e959faaev8z94abac9iadb19b9j9ga09v9ha59q98969w9r979x9k9s9z9m9u9l9ta19n9aa699a29y9oa4a7af9pa3aealaja8akagamauahanawaqavb3a9aybfaxb5azb9bhb0bgb4b8babmb6bcbbb7bnbdbjbpbeaibkaoc1bic2bqblboc3brc4bubwapbxbybzbsarc0c5c6btasc7atdlbvc8c9cbcacccdcecfcgchcicjcpckclelcmekcncqcoemcrcscucvctcyd8cwczcxd7d0d3d2d9d1d4dkd5dad6dcdgdedhdtfnfmdddndmeodxdfdidzendbe0dodjexdpdqdydrdse1dueaewecf4ebeydvf5f8ede3e2dwe4eee8e5e9ege6eiefe7ehejeqepetesereuf3ezfdf1f0fcf6f2fof9faf7fefhfpfqfffbflgkfrg0gag5gfg1figlfggmg2fsgng3fufthbg6fvg4gbg7fkfwgcg8fyg9fxgggdfzh4ghgpgugvgtgigogwgqgjgxh5h6h0fjhrhpgrh7gehshch8hkhihfh9hqhghahlhjhthdhxhmhuhehvhwhnhhhyhogsgyhzibi0ici1idi4iei3i6i7i2i8i5i9gziliaigihifiih1ijh2imh3ikinioipiriqisitiziuivkmiwknixj0iykpj1j2j4jij3j5j8jsj6j9j7jdjcjajjjbjejhjfjkjgjljmjtjojqjnjrkqkojpjujvjwk2jyjxk3jzkck0kdk1k4kekakgkfk7k5kikbk6k8kkkhk9kjklkskrkvkuktl1kyl6kwl3l8kxl0kzl9l4l2l7lal5"
+OPT = {"td": (0, 1, 2, 3), "ea": "aa", "eb": "vv", "lb": ("vvaa", "vvaa"), "ng": ("av", "av"), "gb": ("aaaa", "aaaa")}
+
+
+def bank(t):
+    return t[0] == "B" and t[1:].isdigit()
+
+
+def arrange(ops):
+    n = len(ops)
+    pred = [set() for _ in range(n)]
+    lw, rd = {}, {}
+    for i, o in enumerate(ops):
+        for t in o[2] + o[3]:
+            if t in lw:
+                pred[i].add(lw[t])
+            if t in o[3] or bank(t):
+                pred[i].update(j for j in rd.get(t, ()) if t in o[3] or ops[j][0] != o[0])
+        for t in o[2]:
+            rd.setdefault(t, []).append(i)
+        for t in o[3]:
+            lw[t] = i
+            rd[t] = []
+        pred[i].discard(i)
+    succ = [[] for _ in range(n)]
+    for i in range(n):
+        for j in pred[i]:
+            succ[j].append(i)
+    plan = [int(PLAN[i:i + 2], 36) for i in range(0, len(PLAN), 2)]
+    if sorted(plan) == list(range(n)):
+        at = {i: k for k, i in enumerate(plan)}
+        if all(at[j] < at[i] for i in range(n) for j in pred[i]):
+            return plan
+    best = None
+    for win, seed, amp in TRIES:
+        noise = [1.0 + amp * float(x) for x in np.random.default_rng(seed).random(n)]
+        pr = [0.0] * n
+        for i in range(n - 1, -1, -1):
+            pr[i] = ops[i][5] * noise[i] + ops[i][6] + WAKE + max([pr[j] for j in succ[i]], default=0.0)
+        left = [len(p) for p in pred]
+        est = [0.0] * n
+        ready = {}
+        for i in range(n):
+            if not left[i]:
+                ready.setdefault(ops[i][0], []).append(i)
+        free, order, end = {}, [], 0.0
+        while len(order) < n:
+            pick = None
+            for q, l in ready.items():
+                if not l:
+                    continue
+                f = free.get(q, 0.0)
+                t0 = max(f, min(est[i] for i in l))
+                i = max((i for i in l if est[i] <= t0 + win), key=lambda i: pr[i])
+                s = max(f, est[i])
+                if pick is None or s < pick[0]:
+                    pick = (s, i, q)
+            s, i, q = pick
+            ready[q].remove(i)
+            order.append(i)
+            free[q] = s + ops[i][5]
+            done = free[q] + ops[i][6]
+            end = max(end, done)
+            for j in succ[i]:
+                est[j] = max(est[j], done + (0.0 if q == "p" == ops[j][0] else WAKE))
+                left[j] -= 1
+                if not left[j]:
+                    ready.setdefault(ops[j][0], []).append(j)
+        if best is None or end < best[0]:
+            best = (end, order, (win, seed, amp))
+    ORDER["best"] = (best[0], best[2])
+    return best[1]
+
+
+def rank_program(g, core, T, topo):
+    rank = T.rank_of(core)
+    if rank is None:
+        return
+    N = len(T.cores)
+    prv, nxt = T.cores[(rank - 1) % N], T.cores[(rank + 1) % N]
+    Q = {"v": g.vector, "a": g.scalar, "p": g.tensor, "gq": g, "s": g.sync}
+    V, S, P = g.vector, g.scalar, g.tensor
+    cnt = {"v": 0, "a": 0, "p": 0, "gq": 0}
+    seen = {q: {} for q in Q}
+    lastw, readers = {}, {}
+
+    def need(q, ev):
+        s, n = ev
+        if s == "p" and q == "p":
+            return
+        if seen[q].get(s, 0) < n:
+            seen[q][s] = n
+            Q[q].wait_ge(T.sem[s], n)
+
+    ops = []
+
+    def op(q, fn, r=(), w=(), ev=None, cost=100.0, late=0.0):
+        ops.append((q, fn, list(r), list(w), ev, cost, late))
+
+    def issue(q, fn, r, w, ev):
+        want = {}
+        for t in list(r) + list(w):
+            evs = [lastw.get(t)]
+            if t in w or bank(t):
+                evs += [e for e in readers.get(t, {}).items() if t in w or e[0] != q]
+            for e in evs:
+                if e is not None:
+                    want[e[0]] = max(want.get(e[0], 0), e[1])
+        for e in want.items():
+            need(q, e)
+        ins = fn()
+        if ev is None:
+            cnt[q] += 1
+            ev = (q, cnt[q])
+            ins.then_inc(T.sem[q], 1)
+        elif ev[0] != "snt":
+            ins.then_inc(T.sem[ev[0]], 16)
+        for t in r:
+            readers.setdefault(t, {})[ev[0]] = ev[1]
+        for t in w:
+            lastw[t] = ("h" + t[4:], 8) if t[:4] == "HALO" else ev
+            readers[t] = {}
+
+    def nel(ap):
+        n = 1
+        for x in ap.shape[1:]:
+            n *= x
+        return n
+
+    def gathers(r):
+        return any(t in LISTS for t in r)
+
+    def vcost(out, r, k):
+        return 50 + nel(out) * GAM * CYC if gathers(r) else VFIX + max(64, nel(out) * k) * CYC
+
+    def short(*aps):
+        return all("16" in str(x.dtype) for x in aps)
+
+    def tt(out, a, b, o, r, w):
+        k = 1.0 if any(bank(t) for t in r) else 2.0
+        op("v", lambda: V.tensor_tensor(out, a, b, o), r, w, cost=vcost(out, r, k))
+
+    def ts(out, a, s1, o1, r, w, s2=None, o2=None):
+        c = vcost(out, r, 1.0 if gathers(r) or not short(out, a) else 0.5)
+        if o2 is None:
+            op("v", lambda: V.tensor_scalar(out, a, s1, None, o1), r, w, cost=c)
+        else:
+            op("v", lambda: V.tensor_scalar(out, a, s1, s2, o1, o2), r, w, cost=c)
+
+    def cp(out, a, r, w):
+        op("v", lambda: V.tensor_copy(out, a), r, w, cost=vcost(out, r, 1.0))
+
+    def fill(out, w):
+        op("v", lambda: V.memset(out, 0.0), (), w, cost=vcost(out, (), 0.5 if short(out) else 1.0))
+
+    def act(out, a, r, w, func=F.Copy, **kw):
+        op("a", lambda: S.activation(out, a, func, **kw), r, w, cost=65 + nel(out) * GAM * CYC if gathers(r) else AFIX + nel(out) * CYC)
+
+    def mm(items, r, w):
+        def fn():
+            for o, l, rh, st, sp in items:
+                ins = P.matmul(o, l, rh, st, sp)
+            return ins
+        op("p", fn, r, w, cost=sum(PFIX + max(64, nel(x[2])) * (1 if short(x[1]) else 4) * PCYC for x in items))
+
+    def dma(q, out, in_, r, w, ev, late):
+        op(q, lambda: Q[q].dma_start(out, in_), r, w, ev, 100.0, late)
+
+    def grp(out, pairs, r, w):
+        mm([(out, l, rh, i == 0, i == len(pairs) - 1) for i, (l, rh) in enumerate(pairs)], r, w)
+
+    def ps(b, c0=0, c1=512, st=1):
+        return T.ps[:, 512 * b + c0:512 * b + c1:st]
+
+    def ch(t, c, o=0):
+        return t[:, o + 512 * c:o + 512 * c + 512]
+
+    def gat(win, lst, c0=0, c1=4):
+        return win.indirect(T.LST[:, 128 * lst + 32 * c0:128 * lst + 32 * c1])
+
+    def lst(i):
+        return T.LST[:, 128 * i:128 * i + 128]
+
+    def allc(n):
+        return [n + str(c) for c in range(4)]
+    LB_, LA_, LL_, LZ_, LN_, LU_, LX_, LW_ = range(8)
+    I = T.II[:, 0:128]
+    XW, GW, NW, EW, LW = T.X[:, 0:W], T.G[:, 0:W], T.NB[:, 0:W], T.WE[:, 0:2048 + W], T.LT[:, 0:16]
+    ET = T.WE[:, 2048:2048 + W]
+    SAB = T.S4[:, 1:3]
+    WEe = ["WEe", "WEr0", "WEr1"]
+    WEt = allc("WE") + WEe
+
+    def reduce16(src, tok, bank, c0, rhs=None, rtok=("BO",), n=8):
+        step = 4 if rhs is None else 16
+        for k0 in range(0, 16, step):
+            mm([(ps(bank, c0 + k, c0 + 16 * n, 16), src[:, k:2048:16], T.BO[:] if rhs is None else rhs(k), True, True) for k in range(k0, k0 + step)],
+               list(tok) + list(rtok), ["B%d" % bank])
+
+    dma("s", T.X[:], T.xrec[:], [], ["X", "qs"], ("dx", 16), 4600.0)
+    dma("a", T.PI[:, 128:256], T.pa[:], [], ["PIa"], ("dpa", 16), 2300.0)
+    dma("a", T.EI[:], T.erec[:], [], ["EI"], ("de", 16), 2300.0)
+    dma("s", T.PI[:, 0:128], T.pb[:], [], ["PIb"], ("dpb", 16), 2300.0)
+    dma("a", T.PI[:, 256:384], T.lam[:], [], ["PIl"], ("dpl", 16), 2300.0)
+    dma("s", T.G[:], T.grec[:], ["qs"], ["G"], ("dg", 16), 4600.0)
+
+    def iota(n, pat, base=0, cm=0, ap=None):
+        o = T[n][:] if ap is None else ap
+        op("gq", lambda: g.iota(o, pat, base, cm, allow_small_or_imprecise_dtypes=True), w=[n], cost=130 + 2 * CYC * nel(o))
+
+    def sel(n, src, pat, cmp, fill, base=0, cm=1, ap=None, sap=None):
+        o = T[n][:] if ap is None else ap
+        op("gq", lambda: g.affine_select(o, T[src][:] if sap is None else sap, pat, cmp, fill, base, cm), [src], [n], cost=170 + 2 * CYC * nel(o))
+    Z128 = T.ZERO[:, 0:128]
+
+    def diag(n, v):
+        sel(n, "ZERO", [[-1, 128]], A.not_equal, v, sap=Z128)
+
+    def keepdiag(n):
+        sel(n, n, [[-1, 128]], A.is_equal, 0.0)
+
+    def rows(n, lead, lo, hi, tail=(), ap=None):
+        sel(n, n, [[-lead[0], lead[1]], [-16, 8]] + list(tail), A.is_ge, 0.0, -lo, 1, ap, ap)
+        sel(n, n, [[lead[0], lead[1]], [16, 8]] + list(tail), A.is_ge, 0.0, hi, -1, ap, ap)
+    GK = [[-16, 8], [256, 16]]
+
+    def consts0():
+        iota("ZERO", [[0, 512]])
+        sel("II", "ZERO", [[-1, 128]], A.not_equal, 1.0, ap=I, sap=Z128)
+        iota("LT", [[1, 16]])
+        diag("I8", 8.0)
+        iota("X3E", [[1, 2], [0, 16]])
+        rows("X3E", [0, 4], 6, 7)
+        iota("BO", [[0, 8]], 1)
+        rows("BO", [0, 1], 0, 15)
+        iota("ONE", [[0, 128]], 1)
+        iota("PP", [[1, 128]])
+        diag("I2", 2.0)
+        diag("I16", 16.0)
+        sel("DMUL", "I16", GK, A.not_equal, 1.0)
+        iota("DADD", [[0, 8], [1, 16]], H - 1)
+        sel("DADD", "DADD", [[0, 8], [1, 16]], A.not_equal, 0.0, 0, 0)
+        keepdiag("DADD")
+        for n, b, cm in (("DA", 0, 16), ("DB", H + 1, -1), ("DC", 2048, -16), ("DD", -14, 1)):
+            iota(n, [[0, 128]], b, cm)
+            keepdiag(n)
+        sel("II4", "ZERO", [[0, 3], [-1, 128]], A.not_equal, 1.0, ap=T.II[:, 128:512], sap=T.ZERO[:, 0:384])
+        diag("IM1", -1.0)
+
+    def consts1():
+        for n, v in (("IM2", -2.0), ("I7", 7.0), ("I32", 1.0), ("IM8", -8.0)):
+            diag(n, v)
+        x32 = [[0, 8], [-1, 32]]
+        sel("SM", "ZERO", x32, A.is_gt, 0.25, 16, 0, sap=T.ZERO[:, 0:256])
+        rows("SM", [0, 1], 0, 15, [[0, 32]])
+        sel("S2", "ZERO", x32, A.is_gt, -0.125, 15, 0, sap=T.ZERO[:, 0:256])
+        sel("S2", "S2", x32, A.is_gt, -0.25, 16, 0)
+        rows("S2", [0, 1], 0, 15, [[0, 32]])
+        sel("S0", "ZERO", [[0, 8], [-1, 16]], A.is_gt, -0.125, 1, 0, sap=Z128)
+        rows("S0", [0, 1], 0, 15, [[0, 16]])
+        sel("E0", "ZERO", GK, A.not_equal, 1.0, sap=Z128)
+        iota("ZK", [[0, 8], [1, 16]])
+        sel("ZK", "ZK", [[-16, 8], [0, 16]], A.is_equal, 0.0, -15)
+        for j in range(1, 15):
+            sel("ZM%d" % j, "ZK", [[-16, 8], [0, 16]], A.not_equal, -15.0, -j, ap=T.ZM[:, j - 1])
+        sel("IMID", "II", [[0, 8], [1, 16]], A.not_equal, 0.0, 0, 0, sap=I)
+        sel("IMID", "IMID", [[0, 8], [1, 16]], A.not_equal, 0.0, -15, 0)
+        sel("IEND", "ZERO", GK, A.not_equal, 3328.0, sap=Z128)
+        sel("IEND", "IEND", GK, A.not_equal, 3328.0, -15 - 256 * 15)
+        iota("KS", [[0, 8], [16, 16]])
+        sel("KS", "KS", [[0, 8], [1, 16]], A.not_equal, 0.0, -15, 0)
+        sel("KS", "KS", [[-16, 8], [0, 16]], A.is_equal, 0.0, -15)
+        sel("KS", "KS", GK, A.not_equal, -1.0)
+        sel("KS", "KS", GK, A.not_equal, -1.0, -256 * 15)
+        iota("X3", [[0, 32]], 1)
+        rows("X3", [2, 4], 0, 1)
+        iota("XP", [[0, 64]], -240)
+        rows("XP", [0, 8], 8, 9)
+        iota("XH", [[-30, 8], [0, 8]], -15)
+        rows("XH", [0, 8], 10, 11)
+
+    consts0()
+    consts1()
+    fill(T.WE[:, 1920:2048 + W], ["WEe"])
+    fill(T.ZB[:], ["ZB%d" % i for i in range(5)])
+    cp(lst(LA_), T.PI[:, 128:256], ["PIa"], ["LA"])
+    ts(T.EF[:, 0:160], T.EI[:], 1.0 / 32, A.mult, ["EI"], ["EF0"])
+    cp(lst(LB_), T.PI[:, 0:128], ["PIb"], ["LB"])
+    ts(T.EF[:, 160:320], T.EF[:, 0:160], MAG32, A.add, ["EF0"], ["EF1"], -MAG32, A.add)
+    cp(lst(LL_), T.PI[:, 256:384], ["PIl"], ["Ll"])
+    tt(T.EF[:, 320:480], T.EF[:, 0:160], T.EF[:, 160:320], A.subtract, ["EF0", "EF1"], ["EF2"])
+    dma("s", T.WE[6:128:16, 2048:2048 + W], T.EF[:, 160:320], ["EF1", "WEe"], ["WEr0"], ("dw", 32), 2300.0)
+    dma("s", T.WE[7:128:16, 2048:2048 + W], T.EF[:, 320:480], ["EF2", "WEe"], ["WEr1"], ("dw", 32), 2300.0)
+    dma("s", T.NB[:], T.nbr[:], ["WEr0", "WEr1"], ["NB"], ("dn", 16), 7200.0)
+    ts(T.H16[:, 0:256], T.PI[:, 0:256], -1280.0, A.add, ["PIa", "PIb"], ["H16a"])
+    cp(T.H16[:, 256:384], T.PI[:, 256:384], ["PIl"], ["H16l"])
+    ast = ["AS%d" % i for i in (0, 2, 3, 4, 6, 7, 8, 9, 10, 11)]
+    fill(T.AS[:], ast)
+    mm([(ps(7, 128 * i, 128 * i + 128), T.H16[:, 128 * i:128 * i + 128], I, True, True) for i in range(3)], ["H16a", "H16l", "II"], ["B7"])
+
+    def state_l(bank, c0):
+        act(T.LL[:, 1], ps(bank, c0, c0 + 128), ["B%d" % bank], ["LL1"])
+        act(T.LL[:, 0], ps(bank, c0, c0 + 128), ["B%d" % bank], ["LL0"], F.Identity, scale=-1.0, bias=8.0)
+        act(T.LL[:, 2], ps(bank, c0, c0 + 128), ["B%d" % bank], ["LL2"], F.Identity, scale=-1.0, bias=8.0)
+
+    def xa(c):
+        act(ch(T.XA, c), gat(XW, LA_, c, c + 1), ["X", "LA"], ["XA%d" % c])
+
+    def dd(c):
+        tt(ch(T.D, c), gat(XW, LB_, c, c + 1), ch(T.XA, c), A.subtract, ["X", "LB", "XA%d" % c], ["D%d" % c])
+        mm([(ps(c), I, ch(T.D, c), True, True)], ["D%d" % c, "II"], ["B%d" % c])
+
+    def rr(r, c):
+        b = 4 + c % 2
+        grp(ps(b), [(T.I8[:], ch(T.XA, c)), (I, ch(T.LD, c))], ["I8", "II", "XA%d" % c, "LD%d" % c], ["B%d" % b])
+        act(ch(T["RW%d" % r], c, H), ps(b), ["B%d" % b], ["R%d" % c])
+        act(ch(T.XN2, c), ps(b), ["B%d" % b], ["RS%d" % c])
+
+    def energy():
+        tt(T.EM[:], T.SE[:], T.LL[:, 1:3], A.mult, ["SE", "LL1", "LL2"], ["EM"])
+        tt(T.EE[:], T.EM[:, 0], T.EM[:, 1], A.add, ["EM"], ["EE"])
+
+    def send(r):
+        sn, rw = T["SN%d" % r], T["RW%d" % r]
+        if r == 0:
+            cp(sn[:, 128:H], T.EE[:, :, 0], ["EE"], ["SN%d0" % r])
+            cp(sn[:, H + 128:2 * H], T.EE[:, :, 15], ["EE"], ["SN%d1" % r])
+        else:
+            tt(T.Q4[:], T.SE[:, :, :, END], T.LE[:], A.mult, ["SE", "LE0", "LE1"], ["Q4"])
+            tt(sn[:, 128:H], T.Q4[:, 0, :, 0], T.Q4[:, 1, :, 0], A.add, ["Q4"], ["SN%d0" % r])
+            tt(sn[:, H + 128:2 * H], T.Q4[:, 0, :, 1], T.Q4[:, 1, :, 1], A.add, ["Q4"], ["SN%d1" % r])
+        e0, e1 = topo.engines(core, prv), topo.engines(core, nxt)
+        m0 = sum(1 << e for e in e0[0:4])
+        m1 = sum(1 << e for e in [x for x in e1 if not m0 >> x & 1][0:4])
+        a0, a1 = topo.addr(prv), topo.addr(nxt)
+        trs = [RemoteDMATransfer(dst_ids=[DstId(rid=a0[0], pnc=a0[1])], dma_engine_mask=m0, remote_sem=T.sem["h%d" % r],
+                                 src=sn[:, 0:H], dst=rw[:, H + 2048:2 * H + 2048]),
+               RemoteDMATransfer(dst_ids=[DstId(rid=a1[0], pnc=a1[1])], dma_engine_mask=m1, remote_sem=T.sem["h%d" % r],
+                                 src=sn[:, H:2 * H], dst=rw[:, 0:H])]
+        op("gq", lambda: g.remote_dma_fused(trs, local_sem=T.sem.snt), ["SN%d%d" % (r, i) for i in range(4)], ["HALO%d" % r],
+           ("snt", 8 * (r + 1)), 300.0, 3000.0)
+
+    def ends_r(r, src, o, tok):
+        sn = T["SN%d" % r]
+        act(sn[:, 0:128], src[:, o:o + 2048:16], tok, ["SN%d2" % r])
+        act(sn[:, H:H + 128], src[:, o + 15:o + 2048:16], tok, ["SN%d3" % r])
+
+    def zprod():
+        ts(T.MM[:, 0:3:2], T.LL[:, 1:3], 8.0, A.is_equal, ["LL1", "LL2"], ["MM0"])
+        ts(T.MM[:, 1], T.LL[:, 1], 8.0, A.not_equal, ["LL1"], ["MM1"])
+        tt(T.ZP[:], T.MM[:, 0:2], SAB, A.mult, ["MM0", "MM1", "SAB"], ["ZP"])
+        grp(ps(6, 128, 256), [(T.ZP[:, 0], I), (T.ZP[:, 1], I)], ["ZP", "II"], ["B6"])
+
+    def nblist(r):
+        rw = T["RW%d" % r]
+        tt(T.ZB[:, 0, :, 1:15], T.EE[:, :, 2:16], T.EE[:, :, 0:14], A.is_ge, ["EE"], ["ZB0"])
+        tt(T.ZB[:, 1, :, 0], T.EE[:, :, 1], rw[:, 128:H], A.is_ge, ["EE", "HALO%d" % r], ["ZB1"])
+        tt(T.ZB[:, 2, :, 15], rw[:, H + 2048 + 128:2 * H + 2048], T.EE[:, :, 14], A.is_ge, ["EE", "HALO%d" % r], ["ZB2"])
+        grp(ps(7, 128, 256), [(T.DMUL[:], T.PP[:]), (T.DADD[:], T.ONE[:]), (T.ZB[:, 0], T.I2[:]), (T.ZB[:, 1], T.DA[:]), (T.ZB[:, 1], T.DB[:]),
+                              (T.ZB[:, 2], T.DC[:]), (T.ZB[:, 2], T.DD[:])],
+            ["DMUL", "PP", "DADD", "ONE", "ZB0", "ZB1", "ZB2", "I2", "DA", "DB", "DC", "DD"], ["B7"])
+
+    def prod(dst, tok, src, stok, c0=0, c1=4, o=0):
+        tt(dst[:, 512 * c0:512 * c1], T.ps[:, 512 * c0:512 * c1], src[:, o + 512 * c0:o + 512 * c1], A.mult,
+           ["B%d" % c for c in range(c0, c1)] + [stok + str(c) for c in range(c0, c1)], [tok + str(c) for c in range(c0, c1)])
+
+    def tan(r, c):
+        rw = T["RW%d" % r]
+        tt(ch(T.TT, c), gat(rw[:, 0:2048 + 2 * H], LN_, c, c + 1), ch(T.XN2, c), A.subtract, allc("R") + ["HALO%d" % r, "LN", "RS%d" % c], ["T%d" % c])
+
+    def gather(q, dst, tok, win, wtok, l, ltok, c0=0, c1=4, bias=None):
+        o, w_ = dst[:, 512 * c0:512 * c1], [tok + str(c) for c in range(c0, c1)]
+        if q == "a" and bias is None:
+            act(o, gat(win, l, c0, c1), list(wtok) + [ltok], w_)
+        elif q == "a":
+            act(o, gat(win, l, c0, c1), list(wtok) + [ltok], w_, F.Identity, bias=bias)
+        elif bias is None:
+            cp(o, gat(win, l, c0, c1), list(wtok) + [ltok], w_)
+        else:
+            ts(o, gat(win, l, c0, c1), bias, A.add, list(wtok) + [ltok], w_)
+
+    def nextract():
+        it = [(ps(7), Z128, T.ZERO[:], True, False)] + [(ps(7, 128 * i, 128 * i + 128), T.IM1[:], T.S4[:, 2], False, False) for i in range(2)]
+        mm(it, ["ZERO", "IM1", "SAB"], ["B7"])
+        mm([(ps(7, k, 512, 16), T.NG[:, k:2048:16], T.II[:, k:512:16], False, k == 15) for k in range(16)], allc("NG") + ["II", "II4"], ["B7"])
+
+    def nstate():
+        act(T.S4[:, 0:4:3], ps(7, 256, 512), ["B7"], ["NS"])
+
+    def umask():
+        tt(ps(7, 0, 256), ps(7, 0, 256), T.MM[:, 0:3:2], A.mult, ["B7", "MM0"], ["B7"])
+
+    m8 = [T.C2[:, 8 * m:8 * m + 8, :] for m in range(8)]
+
+    def l_sums():
+        grp(ps(3, 0, 128), [(T.ZB[:, 3], I)] + [(x, I) for x in m8], ["C20", "C21", "ZB3", "II"], ["B3"])
+
+    def l_sums2():
+        grp(ps(6, 0, 128), [(I, T.ZB[:, 3])] + [(I, x) for x in m8], ["C20", "C21", "ZB3", "II"], ["B6"])
+
+    for r in range(3):
+        last = r == 2
+        rw = T["RW%d" % r]
+        if r == 0:
+            xa(0)
+            cp(SAB, ps(7, 0, 256), ["B7"], ["SAB"])
+            xa(1), dd(0), xa(2), dd(1), xa(3)
+            state_l(7, 256)
+            dd(2), dd(3)
+            for h in range(2):
+                gather(OPT["ea"][h], T.WG, "WG", ET, WEe, LA_, "LA", 2 * h, 2 * h + 2)
+                gather(OPT["eb"][h], T.RP, "RP", ET, WEe, LB_, "LB", 2 * h, 2 * h + 2)
+            reduce16(T.WG, allc("WG"), 6, 384, lambda k: T.X3E[:, 16:24], ("X3E",))
+            reduce16(T.RP, allc("RP"), 6, 256, lambda k: T.X3E[:, 16:24], ("X3E",))
+            cp(T.SE[:], ps(6, 256, 512), ["B6"], ["SE"])
+        else:
+            xa(0)
+            ts(T.C2[:, :, 0:8], ps(0), 0.0, A.is_ge, ["B0"], ["C20"])
+            xa(1)
+            ts(T.C2[:, :, 8:16], ps(1), 0.0, A.is_ge, ["B1"], ["C21"])
+            act(T.SE[:], ps(2, 256, 512), ["B2"], ["SE"])
+            l_sums()
+            l_sums2()
+            xa(2), xa(3)
+            state_l(6, 0)
+            cp(lst(LL_), ps(3, 0, 128), ["B3"], ["Ll"])
+            ends_r(r, T.RP, 0, allc("RP"))
+            tt(T.SE[:, :, :, END], T.SE[:, :, :, END], T.UD[:, :, :, END], A.mult, ["SE", "UD"], ["SE"])
+            tt(T.SE[:, :, :, END], T.SE[:, :, :, END], T.EP[:], A.add, ["SE", "EP"], ["SE"])
+            dd(0), dd(1), dd(2), dd(3)
+        energy()
+        for c in range(4):
+            gather(OPT["lb"][min(r, 1)][c], T.LW, "W", LW, ["LT"], LL_, "Ll", c, c + 1)
+            prod(T.LD, "LD", T.LW, "W", c, c + 1)
+            rr(r, c)
+        if r == 0:
+            ends_r(r, rw, H, allc("R"))
+        send(r)
+        zprod()
+        act(lst(LZ_), ps(6, 128, 256), ["B6"], ["LZ"], F.Identity, bias=1280.0)
+        nblist(r)
+        cp(lst(LN_), ps(7, 128, 256), ["B7"], ["LN"])
+        for h in range(2):
+            gather(OPT["ng"][min(r, 1)][h], T.NG, "NG", NW, ["NB"], LZ_, "LZ", 2 * h, 2 * h + 2, bias=-1280.0)
+        nextract()
+        nstate()
+        umask()
+        for c in range(4):
+            gather("a", T.GA, "GA", GW, ["G"], LA_, "LA", c, c + 1)
+            gather(OPT["gb"][min(r, 1)][c], T.GB, "GB", GW, ["G"], LB_, "LB", c, c + 1)
+            tan(r, c)
+            if c in OPT["td"]:
+                prod(T.PR0, "P0", T.TT, "T", c, c + 1)
+            b = 4 + c % 2
+            grp(ps(b), [(I, ch(T.GB, c)), (T.IM1[:], ch(T.GA, c))], ["II", "IM1", "GA%d" % c, "GB%d" % c], ["B%d" % b])
+            tt(ch(T.L2, c), ps(b), ch(T.LW, c), A.mult, ["B%d" % b, "W%d" % c], ["L2%d" % c])
+            grp(ps(c), [(T.I8[:], ch(T.GA, c)), (I, ch(T.L2, c))], ["II", "I8", "GA%d" % c, "L2%d" % c], ["B%d" % c])
+        for h in range(2):
+            act(T.PR3[:, 1024 * h:1024 * h + 1024], T.TT[:, 1024 * h:1024 * h + 1024], ["T%d" % (2 * h), "T%d" % (2 * h + 1)],
+                ["P3%d" % (2 * h), "P3%d" % (2 * h + 1)], F.Square)
+        for c in range(4):
+            prod(T.PR1, "P1", T.D, "D", c, c + 1)
+        for c in range(4):
+            prod(T.PR2, "P2", T.TT, "T", c, c + 1)
+            if c not in OPT["td"]:
+                mm([(ps(c), I, ch(T.D, c), True, True)], ["D%d" % c, "II"], ["B%d" % c])
+                prod(T.PR0, "P0", T.TT, "T", c, c + 1)
+        reduce16(T.PR1, allc("P1"), 4, 0)
+        act(T.GM[:, 1], ps(4, 0, 128), ["B4"], ["GM1"])
+        reduce16(T.PR3, allc("P3"), 6, 128)
+        tt(ps(6, 256, 384), ps(6, 128, 256), T.GM[:, 1], A.mult, ["B6", "GM1"], ["B6"])
+        if len(OPT["td"]) == 4:
+            reduce16(T.PR0, allc("P0"), 4, 128)
+            act(T.GM[:, 0], ps(4, 128, 256), ["B4"], ["GM0"])
+            reduce16(T.PR2, allc("P2"), 5, 0)
+        else:
+            reduce16(T.PR2, allc("P2"), 4, 128)
+            act(T.GM[:, 0], ps(4, 128, 256), ["B4"], ["GM0"])
+            reduce16(T.PR0, allc("P0"), 5, 0)
+        tt(T.AB[:], ps(5, 0, 128), T.GM[:, 0], A.mult, ["B5", "GM0"], ["AB"])
+        tt(T.CM[:, 0], T.AB[:], ps(6, 256, 384), A.is_gt, ["AB", "B6"], ["CM0"])
+        tt(T.CM[:, 1], T.AB[:], ps(6, 256, 384), A.is_lt, ["AB", "B6"], ["CM1"])
+        tt(T.UP[:], ps(7, 0, 256), T.CM[:], A.mult, ["B7", "CM0", "CM1"], ["UP"])
+        mm([(ps(4, 0, 128), T.LL[:, 1], I, True, False), (ps(4, 0, 128), T.CM[:, 0], I, False, False), (ps(4, 0, 128), T.CM[:, 1], T.IM1[:], False, False)],
+           ["LL1", "II", "IM1", "CM0", "CM1"], ["B4"])
+        tt(T.UD[:], T.CM[:], T.MM[:, 0:3:2], A.mult, ["CM0", "CM1", "MM0"], ["UD"])
+        grp(ps(5, 0, 128), [(T.S4[:, 2], I), (T.UP[:, 0], T.I32[:]), (T.UP[:, 1], T.I32[:])], ["SAB", "II", "I32", "UP"], ["B5"])
+        mm([(ps(4, 0, 128), T.UD[:, 0], T.IM2[:], False, False), (ps(4, 0, 128), T.UD[:, 1], I, False, True)], ["UD", "IM2", "II"], ["B4"])
+        act(lst(LX_), ps(5, 0, 128), ["B5"], ["LX"], F.Identity, bias=1280.0)
+        cp(lst(LU_), ps(4, 0, 128), ["B4"], ["LU"])
+        lr = [(I, T.LL[:, 1]), (I, T.CM[:, 0]), (T.IM1[:], T.CM[:, 1])]
+        grp(ps(6, 0, 128), lr, ["II", "IM1", "LL1", "CM0", "CM1"], ["B6"])
+        grp(ps(6, 128, 256), lr + [(T.IM8[:], T.UD[:, 0]), (T.I8[:], T.UD[:, 1])], ["II", "IM1", "LL1", "CM0", "CM1", "UD", "I8", "IM8"], ["B6"])
+
+        def rp(c):
+            gather("a", T.XN, "XN", XW, ["X"], LX_, "LX", c, c + 1)
+            tt(ch(T.L2, c), gat(LW, LU_, c, c + 1), ch(T.D, c), A.mult, ["LT", "LU", "D%d" % c], ["L2%d" % c])
+            grp(ps(c), [(T.I7[:], ch(T.XA, c)), (I, ch(T.L2, c)), (I, ch(T.XN, c))], ["II", "I7", "XA%d" % c, "L2%d" % c, "XN%d" % c], ["B%d" % c])
+
+        def rpev(c):
+            act(ch(T.RP, c), ps(c), ["B%d" % c], ["RP%d" % c])
+
+        def mx(c):
+            tt(T.MX[:, 512 * c:512 * c + 511], ps(c, 1, 512), T.RP[:, 512 * c:512 * c + 511], A.max, ["B%d" % c, "RP%d" % c], ["MX%d" % c])
+        rp(0), rp(1), rpev(0), rp(2), rpev(1), rp(3), rpev(2), rpev(3)
+        ts(T.SL[:, 0], ps(6, 0, 128), 4.0, A.is_gt, ["B6"], ["SL0"])
+        ts(T.SL[:, 1], ps(6, 0, 128), 4.0, A.is_le, ["B6"], ["SL1"])
+        mx(0), mx(1)
+        tt(T.AS[:, :, 2, :], T.SL[:, 0], T.S4[:, 1], A.mult, ["SL0", "SAB"], ["AS2"])
+        mx(2), mx(3)
+        mm([(ps(4, 0, 128), T.RP[:, k:2048:16], T.S0[:] if k == 0 else T.S2[:, :, 15 - k:31 - k], k == 0, False) for k in range(16)],
+           allc("RP") + ["S0", "S2"], ["B4"])
+        mm([(ps(4, 0, 128), T.MX[:, k:2048:16], T.SM[:, :, 15 - k:31 - k], False, k == 14) for k in range(15)], allc("MX") + ["SM"], ["B4"])
+        act(T.ZB[:, 3, :, 0], ps(6, 128, 256, 16), ["B6"], ["ZB3"])
+        act(T.ZB[:, 3, :, 15], ps(6, 143, 256, 16), ["B6"], ["ZB3"])
+        tt(T.AS[:, :, 3, :], T.SL[:, 1], T.S4[:, 2], A.mult, ["SL1", "SAB"], ["AS3"])
+        act(T.AS[:, :, 0:2, 0:15], T.AS[:, :, 2:4, 1:16], ["AS2", "AS3"], ["AS0"])
+        if not last:
+            tt(T.EM[:], T.SL[:], T.SE[:], A.mult, ["SL0", "SL1", "SE"], ["EM"])
+            act(T.ZB[:, 4, :, END], T.S4[:, 0, :, END], ["NS"], ["ZB4"])
+            act(T.LE[:, 0], T.ZB[:, 3, :, END], ["ZB3"], ["LE0"])
+            act(T.LE[:, 1], T.ZB[:, 3, :, END], ["ZB3"], ["LE1"], F.Identity, scale=-1.0, bias=8.0)
+        ts(T.PH[:, 0], ps(4, 0, 128), MAG64, A.add, ["B4"], ["PH0"], -MAG64, A.add)
+        tt(T.PH[:, 1], ps(4, 0, 128), T.PH[:, 0], A.subtract, ["B4", "PH0"], ["PH1"])
+        act(T.AS[:, :, 8, :], T.PH[:, 0], ["PH0"], ["AS8"])
+        mm([(ps(5, 0, 128), T.E0[:], T.ONE[:], True, False), (ps(5, 0, 128), T.PH[:, 0], I, False, True), (ps(5, 128, 256), T.PH[:, 1], I, True, True)],
+           ["PH0", "PH1", "II", "E0", "ONE"], ["B5"])
+        act(T.AS[:, :, 9, :], T.PH[:, 1], ["PH1"], ["AS9"])
+        if not last:
+            tt(T.EC[:], T.EM[:, 0], T.EM[:, 1], A.add, ["EM"], ["EC"])
+        cp(T.PL[:], ps(5, 0, 256), ["B5"], ["PL"])
+        js = [list(range(1, 5)), list(range(5, 9)), list(range(9, 12)), list(range(12, 15))]
+
+        def zmm(c):
+            it = []
+            for i, j in enumerate(js[c]):
+                o = ps(6 + c % 2, 128 * i, 128 * i + 128)
+                it += [(o, T.ZM[:, j - 1], T.PL[:, 0:128], True, False), (o, T.ZM[:, j - 1], T.PL[:, 128:256], False, True)]
+            mm(it, ["PL"] + ["ZM%d" % j for j in js[c]], ["B%d" % (6 + c % 2)])
+
+        def zcmp(c):
+            j0, n = js[c][0] - 1, len(js[c])
+            ts(T.CZ[:, 128 * j0:128 * (j0 + n)], ps(6 + c % 2, 0, 128 * n), 0.0, A.is_ge, ["B%d" % (6 + c % 2)], ["CZ%d" % c], 128.0, A.mult)
+
+        def zcnt(c):
+            it = []
+            if c == 0:
+                it += [(ps(4, 0, 128), T.IMID[:], T.PP[:], True, False), (ps(4, 0, 128), T.IEND[:], T.ONE[:], False, False)]
+                if not last:
+                    it.append((ps(4, 0, 128), T.ZB[:, 4], I, False, False))
+            it += [(ps(4, 0, 128), T.IMID[:], T.CZ[:, 128 * (j - 1):128 * j], False, j == 14) for j in js[c]]
+            mm(it, ["CZ%d" % c, "IMID", "IEND", "PP", "ONE", "II", "ZB4"], ["B4"])
+
+        def wmm(c):
+            mm([(T.ps[:, 128 * j:128 * j + 128], T.AS[:, :, :, j], I, True, True) for j in range(4 * c, min(4 * c + 4, 15))], ast + ["II"], ["B%d" % c])
+            n = 512 if c < 3 else 384
+            act(T.WE[:, 512 * c:512 * c + n], ps(c, 0, n), ["B%d" % c], ["WE%d" % c])
+        zmm(0), zmm(1)
+        if not last:
+            ts(T.AS[:, :, 6, :], T.EC[:], MAG32, A.add, ["EC"], ["AS6"], -MAG32, A.add)
+        tt(T.AS[:, :, 10, 0:15], T.PH[:, 0, :, 1:16], T.PH[:, 0, :, 0:15], A.subtract, ["PH0"], ["AS10"])
+        if not last:
+            tt(T.AS[:, :, 7, :], T.EC[:], T.AS[:, :, 6, :], A.subtract, ["EC", "AS6"], ["AS7"])
+            act(T.AS[:, :, 4:6, 0:15], T.AS[:, :, 6:8, 1:16], ["AS6", "AS7"], ["AS4"])
+        tt(T.AS[:, :, 11, 0:15], T.PH[:, 1, :, 1:16], T.PH[:, 1, :, 0:15], A.subtract, ["PH1"], ["AS11"])
+        zcmp(0), wmm(0), zmm(2), wmm(1)
+        zcmp(1), zmm(3), wmm(2), wmm(3), zcnt(0), zcnt(1)
+        zcmp(2), zcnt(2), zcmp(3), zcnt(3)
+        ud = T.UD[:, :, :, END]
+        tt(T.SS[:], T.UD[:, 0, :, END], T.UD[:, 1, :, END], A.add, ["UD"], ["SS"])
+        tt(T.PQ[:, :, 0], ud, T.S4[:, 0:3:2, :, END], A.mult, ["UD", "NS", "SAB"], ["PQ0"])
+        tt(T.PQ[:, :, 1], ud, T.S4[:, 1:4:2, :, END], A.mult, ["UD", "NS", "SAB"], ["PQ1"])
+        tt(T.SQ[:, 0], T.SS[:], T.S4[:, 1, :, END], A.mult, ["SS", "SAB"], ["SQ0"])
+        tt(T.SQ[:, 1], T.SS[:], T.S4[:, 2, :, END], A.mult, ["SS", "SAB"], ["SQ1"])
+        cp(lst(LW_), ps(4, 0, 128), ["B4"], ["LW"])
+        for h in range(2):
+            it = [(ps(h), Z128, T.LD[:, 0:512], True, False)]
+            for m in range(8):
+                it += [(ps(h, 64 * m, 64 * m + 64), T.PL[:, 128 * i:128 * i + 128], T.KS[:, :, 8 * h:8 * h + 8], False, False) for i in range(2)]
+            mm(it, ["ZERO", "LD0", "PL", "KS"], ["B%d" % h])
+        gather("a", T.WG, "WG", EW, WEt, LW_, "LW", 2, 4)
+        gather("v", T.WG, "WG", EW, WEt, LW_, "LW", 0, 2)
+        it = []
+        for k in range(16):
+            l_ = T.WG[:, k:2048:16]
+            if k % 15:
+                it.append((ps(2, k, 512, 16), l_, T.X3[:], True, True))
+            else:
+                e, o = k // 15, ps(2, k, 256, 16)
+                it += [(ps(2, k, 512, 16), l_, T.X3E[:], True, False), (o, I, T.S4[:, 1:3, :, k], False, False), (o, T.IM1[:], T.SQ[:, :, :, e], False, False),
+                       (o, I, T.PQ[:, 0, :, :, e], False, False), (o, I, T.PQ[:, 1, :, :, e], False, True)]
+        mm(it, allc("WG") + ["X3", "X3E", "SAB", "SQ0", "SQ1", "PQ0", "PQ1", "II", "IM1"], ["B2"])
+
+        def diffs(h):
+            it = []
+            ks = [k for k in range(8 * h, 8 * h + 8) if k % 15]
+            for k in ks:
+                o = ps(h, k % 8, 512, 8)
+                it += [(o, T.WG[:, k:2048:16], T.XP[:], False, False), (o, T.WG[:, k:2048:16], T.XH[:], False, k == ks[-1])]
+            mm(it, allc("WG") + ["XP", "XH"], ["B%d" % h])
+        if not last:
+            tt(T.DE[:], T.SE[:, 0, :, END], T.SE[:, 1, :, END], A.subtract, ["SE"], ["DE"])
+            tt(T.Q4[:], ud, T.SE[:, :, :, END], A.mult, ["UD", "SE"], ["Q4"])
+            tt(T.Q5[:, 0], T.UD[:, 1, :, END], T.DE[:], A.mult, ["UD", "DE"], ["Q50"])
+            tt(T.EP[:], T.SE[:, :, :, END], T.Q4[:], A.subtract, ["SE", "Q4"], ["EP"])
+        cp(SAB, ps(2, 0, 256), ["B2"], ["SAB"])
+        diffs(0)
+        mm([(ps(5, 0, 128), T.S4[:, 2], I, True, True)], ["SAB", "II"], ["B5"])
+        mm([(ps(4, 0, 128), T.S4[:, 1], I, True, True)], ["SAB", "II"], ["B4"])
+        diffs(1)
+        if not last:
+            tt(T.Q5[:, 1], T.UD[:, 0, :, END], T.DE[:], A.mult, ["UD", "DE"], ["Q51"])
+            tt(T.EP[:, 0], T.EP[:, 0], T.Q5[:, 0], A.subtract, ["EP", "Q50"], ["EP"])
+            act(lst(LA_), ps(5, 0, 128), ["B5"], ["LA"], F.Identity, bias=1280.0)
+            ts(lst(LB_), ps(4, 0, 128), 1280.0, A.add, ["B4"], ["LB"])
+            tt(T.EP[:, 1], T.EP[:, 1], T.Q5[:, 1], A.add, ["EP", "Q51"], ["EP"])
+    act(T.YO[:, 0:128], ps(5, 0, 128), ["B5"], ["YA"], F.Identity, bias=1280.0)
+    ts(T.C2[:, :, 0:8], ps(0), 0.0, A.is_ge, ["B0"], ["C20"])
+    act(T.YO[:, 128:256], ps(4, 0, 128), ["B4"], ["YB"], F.Identity, bias=1280.0)
+    dma("s", T.ya[:], T.YO[:, 0:128], ["YA"], [], ("o1", 32), 2300.0)
+    ts(T.C2[:, :, 8:16], ps(1), 0.0, A.is_ge, ["B1"], ["C21"])
+    dma("s", T.yb[:], T.YO[:, 128:256], ["YB"], [], ("o1", 32), 2300.0)
+    l_sums()
+    act(T.YO[:, 256:384], ps(3, 0, 128), ["B3"], ["YL"])
+    dma("a", T.yl[:], T.YO[:, 256:384], ["YL"], [], ("o2", 16), 2300.0)
+    if "o" not in ORDER:
+        ORDER["o"] = arrange(ops)
+    for i in ORDER["o"]:
+        issue(*ops[i][:5])
+    for s in ("v", "a", "p", "gq"):
+        g.wait_ge(T.sem[s], cnt[s])
+    for s, n in (("snt", 24), ("o1", 32), ("o2", 16)):
+        g.wait_ge(T.sem[s], n)

@@ -4,54 +4,47 @@ from concourse.mybir import AluOpType, ActivationFunctionType
 A = AluOpType
 F = ActivationFunctionType
 W = 2560
-H = 136
 f32, f16, b16, i32, u16 = "float32", "float16", "bfloat16", "int32", "uint16"
+RWN, SNN, WEN, PAD = 1280, 192, 1152, 1040
 
 
 def _sb(shape, dt):
     return ("sbuf", [128] + shape, dt)
 
 
+MC = ["IEND", "EP8", "EM8", "EM6", "E7", "EN8", "DLM", "DAE", "IM1", "I7", "IM7", "P8", "M8", "IMID", "MID32", "CD", "CD1", "DLA", "DME", "DAF", "DK", "I16", "I64", "N8", "I8", "N2"]
+MF = ["H16", "HM1", "I32", "SH"]
+LISTS = ["LA", "LB", "LZ", "LN", "LU", "LW", "LE"]
+NF = ["EM", "EE", "ME", "ZP", "Z2", "GM0", "GM1", "BV", "CP", "EP", "EC", "RC", "XX", "YY", "SC", "SEH", "SEL", "SPH", "SPL"]
+NH = ["A16", "B16", "AE", "BE", "LL", "LP", "L2L", "M8L", "FD", "UP", "DN", "W8", "S8", "UA", "UB", "UN", "DA", "DB", "DNN"]
+PADS = ["a", "b", "eh", "el", "dh", "dl", "l0", "cm", "c0", "c1", "n0", "n1"]
 SCRATCH = {
     "ps": ("psum", [128, 4096], f32),
-    "X": _sb([W], b16), "G": _sb([W], b16), "NB": _sb([W], i32), "WE": _sb([2048 + W], f32),
-    "RW0": _sb([2048 + 2 * H], f32), "RW1": _sb([2048 + 2 * H], f32), "RW2": _sb([2048 + 2 * H], f32),
-    "SN0": _sb([2 * H], f32), "SN1": _sb([2 * H], f32), "SN2": _sb([2 * H], f32),
-    "XA": _sb([2048], b16), "D": _sb([2048], b16), "L2": _sb([2048], f16), "LD": _sb([2048], f16), "GA": _sb([2048], b16), "GB": _sb([2048], b16),
-    "TT": _sb([2048], f16), "PR0": _sb([2048], f32), "PR1": _sb([2048], f32), "PR2": _sb([2048], f32), "PR3": _sb([2048], f32),
-    "NG": _sb([2048], f16), "XN": _sb([2048], b16), "RP": _sb([2048], f16), "MX": _sb([2048], f16),
-    "CZ": _sb([1792], f16), "WG": _sb([2048], f16), "AS": _sb([8, 16, 16], f16), "C2": _sb([64, 16], f16),
-    "LST": _sb([1024], u16), "PI": _sb([384], i32), "H16": _sb([384], f16), "EI": _sb([160], i32), "EF": _sb([480], f32),
-    "S4": _sb([4, 8, 16], f16), "SE": _sb([2, 8, 16], f32), "LL": _sb([3, 8, 16], f16), "MM": _sb([3, 8, 16], f16),
-    "EM": _sb([2, 8, 16], f32), "EE": _sb([8, 16], f32), "ZP": _sb([2, 128], f16), "DE": _sb([8, 2], f32),
-    "GM": _sb([2, 128], f32), "LW": _sb([2048], b16), "XN2": _sb([2048], f16), "AB": _sb([128], f32), "CM": _sb([2, 8, 16], f16),
-    "UD": _sb([2, 8, 16], f16), "SL": _sb([2, 8, 16], f16), "EC": _sb([8, 16], f32), "PH": _sb([2, 8, 16], f16), "PL": _sb([256], f16),
-    "ZB": _sb([5, 8, 16], f16), "PQ": _sb([2, 2, 8, 2], f16), "SS": _sb([8, 2], f16), "SQ": _sb([2, 8, 2], f16),
-    "EP": _sb([2, 8, 2], f32), "Q4": _sb([2, 8, 2], f32), "LE": _sb([2, 8, 2], f32), "Q5": _sb([2, 8, 2], f32), "YO": _sb([384], f32),
-    "I32": _sb([128], f32), "UP": _sb([2, 128], f32),
-    "ZERO": _sb([512], b16), "ONE": _sb([128], b16), "II": _sb([512], b16), "LT": _sb([16], b16), "PP": _sb([128], b16), "BO": _sb([8], f32),
-    "X3": _sb([32], b16), "X3E": _sb([32], b16), "XP": _sb([64], b16), "XH": _sb([64], b16), "KS": _sb([8, 16], b16),
-    "ZM": _sb([14, 128], b16), "SM": _sb([8, 32], b16), "S2": _sb([8, 32], b16), "S0": _sb([128], b16),
+    "X": _sb([W], b16), "G": _sb([W], b16), "NB": _sb([W], i32), "ET": _sb([W], i32),
+    "RW": _sb([6 * RWN], f32), "SN": _sb([6, 3, 64], f32), "WE": _sb([2 * WEN], f32),
+    "XA": _sb([2 * PAD], b16), "XU": _sb([2 * PAD], b16), "L2": _sb([2 * PAD], f16),
+    "D": _sb([2048], b16), "GA": _sb([2048], b16), "DG": _sb([2048], b16), "LG": _sb([2048], f16),
+    "TT": _sb([2048], f16), "NG": _sb([2048], f16), "AD": _sb([2048], f16), "WG": _sb([2048], f16), "CZ": _sb([1792], b16),
+    "PR0": _sb([2048], f32), "PR1": _sb([2048], f32), "PR2": _sb([2048], f32), "PR3": _sb([2048], f32), "EG": _sb([512], f16),
+    "LST": _sb([128 * len(LISTS)], u16), "NFB": _sb([128 * len(NF)], f32), "NHB": _sb([128 * len(NH)], f16),
+    "PB": _sb([2 * len(PADS), 18, 8], f16), "PH": _sb([4, 130], f16), "IT": _sb([16, 8], b16), "BOX": _sb([128], b16),
+    "PI": _sb([384], i32), "EI": _sb([3, 160], i32), "YO": _sb([384], f32),
+    "II": _sb([8, 16], b16), "MCB": _sb([len(MC), 8, 16], b16), "MFB": _sb([len(MF), 8, 16], f32),
+    "BK": _sb([16, 8, 16], b16), "ZM": _sb([14, 128], b16), "ZK": _sb([128], b16),
+    "ZERO": _sb([512], b16), "ONE": _sb([128], b16), "PP": _sb([64], b16), "KI": _sb([128], b16), "BO": _sb([8], f32),
+    "PM": _sb([2, 18, 8], f16), "CK": _sb([2, 144], f16), "EK": _sb([3, 144], f16), "E0": _sb([6, 8], f16), "SM": _sb([15, 128], b16),
+    "XH": _sb([8, 8], b16), "XL": _sb([2, 8], b16), "KS": _sb([2, 64], b16), "CR": _sb([128], b16), "DL": _sb([128], f16),
 }
-DIAG = ["I8", "I2", "IM1", "IM8", "IM2", "I7", "I16", "DMUL", "DADD", "DA", "DB", "DC", "DD", "IMID", "IEND", "E0", "ZK"]
-for _n in DIAG:
-    SCRATCH[_n] = _sb([128], b16)
-SEMAPHORES = ["v", "a", "p", "gq", "dx", "dg", "dn", "de", "dpa", "dpb", "dpl", "dw", "h0", "h1", "h2", "snt", "o1", "o2"]
-MAG32 = 402653184.0
-MAG64 = 805306368.0
+SEMAPHORES = ["v", "a", "p", "gq", "dx", "dg", "dn", "de", "dw", "dz", "dpa", "dpb", "dpl", "snt", "o1", "o2"] + [n + str(i) for n in "hw" for i in range(6)]
+MAG = 12582912.0
 END = slice(0, 16, 15)
-
-
-LISTS = ("LA", "LB", "Ll", "LZ", "LN", "LU", "LX", "LW")
-CYC, GAM, PCYC, VFIX, AFIX, PFIX, WAKE = 0.83, 1.56, 0.417, 60.0, 90.0, 10.0, 120.0
-TRIES = [(300.0, 0, 0.0)]
+CYC, GAM, PCYC, FIX, WAKE = 0.83, 1.56, 0.417, 50.0, 70.0
+OPT = {"lead": 6000.0, "turns": 600, "seed": 2, "ud": 0, "e1": "aa", "radd": "av", "D": 2, "DG": 2, "cz": "aa", "wg": "aa", "ng": "aa", "e0": "aa", "sg": "a", "tail": 5, "ga": "aa", "xu": "aa", "xa": "aa", "dma": 2500.0, "rem": 3500.0}
 ORDER = {}
-PLAN = "2b02080004030g010h060a072c092h0x2e3p3k100z3u2g2f0y2j2i0w2d2k2n3f2q050i2m0b2s2t0l2p0c2v0j2r2u0m2w2y2l0k390n2x360o0q0p3g0r383l0s3h0u373m0t0v3n3a1c3i0d32113b3o0e1534333j0f3q2z16354k3v3r19313c173w3s443d123x453e3y1846401a413z42472o3t431b4r13498l4l1d14304o4s1e4p1v4y4v1s1w4b4z4a4w1n4c1o564d521p4m4g1j551k501l48594e1m4t1q4n1r1f574q5c1g1h5a5d1i581t4u5b1x531u4x1y515r225e1z54235f5s205h245t215g5u25285j5m26295i5n272a5l5o5k5p4f615q5w5x5v5y5z4h60624i634j7b64656766686f696a6b8a6c8b6d6g6e8d6h6i6k6y6j6l6s786m6t6n6p6o6u6z6r6q6x6w706v7a76739c74779d727c7d7j75717n798c7p7e7q8m7f7g7o7i7h7r7k808o828e818n7m8u8v8y837l7y7w7s7t7x7z7v7u8884868587898h8f8j8i8g8k8t8p938s8r8q8x8w92b290919e959faaev8z94abac9iadb19b9j9ga09v9ha59q98969w9r979x9k9s9z9m9u9l9ta19n9aa699a29y9oa4a7af9pa3aealaja8akagamauahanawaqavb3a9aybfaxb5azb9bhb0bgb4b8babmb6bcbbb7bnbdbjbpbeaibkaoc1bic2bqblboc3brc4bubwapbxbybzbsarc0c5c6btasc7atdlbvc8c9cbcacccdcecfcgchcicjcpckclelcmekcncqcoemcrcscucvctcyd8cwczcxd7d0d3d2d9d1d4dkd5dad6dcdgdedhdtfnfmdddndmeodxdfdidzendbe0dodjexdpdqdydrdse1dueaewecf4ebeydvf5f8ede3e2dwe4eee8e5e9ege6eiefe7ehejeqepetesereuf3ezfdf1f0fcf6f2fof9faf7fefhfpfqfffbflgkfrg0gag5gfg1figlfggmg2fsgng3fufthbg6fvg4gbg7fkfwgcg8fyg9fxgggdfzh4ghgpgugvgtgigogwgqgjgxh5h6h0fjhrhpgrh7gehshch8hkhihfh9hqhghahlhjhthdhxhmhuhehvhwhnhhhyhogsgyhzibi0ici1idi4iei3i6i7i2i8i5i9gziliaigihifiih1ijh2imh3ikinioipiriqisitiziuivkmiwknixj0iykpj1j2j4jij3j5j8jsj6j9j7jdjcjajjjbjejhjfjkjgjljmjtjojqjnjrkqkojpjujvjwk2jyjxk3jzkck0kdk1k4kekakgkfk7k5kikbk6k8kkkhk9kjklkskrkvkuktl1kyl6kwl3l8kxl0kzl9l4l2l7lal5"
-OPT = {"td": (0, 1, 2, 3), "ea": "aa", "eb": "vv", "lb": ("vvaa", "vvaa"), "ng": ("av", "av"), "gb": ("aaaa", "aaaa")}
 
 
 def bank(t):
-    return t[0] == "B" and t[1:].isdigit()
+    return t[0] == "b" and t[2] == "."
 
 
 def arrange(ops):
@@ -62,8 +55,8 @@ def arrange(ops):
         for t in o[2] + o[3]:
             if t in lw:
                 pred[i].add(lw[t])
-            if t in o[3] or bank(t):
-                pred[i].update(j for j in rd.get(t, ()) if t in o[3] or ops[j][0] != o[0])
+            if t in o[3]:
+                pred[i].update(rd.get(t, ()))
         for t in o[2]:
             rd.setdefault(t, []).append(i)
         for t in o[3]:
@@ -74,50 +67,60 @@ def arrange(ops):
     for i in range(n):
         for j in pred[i]:
             succ[j].append(i)
-    plan = [int(PLAN[i:i + 2], 36) for i in range(0, len(PLAN), 2)]
-    if sorted(plan) == list(range(n)):
-        at = {i: k for k, i in enumerate(plan)}
-        if all(at[j] < at[i] for i in range(n) for j in pred[i]):
-            return plan
-    best = None
-    for win, seed, amp in TRIES:
-        noise = [1.0 + amp * float(x) for x in np.random.default_rng(seed).random(n)]
-        pr = [0.0] * n
-        for i in range(n - 1, -1, -1):
-            pr[i] = ops[i][5] * noise[i] + ops[i][6] + WAKE + max([pr[j] for j in succ[i]], default=0.0)
-        left = [len(p) for p in pred]
-        est = [0.0] * n
-        ready = {}
-        for i in range(n):
-            if not left[i]:
-                ready.setdefault(ops[i][0], []).append(i)
-        free, order, end = {}, [], 0.0
-        while len(order) < n:
-            pick = None
-            for q, l in ready.items():
-                if not l:
-                    continue
-                f = free.get(q, 0.0)
-                t0 = max(f, min(est[i] for i in l))
-                i = max((i for i in l if est[i] <= t0 + win), key=lambda i: pr[i])
-                s = max(f, est[i])
-                if pick is None or s < pick[0]:
-                    pick = (s, i, q)
-            s, i, q = pick
-            ready[q].remove(i)
-            order.append(i)
-            free[q] = s + ops[i][5]
-            done = free[q] + ops[i][6]
-            end = max(end, done)
-            for j in succ[i]:
-                est[j] = max(est[j], done + (0.0 if q == "p" == ops[j][0] else WAKE))
+    needs = [[o[0]] + sorted(set(t[1] for t in o[2] + o[3] if bank(t))) for o in ops]
+
+    def place(before, after, key, back):
+        left = [len(p) for p in before]
+        ready = [i for i in range(n) if not left[i]]
+        busy, start, end = {}, [0.0] * n, [0.0] * n
+        while ready:
+            i = max(ready, key=lambda i: key[i])
+            ready.remove(i)
+            q, c, late = ops[i][0], ops[i][5], ops[i][6]
+            s = max([end[j] + (0.0 if q == "p" == ops[j][0] else WAKE) for j in before[i]], default=0.0) + (late if back else 0.0)
+            moved = True
+            while moved:
+                moved = False
+                for k, res in enumerate(needs[i]):
+                    l = busy.setdefault(res, [])
+                    for t0, t1, q2 in l[find(l, s - 2500.0):]:
+                        gap = WAKE if k and q2 != q else 0.0
+                        if t0 - gap >= s + c:
+                            break
+                        if t1 + gap > s and (k == 0 or q2 != q):
+                            s, moved = t1 + gap, True
+            for res in needs[i]:
+                busy[res].insert(find(busy[res], s), (s, s + c, q))
+            start[i], end[i] = s, s + c + (0.0 if back else late)
+            for j in after[i]:
                 left[j] -= 1
                 if not left[j]:
-                    ready.setdefault(ops[j][0], []).append(j)
-        if best is None or end < best[0]:
-            best = (end, order, (win, seed, amp))
-    ORDER["best"] = (best[0], best[2])
-    return best[1]
+                    ready.append(j)
+        return start, end
+
+    def find(l, t):
+        lo, hi = 0, len(l)
+        while lo < hi:
+            m = (lo + hi) // 2
+            lo, hi = (m + 1, hi) if l[m][0] < t else (lo, m)
+        return lo
+
+    def settle(key):
+        one = place(pred, succ, key, False)
+        two = place(pred, succ, place(succ, pred, one[1], True)[1], False)
+        return min((max(one[1]), one[0]), (max(two[1]), two[0]))
+    key = [0.0] * n
+    for i in range(n - 1, -1, -1):
+        key[i] = ops[i][5] + ops[i][6] + WAKE + max([key[j] for j in succ[i]], default=OPT["lead"] * (ops[i][7] == 0))
+    best = settle(key)
+    rng = np.random.default_rng(OPT["seed"])
+    for _ in range(OPT["turns"]):
+        mid, wide, s, by = rng.uniform(0, best[0]), rng.uniform(2000, 10000), int(rng.integers(2)), rng.normal(0, 2500)
+        new = settle([(by if ops[i][7] == s and abs(t - mid) < wide else 0.0) - t for i, t in enumerate(best[1])])
+        if new[0] <= best[0]:
+            best = new
+    ORDER["t"] = best
+    return sorted(range(n), key=lambda i: (best[1][i], i))
 
 
 def rank_program(g, core, T, topo):
@@ -130,32 +133,27 @@ def rank_program(g, core, T, topo):
     V, S, P = g.vector, g.scalar, g.tensor
     cnt = {"v": 0, "a": 0, "p": 0, "gq": 0}
     seen = {q: {} for q in Q}
-    lastw, readers = {}, {}
-
-    def need(q, ev):
-        s, n = ev
-        if s == "p" and q == "p":
-            return
-        if seen[q].get(s, 0) < n:
-            seen[q][s] = n
-            Q[q].wait_ge(T.sem[s], n)
-
-    ops = []
+    lastw, readers, users = {}, {}, {}
+    ops, lead = [], [0.0]
 
     def op(q, fn, r=(), w=(), ev=None, cost=100.0, late=0.0):
-        ops.append((q, fn, list(r), list(w), ev, cost, late))
+        ops.append((q, fn, list(r), list(w), ev, cost, late, lead[0]))
 
     def issue(q, fn, r, w, ev):
         want = {}
-        for t in list(r) + list(w):
+        for t in r + w:
             evs = [lastw.get(t)]
-            if t in w or bank(t):
-                evs += [e for e in readers.get(t, {}).items() if t in w or e[0] != q]
+            if t in w:
+                evs += readers.get(t, {}).items()
+            if bank(t):
+                evs += [e for e in users.get(t[1], {}).items() if e[0] != q]
             for e in evs:
                 if e is not None:
                     want[e[0]] = max(want.get(e[0], 0), e[1])
-        for e in want.items():
-            need(q, e)
+        for s, n in want.items():
+            if not s == "p" == q and seen[q].get(s, 0) < n:
+                seen[q][s] = n
+                Q[q].wait_ge(T.sem[s], n)
         ins = fn()
         if ev is None:
             cnt[q] += 1
@@ -168,6 +166,9 @@ def rank_program(g, core, T, topo):
         for t in w:
             lastw[t] = ("h" + t[4:], 8) if t[:4] == "HALO" else ev
             readers[t] = {}
+        for t in r + w:
+            if bank(t):
+                users.setdefault(t[1], {})[q] = ev[1]
 
     def nel(ap):
         n = 1
@@ -175,507 +176,473 @@ def rank_program(g, core, T, topo):
             n *= x
         return n
 
-    def gathers(r):
-        return any(t in LISTS for t in r)
-
-    def vcost(out, r, k):
-        return 50 + nel(out) * GAM * CYC if gathers(r) else VFIX + max(64, nel(out) * k) * CYC
-
     def short(*aps):
         return all("16" in str(x.dtype) for x in aps)
 
+    def cost(out, r, k):
+        return FIX + nel(out) * GAM * CYC if any(t[:2] in LISTS for t in r) else FIX + max(64, nel(out) * k) * CYC
+
     def tt(out, a, b, o, r, w):
-        k = 1.0 if any(bank(t) for t in r) else 2.0
-        op("v", lambda: V.tensor_tensor(out, a, b, o), r, w, cost=vcost(out, r, k))
+        op("v", lambda: V.tensor_tensor(out, a, b, o), r, w, cost=cost(out, r, 1.0 if any(bank(t) for t in r) else 2.0))
 
     def ts(out, a, s1, o1, r, w, s2=None, o2=None):
-        c = vcost(out, r, 1.0 if gathers(r) or not short(out, a) else 0.5)
+        c = cost(out, r, 0.5 if short(out, a) else 1.0)
         if o2 is None:
             op("v", lambda: V.tensor_scalar(out, a, s1, None, o1), r, w, cost=c)
         else:
             op("v", lambda: V.tensor_scalar(out, a, s1, s2, o1, o2), r, w, cost=c)
 
-    def cp(out, a, r, w):
-        op("v", lambda: V.tensor_copy(out, a), r, w, cost=vcost(out, r, 1.0))
-
-    def fill(out, w):
-        op("v", lambda: V.memset(out, 0.0), (), w, cost=vcost(out, (), 0.5 if short(out) else 1.0))
+    def fill(out, w, v=0.0):
+        op("v", lambda: V.memset(out, v), (), w, cost=cost(out, (), 0.5 if short(out) else 1.0))
 
     def act(out, a, r, w, func=F.Copy, **kw):
-        op("a", lambda: S.activation(out, a, func, **kw), r, w, cost=65 + nel(out) * GAM * CYC if gathers(r) else AFIX + nel(out) * CYC)
+        op("a", lambda: S.activation(out, a, func, **kw), r, w, cost=cost(out, r, 1.0) + 15.0)
+
+    def move(q, out, a, r, w, bias=None):
+        if q == "a" and bias is None:
+            act(out, a, r, w)
+        elif q == "a":
+            act(out, a, r, w, F.Identity, bias=bias)
+        elif bias is None:
+            op("v", lambda: V.tensor_copy(out, a), r, w, cost=cost(out, r, 0.5 if short(out, a) else 1.0))
+        else:
+            ts(out, a, bias, A.add, r, w)
 
     def mm(items, r, w):
         def fn():
             for o, l, rh, st, sp in items:
                 ins = P.matmul(o, l, rh, st, sp)
             return ins
-        op("p", fn, r, w, cost=sum(PFIX + max(64, nel(x[2])) * (1 if short(x[1]) else 4) * PCYC for x in items))
+        op("p", fn, r, w, cost=sum(max(64, nel(x[2])) * (1 if short(x[1]) else 4) * PCYC for x in items))
+
+    def grp(out, pairs, r, w, start=True, stop=True):
+        mm([(out, l, rh, start and i == 0, stop and i == len(pairs) - 1) for i, (l, rh) in enumerate(pairs)], r, w)
 
     def dma(q, out, in_, r, w, ev, late):
         op(q, lambda: Q[q].dma_start(out, in_), r, w, ev, 100.0, late)
 
-    def grp(out, pairs, r, w):
-        mm([(out, l, rh, i == 0, i == len(pairs) - 1) for i, (l, rh) in enumerate(pairs)], r, w)
-
     def ps(b, c0=0, c1=512, st=1):
         return T.ps[:, 512 * b + c0:512 * b + c1:st]
 
-    def ch(t, c, o=0):
-        return t[:, o + 512 * c:o + 512 * c + 512]
+    def mc(n):
+        return T.MCB[:, MC.index(n)]
 
-    def gat(win, lst, c0=0, c1=4):
-        return win.indirect(T.LST[:, 128 * lst + 32 * c0:128 * lst + 32 * c1])
+    def mf(n):
+        return T.MFB[:, MF.index(n)]
+    I = T.II[:]
 
-    def lst(i):
-        return T.LST[:, 128 * i:128 * i + 128]
-
-    def allc(n):
-        return [n + str(c) for c in range(4)]
-    LB_, LA_, LL_, LZ_, LN_, LU_, LX_, LW_ = range(8)
-    I = T.II[:, 0:128]
-    XW, GW, NW, EW, LW = T.X[:, 0:W], T.G[:, 0:W], T.NB[:, 0:W], T.WE[:, 0:2048 + W], T.LT[:, 0:16]
-    ET = T.WE[:, 2048:2048 + W]
-    SAB = T.S4[:, 1:3]
-    WEe = ["WEe", "WEr0", "WEr1"]
-    WEt = allc("WE") + WEe
-
-    def reduce16(src, tok, bank, c0, rhs=None, rtok=("BO",), n=8):
-        step = 4 if rhs is None else 16
-        for k0 in range(0, 16, step):
-            mm([(ps(bank, c0 + k, c0 + 16 * n, 16), src[:, k:2048:16], T.BO[:] if rhs is None else rhs(k), True, True) for k in range(k0, k0 + step)],
-               list(tok) + list(rtok), ["B%d" % bank])
-
-    dma("s", T.X[:], T.xrec[:], [], ["X", "qs"], ("dx", 16), 4600.0)
-    dma("a", T.PI[:, 128:256], T.pa[:], [], ["PIa"], ("dpa", 16), 2300.0)
-    dma("a", T.EI[:], T.erec[:], [], ["EI"], ("de", 16), 2300.0)
-    dma("s", T.PI[:, 0:128], T.pb[:], [], ["PIb"], ("dpb", 16), 2300.0)
+    dma("a", T.EI[:, 0], T.erec[:], [], ["EI"], ("de", 16), 2300.0)
+    dma("s", T.X[:], T.xrec[:], [], ["X"], ("dx", 16), 4600.0)
+    dma("a", T.PI[:, 0:128], T.pa[:], [], ["PIa"], ("dpa", 16), 2300.0)
+    dma("a", T.PI[:, 128:256], T.pb[:], [], ["PIb"], ("dpb", 16), 2300.0)
     dma("a", T.PI[:, 256:384], T.lam[:], [], ["PIl"], ("dpl", 16), 2300.0)
-    dma("s", T.G[:], T.grec[:], ["qs"], ["G"], ("dg", 16), 4600.0)
+    op("v", lambda: V.memset(T.ET[:], 0), (), ["ET"], cost=W * CYC)
+    ts(T.EI[:, 1], T.EI[:, 0], 10, A.arith_shift_right, ["EI"], ["EI1"])
+    ts(T.EI[:, 2], T.EI[:, 0], 1023, A.bitwise_and, ["EI"], ["EI2"])
+    for i in range(2):
+        dma("s", T.ET[i:128:16, :], T.EI[:, 1 + i], ["EI%d" % (1 + i), "ET"], ["ET%d" % i], ("dw", 32), 2300.0)
+    ETt = ["ET0", "ET1"]
+    dma("s", T.G[:], T.grec[:], ["X"], ["G"], ("dg", 16), 4600.0)
+    dma("s", T.NB[:], T.nbr[:], ["X"], ["NB"], ("dn", 16), 9000.0)
 
     def iota(n, pat, base=0, cm=0, ap=None):
         o = T[n][:] if ap is None else ap
         op("gq", lambda: g.iota(o, pat, base, cm, allow_small_or_imprecise_dtypes=True), w=[n], cost=130 + 2 * CYC * nel(o))
 
-    def sel(n, src, pat, cmp, fill, base=0, cm=1, ap=None, sap=None):
+    def sel(n, src, pat, cmp, v, base=0, cm=1, ap=None, sap=None):
         o = T[n][:] if ap is None else ap
-        op("gq", lambda: g.affine_select(o, T[src][:] if sap is None else sap, pat, cmp, fill, base, cm), [src], [n], cost=170 + 2 * CYC * nel(o))
+        op("gq", lambda: g.affine_select(o, T[src][:] if sap is None else sap, pat, cmp, v, base, cm), [src], [n], cost=170 + 2 * CYC * nel(o))
+
+    def rows(n, lo, hi, lead=(), tail=()):
+        sel(n, n, list(lead) + [[-16, 8]] + list(tail), A.is_ge, 0.0, -lo, 1)
+        sel(n, n, list(lead) + [[16, 8]] + list(tail), A.is_ge, 0.0, hi, -1)
+
+    def put(out, src, v, w, r=()):
+        act(out, src, ["II"] + list(r), [w], F.Identity, scale=float(v))
     Z128 = T.ZERO[:, 0:128]
+    iota("KI", [[0, 128]])
+    sel("II", "KI", [[-1, 128]], A.not_equal, 1.0)
+    sel("IT", "KI", [[-1, 16], [-16, 8]], A.not_equal, 0.125)
+    iota("KI", [[0, 8], [1, 16]])
+    iota("PP", [[1, 64]])
+    iota("ONE", [[0, 128]], 1)
+    iota("BO", [[0, 8]], 1)
+    rows("BO", 0, 15)
+    for n in ("PM", "CK", "EK", "PB", "PH", "ZERO"):
+        fill(T[n][:], [n])
+    for n, k in (("XH", 64), ("XL", 16), ("CR", 128)):
+        iota(n, [[0, k]])
+    for s in range(2):
+        fill(T.WE[:, WEN * s + 1024:WEN * s + WEN], ["WE%d" % s])
+        for row in range(10, 16):
+            dma("s", T.WE[row:128:16, WEN * s:WEN * s + 1024], T.WE[:, 1088:WEN], ["WE0", "G"], ["WR%d%d" % (row, s)], ("dz", 192), 2500.0)
+    fill(T.L2[:, 512:513 + PAD:PAD], ["L2p"])
+    for n in ("XA", "XU"):
+        iota(n + "p", [[0, 2]], ap=T[n][:, 1024:1025 + PAD:PAD])
+        iota(n + "p", [[0, 2]], ap=T[n][:, 1025:1026 + PAD:PAD])
+    for i in range(16):
+        act(T.BK[:, :, :, i], T.IT[:], ["IT"], ["BK%d" % i])
+    BKt = ["BK%d" % i for i in range(16)]
 
-    def diag(n, v):
-        sel(n, "ZERO", [[-1, 128]], A.not_equal, v, sap=Z128)
+    fill(T.MCB[:, 0:8], ["MC0"])
+    fill(T.MFB[:, 0:2], ["MC0"])
 
-    def keepdiag(n):
-        sel(n, n, [[-1, 128]], A.is_equal, 0.0)
+    def diag(n, v, single=(), buf=T.MCB, names=MC, step=0):
+        i = names.index(n)
+        if v:
+            sel(n, "ZERO", [[-1, 128]], A.not_equal, float(v), -step, ap=buf[:, i], sap=Z128)
+        for k, d, row, u in single:
+            o = buf[:, i, :, k:16:d]
+            sel(n, n if v else "MC0", [[-16, 8], [-d, o.shape[2]]], A.not_equal, float(u), -row, ap=o, sap=o)
+    for n, v in (("P8", 0.125), ("M8", -0.125), ("IM1", -1), ("I16", 16), ("I64", 64), ("I7", 0.875), ("IM7", -0.875), ("N8", -8), ("I8", 8), ("N2", -2)):
+        diag(n, v)
+    for n, v, e in (("IEND", 0, 1), ("EP8", 0, 0.125), ("EM8", 0, -0.125), ("EM6", 0, -6), ("E7", 0, 7), ("EN8", 0, -8),
+                    ("IMID", 1, 0), ("MID32", 32, 0), ("CD", 448, 1024), ("CD1", 224, 1024)):
+        diag(n, v, [(0, 15, 0, e)])
+    diag("DLM", 0, [(0, 16, 0, 7), (15, 16, 15, -7)])
+    diag("DLA", 1, [(0, 16, 0, -512), (15, 16, 15, -71)])
+    diag("DME", 16, [(0, 8, 0, 2)])
+    diag("DAE", 0, [(0, 8, 0, 512)])
+    diag("DAF", -1, [(0, 16, 0, 0), (8, 16, 8, -7)])
+    tt(mc("DK"), I, T.KI[:], A.mult, ["II", "KI"], ["DK"])
+    diag("I32", 1, buf=T.MFB, names=MF)
+    diag("SH", 1, [(15, 16, 16, 0)], T.MFB, MF, 1)
+    sel("SH", "SH", [[-1, 128]], A.not_equal, -1.0, 1, ap=mf("SH"), sap=mf("SH"))
+    sel("SH", "SH", [[-16, 8]], A.not_equal, 0.0, 1, ap=T.MFB[:, MF.index("SH"), :, 0], sap=T.MFB[:, MF.index("SH"), :, 0])
+    diag("H16", 0, [(15, 16, 0, 1)], T.MFB, MF)
+    diag("HM1", 0, [(0, 16, 15, -1)], T.MFB, MF)
+    for e in range(2):
+        put(T.PM[:, e, 1:16:2], T.II[:, :, e:16:2], 1, "PM%d" % e, ["PM"])
+        put(T.CK[:, e, 15:143:16], T.II[:, :, 15 * e], 1, "CK%d" % e, ["CK"])
+    for i, (row, v) in enumerate(((0, 1), (1, 1 / 1024), (0, -1), (1, -1 / 1024), (0, 1), (1, 1 / 1024))):
+        put(T.E0[:, i], T.II[:, :, row], v, "E0")
+    tt(T.EK[:, 0, 15:143:16], T.E0[:, 0], T.E0[:, 1], A.add, ["E0", "EK"], ["EK0"])
+    put(T.EK[:, 1, 15:143:16], T.EK[:, 0, 15:143:16], -0.125, "EK1", ["EK0"])
+    put(T.EK[:, 2, 15:143:16], T.EK[:, 0, 15:143:16], 0.125, "EK2", ["EK0"])
+    grp(ps(1, 384, 448), [(mc("DLM"), T.PP[:]), (mc("DLA"), T.ONE[:, 0:64])], ["DLM", "DLA", "PP", "ONE"], ["b1.6"])
+    grp(ps(1, 448, 480), [(mc("DME"), T.PP[:, 0:32]), (mc("DK"), T.ONE[:, 0:32]), (mc("DAE"), T.ONE[:, 0:32]), (mc("DAF"), T.ONE[:, 0:32])], ["DME", "DK", "DAE", "DAF", "PP", "ONE"], ["b1.7"])
+    grp(ps(1, 480, 512), [(mc("I16"), T.PP[:, 0:32]), (mc("DK"), T.ONE[:, 0:32]), (mc("I64"), T.ONE[:, 0:32])], ["I16", "DK", "I64", "PP", "ONE"], ["b1.7"])
+    act(T.DL[:], ps(1, 384, 512), ["b1.6", "b1.7"], ["DL"])
+    sel("BOX", "ONE", [[0, 128]], A.is_gt, 1 / 32, 0, 0)
+    rows("BOX", 0, 15, tail=[[0, 16]])
+    for k in range(15):
+        sel("SM%d" % k, "BOX", [[0, 8], [1, 16]], A.is_gt, 0.0, -k, 0, ap=T.SM[:, k])
+    iota("ZK", [[0, 8], [1, 16]])
+    sel("ZK", "ZK", [[-16, 8], [0, 16]], A.is_equal, 0.0, -15)
+    for j in range(1, 15):
+        sel("ZM%d" % j, "ZK", [[-16, 8], [0, 16]], A.not_equal, -15.0, -j, ap=T.ZM[:, j - 1])
+    iota("KS", [[128, 2], [0, 8], [16, 8]])
+    sel("KS", "KS", [[0, 2], [-16, 8], [0, 8]], A.is_equal, 0.0, -15)
+    sel("KS", "KS", [[8, 2], [0, 8], [1, 8]], A.not_equal, 0.0, -15, 0)
+    for n, q, row, v in [("XH", 0, 0, 1), ("XH", 1, 1, 1), ("XH", 2, 2, 1), ("XH", 3, 3, 1), ("XH", 4, 4, 1), ("XH", 4, 2, -1), ("XH", 5, 5, 1), ("XH", 5, 3, -1),
+                         ("XH", 6, 6, -255), ("XH", 6, 7, 15), ("XH", 7, 6, -30), ("XH", 7, 7, 30),
+                         ("XL", 0, 8, -255), ("XL", 0, 9, 15), ("XL", 1, 8, -30), ("XL", 1, 9, 30)]:
+        sel(n, n, [[-16, 8]], A.not_equal, float(v), -row, ap=T[n][:, q], sap=T[n][:, q])
+    for c, v in ((0, 1 / 1024), (64, 1 / 8192)):
+        sel("CR", "CR", [[0, 64]], A.not_equal, v, ap=T.CR[:, c:c + 64], sap=T.CR[:, c:c + 64])
 
-    def rows(n, lead, lo, hi, tail=(), ap=None):
-        sel(n, n, [[-lead[0], lead[1]], [-16, 8]] + list(tail), A.is_ge, 0.0, -lo, 1, ap, ap)
-        sel(n, n, [[lead[0], lead[1]], [16, 8]] + list(tail), A.is_ge, 0.0, hi, -1, ap, ap)
-    GK = [[-16, 8], [256, 16]]
-
-    def consts0():
-        iota("ZERO", [[0, 512]])
-        sel("II", "ZERO", [[-1, 128]], A.not_equal, 1.0, ap=I, sap=Z128)
-        iota("LT", [[1, 16]])
-        diag("I8", 8.0)
-        iota("X3E", [[1, 2], [0, 16]])
-        rows("X3E", [0, 4], 6, 7)
-        iota("BO", [[0, 8]], 1)
-        rows("BO", [0, 1], 0, 15)
-        iota("ONE", [[0, 128]], 1)
-        iota("PP", [[1, 128]])
-        diag("I2", 2.0)
-        diag("I16", 16.0)
-        sel("DMUL", "I16", GK, A.not_equal, 1.0)
-        iota("DADD", [[0, 8], [1, 16]], H - 1)
-        sel("DADD", "DADD", [[0, 8], [1, 16]], A.not_equal, 0.0, 0, 0)
-        keepdiag("DADD")
-        for n, b, cm in (("DA", 0, 16), ("DB", H + 1, -1), ("DC", 2048, -16), ("DD", -14, 1)):
-            iota(n, [[0, 128]], b, cm)
-            keepdiag(n)
-        sel("II4", "ZERO", [[0, 3], [-1, 128]], A.not_equal, 1.0, ap=T.II[:, 128:512], sap=T.ZERO[:, 0:384])
-        diag("IM1", -1.0)
-
-    def consts1():
-        for n, v in (("IM2", -2.0), ("I7", 7.0), ("I32", 1.0), ("IM8", -8.0)):
-            diag(n, v)
-        x32 = [[0, 8], [-1, 32]]
-        sel("SM", "ZERO", x32, A.is_gt, 0.25, 16, 0, sap=T.ZERO[:, 0:256])
-        rows("SM", [0, 1], 0, 15, [[0, 32]])
-        sel("S2", "ZERO", x32, A.is_gt, -0.125, 15, 0, sap=T.ZERO[:, 0:256])
-        sel("S2", "S2", x32, A.is_gt, -0.25, 16, 0)
-        rows("S2", [0, 1], 0, 15, [[0, 32]])
-        sel("S0", "ZERO", [[0, 8], [-1, 16]], A.is_gt, -0.125, 1, 0, sap=Z128)
-        rows("S0", [0, 1], 0, 15, [[0, 16]])
-        sel("E0", "ZERO", GK, A.not_equal, 1.0, sap=Z128)
-        iota("ZK", [[0, 8], [1, 16]])
-        sel("ZK", "ZK", [[-16, 8], [0, 16]], A.is_equal, 0.0, -15)
-        for j in range(1, 15):
-            sel("ZM%d" % j, "ZK", [[-16, 8], [0, 16]], A.not_equal, -15.0, -j, ap=T.ZM[:, j - 1])
-        sel("IMID", "II", [[0, 8], [1, 16]], A.not_equal, 0.0, 0, 0, sap=I)
-        sel("IMID", "IMID", [[0, 8], [1, 16]], A.not_equal, 0.0, -15, 0)
-        sel("IEND", "ZERO", GK, A.not_equal, 3328.0, sap=Z128)
-        sel("IEND", "IEND", GK, A.not_equal, 3328.0, -15 - 256 * 15)
-        iota("KS", [[0, 8], [16, 16]])
-        sel("KS", "KS", [[0, 8], [1, 16]], A.not_equal, 0.0, -15, 0)
-        sel("KS", "KS", [[-16, 8], [0, 16]], A.is_equal, 0.0, -15)
-        sel("KS", "KS", GK, A.not_equal, -1.0)
-        sel("KS", "KS", GK, A.not_equal, -1.0, -256 * 15)
-        iota("X3", [[0, 32]], 1)
-        rows("X3", [2, 4], 0, 1)
-        iota("XP", [[0, 64]], -240)
-        rows("XP", [0, 8], 8, 9)
-        iota("XH", [[-30, 8], [0, 8]], -15)
-        rows("XH", [0, 8], 10, 11)
-
-    consts0()
-    consts1()
-    fill(T.WE[:, 1920:2048 + W], ["WEe"])
-    fill(T.ZB[:], ["ZB%d" % i for i in range(5)])
-    cp(lst(LA_), T.PI[:, 128:256], ["PIa"], ["LA"])
-    ts(T.EF[:, 0:160], T.EI[:], 1.0 / 32, A.mult, ["EI"], ["EF0"])
-    cp(lst(LB_), T.PI[:, 0:128], ["PIb"], ["LB"])
-    ts(T.EF[:, 160:320], T.EF[:, 0:160], MAG32, A.add, ["EF0"], ["EF1"], -MAG32, A.add)
-    cp(lst(LL_), T.PI[:, 256:384], ["PIl"], ["Ll"])
-    tt(T.EF[:, 320:480], T.EF[:, 0:160], T.EF[:, 160:320], A.subtract, ["EF0", "EF1"], ["EF2"])
-    dma("s", T.WE[6:128:16, 2048:2048 + W], T.EF[:, 160:320], ["EF1", "WEe"], ["WEr0"], ("dw", 32), 2300.0)
-    dma("s", T.WE[7:128:16, 2048:2048 + W], T.EF[:, 320:480], ["EF2", "WEe"], ["WEr1"], ("dw", 32), 2300.0)
-    dma("s", T.NB[:], T.nbr[:], ["WEr0", "WEr1"], ["NB"], ("dn", 16), 7200.0)
-    ts(T.H16[:, 0:256], T.PI[:, 0:256], -1280.0, A.add, ["PIa", "PIb"], ["H16a"])
-    cp(T.H16[:, 256:384], T.PI[:, 256:384], ["PIl"], ["H16l"])
-    ast = ["AS%d" % i for i in (0, 2, 3, 4, 6, 7, 8, 9, 10, 11)]
-    fill(T.AS[:], ast)
-    mm([(ps(7, 128 * i, 128 * i + 128), T.H16[:, 128 * i:128 * i + 128], I, True, True) for i in range(3)], ["H16a", "H16l", "II"], ["B7"])
-
-    def state_l(bank, c0):
-        act(T.LL[:, 1], ps(bank, c0, c0 + 128), ["B%d" % bank], ["LL1"])
-        act(T.LL[:, 0], ps(bank, c0, c0 + 128), ["B%d" % bank], ["LL0"], F.Identity, scale=-1.0, bias=8.0)
-        act(T.LL[:, 2], ps(bank, c0, c0 + 128), ["B%d" % bank], ["LL2"], F.Identity, scale=-1.0, bias=8.0)
-
-    def xa(c):
-        act(ch(T.XA, c), gat(XW, LA_, c, c + 1), ["X", "LA"], ["XA%d" % c])
-
-    def dd(c):
-        tt(ch(T.D, c), gat(XW, LB_, c, c + 1), ch(T.XA, c), A.subtract, ["X", "LB", "XA%d" % c], ["D%d" % c])
-        mm([(ps(c), I, ch(T.D, c), True, True)], ["D%d" % c, "II"], ["B%d" % c])
-
-    def rr(r, c):
-        b = 4 + c % 2
-        grp(ps(b), [(T.I8[:], ch(T.XA, c)), (I, ch(T.LD, c))], ["I8", "II", "XA%d" % c, "LD%d" % c], ["B%d" % b])
-        act(ch(T["RW%d" % r], c, H), ps(b), ["B%d" % b], ["R%d" % c])
-        act(ch(T.XN2, c), ps(b), ["B%d" % b], ["RS%d" % c])
-
-    def energy():
-        tt(T.EM[:], T.SE[:], T.LL[:, 1:3], A.mult, ["SE", "LL1", "LL2"], ["EM"])
-        tt(T.EE[:], T.EM[:, 0], T.EM[:, 1], A.add, ["EM"], ["EE"])
-
-    def send(r):
-        sn, rw = T["SN%d" % r], T["RW%d" % r]
-        if r == 0:
-            cp(sn[:, 128:H], T.EE[:, :, 0], ["EE"], ["SN%d0" % r])
-            cp(sn[:, H + 128:2 * H], T.EE[:, :, 15], ["EE"], ["SN%d1" % r])
-        else:
-            tt(T.Q4[:], T.SE[:, :, :, END], T.LE[:], A.mult, ["SE", "LE0", "LE1"], ["Q4"])
-            tt(sn[:, 128:H], T.Q4[:, 0, :, 0], T.Q4[:, 1, :, 0], A.add, ["Q4"], ["SN%d0" % r])
-            tt(sn[:, H + 128:2 * H], T.Q4[:, 0, :, 1], T.Q4[:, 1, :, 1], A.add, ["Q4"], ["SN%d1" % r])
+    def send(h, tok):
+        rw0 = RWN * h
         e0, e1 = topo.engines(core, prv), topo.engines(core, nxt)
         m0 = sum(1 << e for e in e0[0:4])
-        m1 = sum(1 << e for e in [x for x in e1 if not m0 >> x & 1][0:4])
+        m1 = sum(1 << e for e in [y for y in e1 if not m0 >> y & 1][0:4])
         a0, a1 = topo.addr(prv), topo.addr(nxt)
-        trs = [RemoteDMATransfer(dst_ids=[DstId(rid=a0[0], pnc=a0[1])], dma_engine_mask=m0, remote_sem=T.sem["h%d" % r],
-                                 src=sn[:, 0:H], dst=rw[:, H + 2048:2 * H + 2048]),
-               RemoteDMATransfer(dst_ids=[DstId(rid=a1[0], pnc=a1[1])], dma_engine_mask=m1, remote_sem=T.sem["h%d" % r],
-                                 src=sn[:, H:2 * H], dst=rw[:, 0:H])]
-        op("gq", lambda: g.remote_dma_fused(trs, local_sem=T.sem.snt), ["SN%d%d" % (r, i) for i in range(4)], ["HALO%d" % r],
-           ("snt", 8 * (r + 1)), 300.0, 3000.0)
+        trs = [RemoteDMATransfer(dst_ids=[DstId(rid=a0[0], pnc=a0[1])], dma_engine_mask=m0, remote_sem=T.sem["h%d" % h],
+                                 src=T.SN[:, h, 1:3], dst=T.RW[:, rw0:rw0 + 128]),
+               RemoteDMATransfer(dst_ids=[DstId(rid=a1[0], pnc=a1[1])], dma_engine_mask=m1, remote_sem=T.sem["h%d" % h],
+                                 src=T.SN[:, h, 0:2], dst=T.RW[:, rw0 + 1152:rw0 + 1280])]
+        op("gq", lambda: g.remote_dma_fused(trs, local_sem=T.sem.snt), ["SN0%d" % h, "SN1%d" % h, tok], ["HALO%d" % h], ("snt", 48), 300.0, OPT["rem"])
 
-    def ends_r(r, src, o, tok):
-        sn = T["SN%d" % r]
-        act(sn[:, 0:128], src[:, o:o + 2048:16], tok, ["SN%d2" % r])
-        act(sn[:, H:H + 128], src[:, o + 15:o + 2048:16], tok, ["SN%d3" % r])
+    def stream(r, s):
+        first, last = r == 0, r == 2
+        sb, wb, mb = s, (2 + 2 * s, 3 + 2 * s), 6 + s
+        x = str(s)
+        o, po = 1024 * s, PAD * s
 
-    def zprod():
-        ts(T.MM[:, 0:3:2], T.LL[:, 1:3], 8.0, A.is_equal, ["LL1", "LL2"], ["MM0"])
-        ts(T.MM[:, 1], T.LL[:, 1], 8.0, A.not_equal, ["LL1"], ["MM1"])
-        tt(T.ZP[:], T.MM[:, 0:2], SAB, A.mult, ["MM0", "MM1", "SAB"], ["ZP"])
-        grp(ps(6, 128, 256), [(T.ZP[:, 0], I), (T.ZP[:, 1], I)], ["ZP", "II"], ["B6"])
+        def opt(n):
+            return "av" if 2 * r + s >= OPT["tail"] else OPT[n]
 
-    def nblist(r):
-        rw = T["RW%d" % r]
-        tt(T.ZB[:, 0, :, 1:15], T.EE[:, :, 2:16], T.EE[:, :, 0:14], A.is_ge, ["EE"], ["ZB0"])
-        tt(T.ZB[:, 1, :, 0], T.EE[:, :, 1], rw[:, 128:H], A.is_ge, ["EE", "HALO%d" % r], ["ZB1"])
-        tt(T.ZB[:, 2, :, 15], rw[:, H + 2048 + 128:2 * H + 2048], T.EE[:, :, 14], A.is_ge, ["EE", "HALO%d" % r], ["ZB2"])
-        grp(ps(7, 128, 256), [(T.DMUL[:], T.PP[:]), (T.DADD[:], T.ONE[:]), (T.ZB[:, 0], T.I2[:]), (T.ZB[:, 1], T.DA[:]), (T.ZB[:, 1], T.DB[:]),
-                              (T.ZB[:, 2], T.DC[:]), (T.ZB[:, 2], T.DD[:])],
-            ["DMUL", "PP", "DADD", "ONE", "ZB0", "ZB1", "ZB2", "I2", "DA", "DB", "DC", "DD"], ["B7"])
+        def st(i, n=1):
+            return ps(sb, 64 * i, 64 * (i + n))
 
-    def prod(dst, tok, src, stok, c0=0, c1=4, o=0):
-        tt(dst[:, 512 * c0:512 * c1], T.ps[:, 512 * c0:512 * c1], src[:, o + 512 * c0:o + 512 * c1], A.mult,
-           ["B%d" % c for c in range(c0, c1)] + [stok + str(c) for c in range(c0, c1)], [tok + str(c) for c in range(c0, c1)])
+        def mi(i, n=1):
+            return ps(mb, 64 * i, 64 * (i + n))
 
-    def tan(r, c):
-        rw = T["RW%d" % r]
-        tt(ch(T.TT, c), gat(rw[:, 0:2048 + 2 * H], LN_, c, c + 1), ch(T.XN2, c), A.subtract, allc("R") + ["HALO%d" % r, "LN", "RS%d" % c], ["T%d" % c])
+        def sk(i):
+            return "b%d.%d" % (sb, i)
 
-    def gather(q, dst, tok, win, wtok, l, ltok, c0=0, c1=4, bias=None):
-        o, w_ = dst[:, 512 * c0:512 * c1], [tok + str(c) for c in range(c0, c1)]
-        if q == "a" and bias is None:
-            act(o, gat(win, l, c0, c1), list(wtok) + [ltok], w_)
-        elif q == "a":
-            act(o, gat(win, l, c0, c1), list(wtok) + [ltok], w_, F.Identity, bias=bias)
-        elif bias is None:
-            cp(o, gat(win, l, c0, c1), list(wtok) + [ltok], w_)
+        def mk(i):
+            return "b%d.%d" % (mb, i)
+
+        def wk(e):
+            return "b%d.w" % wb[e]
+
+        def nf(n, k=1):
+            c = 64 * (len(NF) * s + NF.index(n))
+            return T.NFB[:, c:c + 64 * k]
+
+        def nh(n, k=1):
+            c = 64 * (len(NH) * s + NH.index(n))
+            return T.NHB[:, c:c + 64 * k]
+
+        def lst(n, c0=0, c1=64):
+            c = 64 * (len(LISTS) * s + LISTS.index(n))
+            return T.LST[:, c + c0:c + c1]
+
+        def pad(n, k=1):
+            i = len(PADS) * s + PADS.index(n)
+            return T.PB[:, i:i + k, 1:16:2]
+
+        def turn(n, rhs):
+            i = len(PADS) * s + PADS.index(n)
+            return [(T.PB[:, i, 1:17], rhs[:, :, 0:16:2]), (T.PB[:, i, 0:16], rhs[:, :, 1:16:2])]
+
+        def half(t, c, base=o):
+            return t[:, base + 512 * c:base + 512 * c + 512]
+
+        def par(t, e, base=o, sh=0):
+            return t[:, base + e + sh:base + 1024 + sh:2]
+
+        def both(n):
+            return [n + x + "0", n + x + "1"]
+
+        def gather(q, dst, base, tok, win, wtok, ln, bias=None):
+            if len(q) == 1:
+                return move(q, dst[:, base:base + 1024], win.indirect(lst(ln)), wtok + [ln + x], both(tok), bias)
+            for c in range(2):
+                move(q[c], half(dst, c, base), win.indirect(lst(ln, 32 * c, 32 * c + 32)), wtok + [ln + x], [tok + x + str(c)], bias)
+
+        def gsub(dst, tok, win, wtok, ln, src, base, stok):
+            if OPT[tok] == 1:
+                return tt(dst[:, o:o + 1024], win.indirect(lst(ln)), src[:, base:base + 1024], A.subtract, [wtok, ln + x] + both(stok), both(tok))
+            for c in range(2):
+                tt(half(dst, c), win.indirect(lst(ln, 32 * c, 32 * c + 32)), half(src, c, base), A.subtract, [wtok, ln + x, stok + x + str(c)], [tok + x + str(c)])
+
+        def spread(src, tok):
+            for e in range(2):
+                mm([(ps(wb[e], kk, 512, 8), T.BK[:, 2 * kk + e], src, True, True) for kk in range(8)], BKt + [tok], [wk(e)])
+
+        def ends(i, q):
+            return [(T.EK[:, i, 15 - 15 * e:143 - 15 * e], T.EG[:, 256 * s + 2 * q + e:256 * s + 256:4]) for e in range(2)]
+
+        def energies(ea, de, r_):
+            grp(st(SEA), turn("eh", I) + turn("el", I) + ea, ["II", "e" + x] + r_, [sk(SEA)])
+            grp(st(SDE), turn("dh", mc("P8")) + turn("dl", mc("P8")) + de, ["P8", "e" + x] + r_, [sk(SDE)])
+        SA, SB, SBA, SEA, SDE, SL, SN_, SLR = range(8)
+        h = 2 * r + s
+        rw0, we0 = RWN * h, WEN * s
+        RE, RO = T.RW[:, rw0 + 128:rw0 + 640], T.RW[:, rw0 + 640:rw0 + 1152]
+        EE = T.SN[:, h, 1] if first else nf("EE")
+        hx = str(h)
+        M1 = mc("IM1")
+
+        if first:
+            for n, i in (("LA", 0), ("LB", 1)):
+                move("v", lst(n), T.PI[:, 128 * i + 64 * s:128 * i + 64 * s + 64], ["PI" + "ab"[i]], [n + x])
+                ts(nh("AB"[i] + "16"), T.PI[:, 128 * i + 64 * s:128 * i + 64 * s + 64], -1280.0, A.add, ["PI" + "ab"[i]], ["AB"[i] + "16" + x])
+            move("v", nh("LL"), T.PI[:, 256 + 64 * s:320 + 64 * s], ["PIl"], ["LL" + x])
+            mm([(st(SA, 2), I, nh("A16", 2), True, True), (st(SL), I, nh("LL"), True, True)], ["II", "A16" + x, "B16" + x, "LL" + x], [sk(SA), sk(SB), sk(SL)])
+            grp(st(SBA), [(mc("P8"), nh("B16")), (mc("M8"), nh("A16"))], ["P8", "M8", "A16" + x, "B16" + x], [sk(SBA)])
+            gather(OPT["e" + x][0], T.AD, o, "AD", T.ET[:, 0:W], ETt, "LA")
+            gather(OPT["e" + x][1], T.WG, o, "WG", T.ET[:, 0:W], ETt, "LB")
+            it = []
+            for y in range(8):
+                it += [(ps(mb, y, 256, 8), T.AD[:, o + y:o + 1024:8], T.E0[:, 0:4], True, False), (ps(mb, 128 + y, 256, 8), T.WG[:, o + y:o + 1024:8], T.E0[:, 4:6], False, True)]
+            mm(it, ["E0"] + both("AD") + both("WG"), [mk(i) for i in range(4)])
+            act(pad("eh", k=4), mi(0, 4), [mk(i) for i in range(4)] + ["PB"], ["e" + x])
+            energies([], [], [])
+        gather(OPT["xa"], T.XA, po, "XA", T.X[:, 0:W], ["X"], "LA")
+        gsub(T.D, "D", T.X[:, 0:W], "X", "LB", T.XA, po, "XA")
+        gather(OPT["ga"], T.GA, o, "GA", T.G[:, 0:W], ["G"], "LA")
+        gsub(T.DG, "DG", T.G[:, 0:W], "G", "LB", T.GA, o, "GA")
+        spread(nh("LL"), "LL" + x)
+        for e in range(2):
+            if h:
+                tt(half(T.LG, e), ps(wb[e]), par(T.DG, e), A.mult, [wk(e)] + both("DG"), ["LG" + x + str(e)])
+            if OPT["radd"][e] == "v":
+                tt(ps(wb[e]), ps(wb[e]), par(T.D, e), A.mult, [wk(e)] + both("D"), [wk(e)])
+                tt((RE, RO)[e], ps(wb[e]), par(T.XA, e, po), A.add, [wk(e)] + both("XA"), ["R" + x + str(e)])
+            else:
+                tt(half(T.TT, e), ps(wb[e]), par(T.D, e), A.mult, [wk(e)] + both("D"), ["T" + x + str(e)])
+                grp(ps(wb[e]), [(I, par(T.XA, e, po)), (I, half(T.TT, e))], ["II", "T" + x + str(e)] + both("XA"), [wk(e)])
+                act((RE, RO)[e], ps(wb[e]), [wk(e)], ["R" + x + str(e)])
+        if not h:
+            spread(nh("LL"), "LL" + x)
+            for e in range(2):
+                tt(half(T.LG, e), ps(wb[e]), par(T.DG, e), A.mult, [wk(e)] + both("DG"), ["LG" + x + str(e)])
+        tt(nf("EM"), st(SDE), nh("LL"), A.mult, [sk(SDE), "LL" + x], ["EM" + x])
+        ee = "E%d" % first + x
+        tt(EE, st(SEA), nf("EM"), A.add, [sk(SEA), "EM" + x], [ee])
+        if first:
+            act(T.SN[:, h, 0], RO[:, 7:512:8], ["R" + x + "1"], ["SN0" + hx])
+            act(T.SN[:, h, 2], RE[:, 0:512:8], ["R" + x + "0"], ["SN1" + hx])
+            send(h, ee)
+        act(nh("M8L"), st(SL), [sk(SL)], ["M8L" + x], F.Relu, scale=8.0, bias=-56.0)
+        tt(nf("ZP"), st(SBA), nh("M8L"), A.mult, [sk(SBA), "M8L" + x], ["ZP" + x])
+        grp(mi(6), [(I, nh("A16")), (mf("I32"), nf("ZP"))], ["II", "I32", "A16" + x, "ZP" + x], [mk(6)])
+        move("a", lst("LZ"), mi(6), [mk(6)], ["LZ" + x], 1280.0)
+        gather(OPT["ng"], T.NG, o, "NG", T.NB[:, 0:W], ["NB"], "LZ", -1280.0)
+        mm([(ps(mb, 384 + y, 512, 8), T.NG[:, o + y:o + 1024:8], T.IT[:, y:16:8], True, True) for y in range(8)], ["IT"] + both("NG"), [mk(6), mk(7)])
+        act(pad("n0", 2), mi(6, 2), [mk(6), mk(7), "PB"], ["n" + x], F.Identity, scale=8.0)
+        grp(st(SN_), turn("n0", I)[0:1] + turn("n1", I)[1:2], ["II", "n" + x], [sk(SN_)])
+        grp(mi(4), [(mf("SH"), EE), (mf("H16"), T.RW[:, rw0:rw0 + 64]), (mf("HM1"), T.RW[:, rw0 + 1216:rw0 + 1280])], ["SH", "H16", "HM1", ee, "HALO" + hx], [mk(4)])
+        ts(mi(4), mi(4), 0.0, A.is_ge, [mk(4)], [mk(4)])
+        tt(nh("FD"), mi(4), T.DL[:, 0:64], A.mult, [mk(4), "DL"], ["FD" + x])
+        it = [(mi(5), I, T.DL[:, 64:128], True, False)]
+        for e in range(2):
+            for pp in range(2):
+                it.append((ps(mb, 320 + 32 * e, 352 + 32 * e), T.PM[:, e, 1 - pp:17 - pp], nh("FD")[:, pp:64:2], False, e + pp == 2))
+        mm(it, ["II", "DL", "PM0", "PM1", "FD" + x], [mk(5)])
+        move("a", lst("LN"), mi(5), [mk(5)], ["LN" + x])
+        wins = (T.RW[:, rw0 + 640:rw0 + 1216], T.RW[:, rw0 + 64:rw0 + 640])
+        for e in range(2):
+            tt(half(T.TT, e), wins[e].indirect(lst("LN", 32 * e, 32 * e + 32)), (RE, RO)[e], A.subtract, both("R") + ["HALO" + hx, "LN" + x], ["T" + x + str(e)])
+            act(par(T.PR2, e), half(T.TT, e), ["T" + x + str(e)], ["P2" + x + str(e)], F.Square)
+            grp(ps(wb[e]), [(I, par(T.GA, e)), (I, half(T.LG, e))], ["II", "LG" + x + str(e)] + both("GA"), [wk(e)])
+            tt(par(T.PR0, e), ps(wb[e]), par(T.D, e), A.mult, [wk(e)] + both("D"), ["P0" + x + str(e)])
+            tt(par(T.PR3, e), ps(wb[e]), half(T.TT, e), A.mult, [wk(e), "T" + x + str(e)], ["P3" + x + str(e)])
+            mm([(ps(wb[e]), I, par(T.D, e), True, True)], ["II"] + both("D"), [wk(e)])
+            tt(par(T.PR1, e), ps(wb[e]), half(T.TT, e), A.mult, [wk(e), "T" + x + str(e)], ["P1" + x + str(e)])
+        for i, j in enumerate((0, 3, 2, 1)):
+            for e in range(2):
+                mm([(ps(mb, 64 * i + y, 64 * i + 64, 8), T["PR%d" % j][:, o + y:o + 1024:8], T.BO[:], True, True) for y in range(e, 8, 2)],
+                   ["BO", "P%d" % j + x + str(e), mk(i)], [mk(i) + str(e)])
+        act(nf("GM0", 2), mi(0, 2), [mk(i) + y for i in (0, 1) for y in ("0", "1", "")], ["GM" + x])
+        tt(mi(2), mi(2), nf("GM0"), A.mult, [mk(2) + "0", mk(2) + "1", "GM" + x], [mk(2)])
+        tt(nf("BV"), mi(3), nf("GM1"), A.mult, [mk(3) + "0", mk(3) + "1", mk(3), "GM" + x], ["BV" + x])
+        if OPT["sg"] == "a":
+            tt(mi(2), mi(2), nf("BV"), A.subtract, [mk(2), "BV" + x], [mk(2)])
+            act(pad("c0"), mi(2), [mk(2), "PB"], ["c0" + x], F.Sign)
+            grp(st(SLR), [(I, nh("LL"))] + turn("c0", M1), ["II", "IM1", "LL" + x, "c0" + x], [sk(SLR)])
         else:
-            ts(o, gat(win, l, c0, c1), bias, A.add, list(wtok) + [ltok], w_)
+            tt(pad("c0"), mi(2), nf("BV"), A.is_lt, [mk(2), "BV" + x, "PB"], ["c0" + x])
+            tt(pad("c1"), mi(2), nf("BV"), A.is_gt, [mk(2), "BV" + x, "PB"], ["c1" + x])
+            grp(st(SLR), [(I, nh("LL"))] + turn("c0", I) + turn("c1", M1), ["II", "IM1", "LL" + x, "c0" + x, "c1" + x], [sk(SLR)])
+        if OPT["ud"]:
+            grp(mi(0), [(I, nh("LL")), (mc("N8"), T.ONE[:, 0:64])] + turn("c0", M1), ["II", "IM1", "N8", "ONE", "LL" + x, "c0" + x], [mk(0)])
+            grp(mi(1), [(M1, nh("LL"))] + turn("c0", I), ["II", "IM1", "LL" + x, "c0" + x], [mk(1)])
+            act(nh("UP", 2), mi(0, 2), [mk(0), mk(1)], ["UP" + x, "DN" + x], F.Relu)
+            lr = [(I, nh("LL"))] + turn("c0", M1)
+            grp(mi(2), lr + [(mc("N8"), nh("UP")), (mc("I8"), nh("DN"))], ["II", "IM1", "N8", "I8", "LL" + x, "c0" + x, "UP" + x, "DN" + x], [mk(2)])
+            grp(mi(3), lr + [(mc("N2"), nh("UP")), (I, nh("DN"))], ["II", "IM1", "N2", "LL" + x, "c0" + x, "UP" + x, "DN" + x], [mk(3)])
+            move("a", nh("LP", 2), mi(2, 2), [mk(2), mk(3)], ["LP" + x, "L2L" + x])
+        else:
+            act(nh("UP"), st(SLR), [sk(SLR)], ["UP" + x], F.Relu, bias=-8.0)
+            act(nh("DN"), st(SLR), [sk(SLR)], ["DN" + x], F.Relu, scale=-1.0)
+            act(nh("W8"), st(SLR), [sk(SLR)], ["W8" + x], F.Abs, scale=-1.0, bias=8.0)
+            act(nh("L2L"), nh("W8"), ["W8" + x], ["L2L" + x], F.Relu, scale=-1.0, bias=8.0)
+            grp(mi(2), [(I, nh("L2L")), (mc("EM6"), nh("UP")), (mc("E7"), nh("DN"))], ["II", "EM6", "E7", "L2L" + x, "UP" + x, "DN" + x], [mk(2)])
+            move("a", nh("LP"), mi(2), [mk(2)], ["LP" + x])
+        for n, m, i in (("UN", "UP", SN_), ("DNN", "DN", SN_), ("UA", "UP", SA), ("DA", "DN", SA), ("UB", "UP", SB), ("DB", "DN", SB)):
+            tt(nh(n), st(i), nh(m), A.mult, [sk(i), m + x], [n + x])
+        for i, terms in ((4, ("A16", "UN", "DNN", "-UA", "-DA")), (5, ("A16", "-UA", "-DA", "UB", "DNN")), (6, ("B16", "-UB", "-DB", "UN", "DA"))):
+            grp(mi(i), [(M1, nh(t[1:])) if t[0] == "-" else (I, nh(t)) for t in terms], ["II", "IM1"] + [t.strip("-") + x for t in terms], [mk(i)])
+        move("a", lst("LU"), mi(4), [mk(4)], ["LU" + x], 1280.0)
+        move("a", nh("AE", 2), mi(5, 2), [mk(5), mk(6)], ["AE" + x])
+        gather(opt("xu"), T.XU, po, "XU", T.X[:, 0:W], ["X"], "LU")
+        spread(nh("L2L"), "L2L" + x)
+        L2 = (T.L2[:, po:po + 512], T.L2[:, po + 528:po + 1040])
+        for e in range(2):
+            tt(L2[e], ps(wb[e]), par(T.D, e), A.mult, [wk(e)] + both("D"), ["L2" + x + str(e)])
+        for e in range(2):
+            grp(ps(wb[e]), [(mc("I7"), par(T.XA, 1 - e, po, 2 * e)), (mc("IM7"), par(T.XA, e, po))], both("XA") + ["I7", "IM7", "XAp"], [wk(e)], stop=False)
+            grp(ps(wb[e]), [(I, (L2[1], T.L2[:, po + 1:po + 513])[e]), (M1, L2[e])], both("L2") + ["II", "IM1", "L2p"], [wk(e)], start=False, stop=False)
+            grp(ps(wb[e]), [(mc("P8"), par(T.XU, 1 - e, po, 2 * e)), (mc("M8"), par(T.XU, e, po))], both("XU") + ["P8", "M8", "XUp"], [wk(e)], start=False)
+            act(half(T.AD, e), ps(wb[e]), [wk(e)], ["AD" + x + str(e)], F.Abs)
+        ts(nh("S8"), st(SLR), 4.0, A.is_gt, [sk(SLR)], ["S8" + x], 8.0, A.mult)
+        tt(nf("CP"), st(SBA), nh("S8"), A.mult, [sk(SBA), "S8" + x], ["CP" + x])
+        tt(nf("SC"), st(SA), nf("CP"), A.add, [sk(SA), "CP" + x], ["SC" + x])
+        nd = 96 if last else 160
 
-    def nextract():
-        it = [(ps(7), Z128, T.ZERO[:], True, False)] + [(ps(7, 128 * i, 128 * i + 128), T.IM1[:], T.S4[:, 2], False, False) for i in range(2)]
-        mm(it, ["ZERO", "IM1", "SAB"], ["B7"])
-        mm([(ps(7, k, 512, 16), T.NG[:, k:2048:16], T.II[:, k:512:16], False, k == 15) for k in range(16)], allc("NG") + ["II", "II4"], ["B7"])
-
-    def nstate():
-        act(T.S4[:, 0:4:3], ps(7, 256, 512), ["B7"], ["NS"])
-
-    def umask():
-        tt(ps(7, 0, 256), ps(7, 0, 256), T.MM[:, 0:3:2], A.mult, ["B7", "MM0"], ["B7"])
-
-    m8 = [T.C2[:, 8 * m:8 * m + 8, :] for m in range(8)]
-
-    def l_sums():
-        grp(ps(3, 0, 128), [(T.ZB[:, 3], I)] + [(x, I) for x in m8], ["C20", "C21", "ZB3", "II"], ["B3"])
-
-    def l_sums2():
-        grp(ps(6, 0, 128), [(I, T.ZB[:, 3])] + [(I, x) for x in m8], ["C20", "C21", "ZB3", "II"], ["B6"])
+        def rowdma(n, here, before):
+            for row, c in ((here, 64), (before, 0)):
+                dma("s", T.WE[row:128:16, we0 + c:we0 + c + 1024], nf(n), [n + x, "WE" + x], ["WR%d" % row + x], ("w" + hx, nd), OPT["dma"])
+        rowdma("SC", 0, 1)
+        if not last:
+            tt(nf("EP"), st(SDE), nh("S8"), A.mult, [sk(SDE), "S8" + x], ["EP" + x])
+            tt(nf("EC"), st(SEA), nf("EP"), A.add, [sk(SEA), "EP" + x], ["EC" + x])
+            ts(nf("SEH"), nf("EC"), MAG, A.add, ["EC" + x], ["SEH" + x], -MAG, A.add)
+            tt(nf("SEL"), nf("EC"), nf("SEH"), A.subtract, ["EC" + x, "SEH" + x], ["SEL" + x])
+            rowdma("SEH", 2, 4)
+            rowdma("SEL", 3, 5)
+            h1 = str(h + 2)
+            for i, k in ((0, 15), (1, 0)):
+                grp(mi(i), [(mc("I7"), T.XA[:, po + k:po + 1024:16]), (I, L2[k % 2][:, k // 2:512:8]), (mc("P8"), T.XU[:, po + k:po + 1024:16])],
+                    both("XA") + both("XU") + both("L2") + ["II", "I7", "P8"], [mk(i)])
+            act(T.SN[:, h + 2, 0:3:2], mi(0, 2), [mk(0), mk(1)], ["SN0" + h1, "SN1" + h1])
+            grp(ps(mb, 192, 208), [(T.CK[:, j % 2, 15 - j:143 - j], nh("AE", 2)[:, 64 * (j // 2 % 2) + j // 4:64 * (j // 2 % 2) + 64:4]) for j in range(16)],
+                ["CK0", "CK1", "AE" + x], [mk(3)])
+            move("a", lst("LE", 0, 16), ps(mb, 192, 208), [mk(3)], ["LE" + x], 1280.0)
+            move("a", T.EG[:, 256 * s:256 * s + 256], T.ET[:, 0:W].indirect(lst("LE", 0, 16)), ETt + ["LE" + x], ["EG" + x])
+            grp(mi(5), ends(0, 0), ["EK0", "EG" + x], [mk(5)])
+            grp(mi(6), ends(1, 0) + ends(2, 1), ["EK1", "EK2", "EG" + x], [mk(6)])
+            tt(nf("ME"), mi(6), nh("LP"), A.mult, [mk(6), "LP" + x], ["ME" + x])
+            tt(T.SN[:, h + 2, 1], mi(5), nf("ME"), A.add, [mk(5), "ME" + x], ["SN2" + h1])
+            send(h + 2, "SN2" + h1)
+        grp(mi(7), [(T.SM[:, k], T.AD[:, o + 512 * (k % 2) + k // 2:o + 512 * (k % 2) + 512:8]) for k in range(15)],
+            ["SM%d" % k for k in range(15)] + both("AD"), [mk(7)])
+        ph = [T.PH[:, 2 * s + i, 1:129:2] for i in range(2)]
+        ts(nf("SPH"), mi(7), MAG, A.add, [mk(7)], ["SPH" + x], -MAG, A.add)
+        tt(nf("SPL"), mi(7), nf("SPH"), A.subtract, [mk(7), "SPH" + x], ["SPL" + x])
+        move("a", T.PH[:, 2 * s:2 * s + 2, 1:129:2], nf("SPH", 2), ["SPH" + x, "SPL" + x, "PH"], ["PH0" + x, "PH1" + x])
+        rowdma("SPH", 6, 7)
+        rowdma("SPL", 8, 9)
+        for e in range(2):
+            it = []
+            for j in range(7):
+                it += [(ps(wb[e], 64 * j, 64 * j + 64), T.ZM[:, 7 * e + j], ph[i], i == 0, i == 1) for i in range(2)]
+            mm(it, ["PH0" + x, "PH1" + x] + ["ZM%d" % (7 * e + j + 1) for j in range(7)], [wk(e)])
+            cz = T.CZ[:, 896 * s + 448 * e:896 * s + 448 * e + 448]
+            if opt("cz")[e] == "a":
+                act(cz, ps(wb[e], 0, 448), [wk(e)], ["CZ" + x + str(e)], F.Sign, bias=1 / 1024)
+            else:
+                ts(cz, ps(wb[e], 0, 448), 0.0, A.is_ge, [wk(e)], ["CZ" + x + str(e)], 2.0, A.mult)
+        cd = "CD" if opt("cz") == "aa" else "CD1"
+        grp(mi(7), [(mc("IMID"), T.PP[:]), (mc(cd), T.ONE[:, 0:64])] + [(mc("MID32"), T.CZ[:, 896 * s + 64 * j:896 * s + 64 * j + 64]) for j in range(14)],
+            ["IMID", cd, "MID32", "PP", "ONE"] + both("CZ"), [mk(7)])
+        move("a", lst("LW"), mi(7), [mk(7)], ["LW" + x])
+        gather(opt("wg"), T.WG, o, "WG", T.WE[:, we0 + 64:we0 + WEN], ["WR%d" % i + x for i in range(16) if not (last and 2 <= i < 6)], "LW")
+        xb = wb[0]
+        it = [(ps(xb), Z128, T.ZERO[:], True, False)]
+        it += [(ps(xb, 384, 448), T.PH[:, 2 * s + i, 1 - y:129 - y], T.KS[:, y], False, False) for i in range(2) for y in range(2)]
+        mm(it, ["ZERO", "KS", "PH0" + x, "PH1" + x], [wk(0)])
+        it = [(ps(xb, y, 512, 8), T.WG[:, o + y:o + 1024:8], T.XH[:], False, False) for y in range(8)]
+        it += [(ps(xb, 384 + y, 512, 8), T.WG[:, o + y:o + 1024:8], T.XL[:], False, False) for y in range(8)]
+        it.append((ps(xb, 384, 512), T.ONE[:], T.CR[:], False, True))
+        mm(it, ["XH", "XL", "ONE", "CR"] + both("WG"), [wk(0)])
+        act(pad("a", k=2), ps(xb, 0, 128), [wk(0), "PB"], ["ab" + x])
+        op("v", lambda: V.reciprocal(nf("RC"), ps(xb, 448, 512)), [wk(0)], ["RC" + x], cost=190 + 384 * CYC)
+        for i, n, e in ((SA, "a", "AE"), (SB, "b", "BE")):
+            grp(st(i), turn(n, I) + [(mc("IEND"), nh(e))], ["II", "IEND", "ab" + x, "AE" + x], [sk(i)])
+        tt(nf("XX"), ps(xb, 384, 448), nf("RC"), A.mult, [wk(0), "RC" + x], ["XX" + x])
+        ts(pad("l0"), nf("XX"), MAG, A.add, ["XX" + x, "PB"], ["l0" + x], -MAG, A.add)
+        tt(nf("YY"), ps(xb, 448, 512), pad("l0"), A.mult, [wk(0), "l0" + x], ["YY" + x])
+        tt(pad("cm"), ps(xb, 384, 448), nf("YY"), A.is_lt, [wk(0), "YY" + x, "PB"], ["cm" + x])
+        grp(st(SL), [(mc("IEND"), nh("LP")), (mc("EN8"), T.ONE[:, 0:64])] + turn("l0", I) + turn("cm", M1),
+            ["II", "IM1", "IEND", "EN8", "ONE", "LP" + x, "l0" + x, "cm" + x], [sk(SL)])
+        if last:
+            for i, (n, q, bias) in enumerate((("ya", "a", 1280.0), ("yb", "a", 1280.0), ("yl", "v", None))):
+                yo = T.YO[:, 192 * s + 64 * i:192 * s + 64 * i + 64]
+                move(q, yo, st((SA, SB, SL)[i]), [sk((SA, SB, SL)[i])], [n + x], bias)
+                dma("sa"[i == 1], T[n][:, 64 * s:64 * s + 64], yo, [n + x], [], ("o2", 32) if i == 1 else ("o1", 64), 2300.0)
+            return
+        move("a", lst("LA", 0, 128), st(SA, 2), [sk(SA), sk(SB)], ["LA" + x, "LB" + x], 1280.0)
+        move("a", nh("A16", 2), st(SA, 2), [sk(SA), sk(SB)], ["A16" + x, "B16" + x])
+        move("a", nh("LL"), st(SL), [sk(SL)], ["LL" + x])
+        grp(st(SBA), turn("b", mc("P8")) + turn("a", mc("M8")) + [(mc("EP8"), nh("BE")), (mc("EM8"), nh("AE"))], ["P8", "M8", "EP8", "EM8", "ab" + x, "AE" + x], [sk(SBA)])
+        act(pad("eh", k=4), ps(xb, 128, 384), [wk(0), "PB"], ["e" + x])
+        energies(ends(0, 0), ends(1, 0) + ends(2, 1), ["EK0", "EK1", "EK2", "EG" + x])
 
     for r in range(3):
-        last = r == 2
-        rw = T["RW%d" % r]
-        if r == 0:
-            xa(0)
-            cp(SAB, ps(7, 0, 256), ["B7"], ["SAB"])
-            xa(1), dd(0), xa(2), dd(1), xa(3)
-            state_l(7, 256)
-            dd(2), dd(3)
-            for h in range(2):
-                gather(OPT["ea"][h], T.WG, "WG", ET, WEe, LA_, "LA", 2 * h, 2 * h + 2)
-                gather(OPT["eb"][h], T.RP, "RP", ET, WEe, LB_, "LB", 2 * h, 2 * h + 2)
-            reduce16(T.WG, allc("WG"), 6, 384, lambda k: T.X3E[:, 16:24], ("X3E",))
-            reduce16(T.RP, allc("RP"), 6, 256, lambda k: T.X3E[:, 16:24], ("X3E",))
-            cp(T.SE[:], ps(6, 256, 512), ["B6"], ["SE"])
-        else:
-            xa(0)
-            ts(T.C2[:, :, 0:8], ps(0), 0.0, A.is_ge, ["B0"], ["C20"])
-            xa(1)
-            ts(T.C2[:, :, 8:16], ps(1), 0.0, A.is_ge, ["B1"], ["C21"])
-            act(T.SE[:], ps(2, 256, 512), ["B2"], ["SE"])
-            l_sums()
-            l_sums2()
-            xa(2), xa(3)
-            state_l(6, 0)
-            cp(lst(LL_), ps(3, 0, 128), ["B3"], ["Ll"])
-            ends_r(r, T.RP, 0, allc("RP"))
-            tt(T.SE[:, :, :, END], T.SE[:, :, :, END], T.UD[:, :, :, END], A.mult, ["SE", "UD"], ["SE"])
-            tt(T.SE[:, :, :, END], T.SE[:, :, :, END], T.EP[:], A.add, ["SE", "EP"], ["SE"])
-            dd(0), dd(1), dd(2), dd(3)
-        energy()
-        for c in range(4):
-            gather(OPT["lb"][min(r, 1)][c], T.LW, "W", LW, ["LT"], LL_, "Ll", c, c + 1)
-            prod(T.LD, "LD", T.LW, "W", c, c + 1)
-            rr(r, c)
-        if r == 0:
-            ends_r(r, rw, H, allc("R"))
-        send(r)
-        zprod()
-        act(lst(LZ_), ps(6, 128, 256), ["B6"], ["LZ"], F.Identity, bias=1280.0)
-        nblist(r)
-        cp(lst(LN_), ps(7, 128, 256), ["B7"], ["LN"])
-        for h in range(2):
-            gather(OPT["ng"][min(r, 1)][h], T.NG, "NG", NW, ["NB"], LZ_, "LZ", 2 * h, 2 * h + 2, bias=-1280.0)
-        nextract()
-        nstate()
-        umask()
-        for c in range(4):
-            gather("a", T.GA, "GA", GW, ["G"], LA_, "LA", c, c + 1)
-            gather(OPT["gb"][min(r, 1)][c], T.GB, "GB", GW, ["G"], LB_, "LB", c, c + 1)
-            tan(r, c)
-            if c in OPT["td"]:
-                prod(T.PR0, "P0", T.TT, "T", c, c + 1)
-            b = 4 + c % 2
-            grp(ps(b), [(I, ch(T.GB, c)), (T.IM1[:], ch(T.GA, c))], ["II", "IM1", "GA%d" % c, "GB%d" % c], ["B%d" % b])
-            tt(ch(T.L2, c), ps(b), ch(T.LW, c), A.mult, ["B%d" % b, "W%d" % c], ["L2%d" % c])
-            grp(ps(c), [(T.I8[:], ch(T.GA, c)), (I, ch(T.L2, c))], ["II", "I8", "GA%d" % c, "L2%d" % c], ["B%d" % c])
-        for h in range(2):
-            act(T.PR3[:, 1024 * h:1024 * h + 1024], T.TT[:, 1024 * h:1024 * h + 1024], ["T%d" % (2 * h), "T%d" % (2 * h + 1)],
-                ["P3%d" % (2 * h), "P3%d" % (2 * h + 1)], F.Square)
-        for c in range(4):
-            prod(T.PR1, "P1", T.D, "D", c, c + 1)
-        for c in range(4):
-            prod(T.PR2, "P2", T.TT, "T", c, c + 1)
-            if c not in OPT["td"]:
-                mm([(ps(c), I, ch(T.D, c), True, True)], ["D%d" % c, "II"], ["B%d" % c])
-                prod(T.PR0, "P0", T.TT, "T", c, c + 1)
-        reduce16(T.PR1, allc("P1"), 4, 0)
-        act(T.GM[:, 1], ps(4, 0, 128), ["B4"], ["GM1"])
-        reduce16(T.PR3, allc("P3"), 6, 128)
-        tt(ps(6, 256, 384), ps(6, 128, 256), T.GM[:, 1], A.mult, ["B6", "GM1"], ["B6"])
-        if len(OPT["td"]) == 4:
-            reduce16(T.PR0, allc("P0"), 4, 128)
-            act(T.GM[:, 0], ps(4, 128, 256), ["B4"], ["GM0"])
-            reduce16(T.PR2, allc("P2"), 5, 0)
-        else:
-            reduce16(T.PR2, allc("P2"), 4, 128)
-            act(T.GM[:, 0], ps(4, 128, 256), ["B4"], ["GM0"])
-            reduce16(T.PR0, allc("P0"), 5, 0)
-        tt(T.AB[:], ps(5, 0, 128), T.GM[:, 0], A.mult, ["B5", "GM0"], ["AB"])
-        tt(T.CM[:, 0], T.AB[:], ps(6, 256, 384), A.is_gt, ["AB", "B6"], ["CM0"])
-        tt(T.CM[:, 1], T.AB[:], ps(6, 256, 384), A.is_lt, ["AB", "B6"], ["CM1"])
-        tt(T.UP[:], ps(7, 0, 256), T.CM[:], A.mult, ["B7", "CM0", "CM1"], ["UP"])
-        mm([(ps(4, 0, 128), T.LL[:, 1], I, True, False), (ps(4, 0, 128), T.CM[:, 0], I, False, False), (ps(4, 0, 128), T.CM[:, 1], T.IM1[:], False, False)],
-           ["LL1", "II", "IM1", "CM0", "CM1"], ["B4"])
-        tt(T.UD[:], T.CM[:], T.MM[:, 0:3:2], A.mult, ["CM0", "CM1", "MM0"], ["UD"])
-        grp(ps(5, 0, 128), [(T.S4[:, 2], I), (T.UP[:, 0], T.I32[:]), (T.UP[:, 1], T.I32[:])], ["SAB", "II", "I32", "UP"], ["B5"])
-        mm([(ps(4, 0, 128), T.UD[:, 0], T.IM2[:], False, False), (ps(4, 0, 128), T.UD[:, 1], I, False, True)], ["UD", "IM2", "II"], ["B4"])
-        act(lst(LX_), ps(5, 0, 128), ["B5"], ["LX"], F.Identity, bias=1280.0)
-        cp(lst(LU_), ps(4, 0, 128), ["B4"], ["LU"])
-        lr = [(I, T.LL[:, 1]), (I, T.CM[:, 0]), (T.IM1[:], T.CM[:, 1])]
-        grp(ps(6, 0, 128), lr, ["II", "IM1", "LL1", "CM0", "CM1"], ["B6"])
-        grp(ps(6, 128, 256), lr + [(T.IM8[:], T.UD[:, 0]), (T.I8[:], T.UD[:, 1])], ["II", "IM1", "LL1", "CM0", "CM1", "UD", "I8", "IM8"], ["B6"])
-
-        def rp(c):
-            gather("a", T.XN, "XN", XW, ["X"], LX_, "LX", c, c + 1)
-            tt(ch(T.L2, c), gat(LW, LU_, c, c + 1), ch(T.D, c), A.mult, ["LT", "LU", "D%d" % c], ["L2%d" % c])
-            grp(ps(c), [(T.I7[:], ch(T.XA, c)), (I, ch(T.L2, c)), (I, ch(T.XN, c))], ["II", "I7", "XA%d" % c, "L2%d" % c, "XN%d" % c], ["B%d" % c])
-
-        def rpev(c):
-            act(ch(T.RP, c), ps(c), ["B%d" % c], ["RP%d" % c])
-
-        def mx(c):
-            tt(T.MX[:, 512 * c:512 * c + 511], ps(c, 1, 512), T.RP[:, 512 * c:512 * c + 511], A.max, ["B%d" % c, "RP%d" % c], ["MX%d" % c])
-        rp(0), rp(1), rpev(0), rp(2), rpev(1), rp(3), rpev(2), rpev(3)
-        ts(T.SL[:, 0], ps(6, 0, 128), 4.0, A.is_gt, ["B6"], ["SL0"])
-        ts(T.SL[:, 1], ps(6, 0, 128), 4.0, A.is_le, ["B6"], ["SL1"])
-        mx(0), mx(1)
-        tt(T.AS[:, :, 2, :], T.SL[:, 0], T.S4[:, 1], A.mult, ["SL0", "SAB"], ["AS2"])
-        mx(2), mx(3)
-        mm([(ps(4, 0, 128), T.RP[:, k:2048:16], T.S0[:] if k == 0 else T.S2[:, :, 15 - k:31 - k], k == 0, False) for k in range(16)],
-           allc("RP") + ["S0", "S2"], ["B4"])
-        mm([(ps(4, 0, 128), T.MX[:, k:2048:16], T.SM[:, :, 15 - k:31 - k], False, k == 14) for k in range(15)], allc("MX") + ["SM"], ["B4"])
-        act(T.ZB[:, 3, :, 0], ps(6, 128, 256, 16), ["B6"], ["ZB3"])
-        act(T.ZB[:, 3, :, 15], ps(6, 143, 256, 16), ["B6"], ["ZB3"])
-        tt(T.AS[:, :, 3, :], T.SL[:, 1], T.S4[:, 2], A.mult, ["SL1", "SAB"], ["AS3"])
-        act(T.AS[:, :, 0:2, 0:15], T.AS[:, :, 2:4, 1:16], ["AS2", "AS3"], ["AS0"])
-        if not last:
-            tt(T.EM[:], T.SL[:], T.SE[:], A.mult, ["SL0", "SL1", "SE"], ["EM"])
-            act(T.ZB[:, 4, :, END], T.S4[:, 0, :, END], ["NS"], ["ZB4"])
-            act(T.LE[:, 0], T.ZB[:, 3, :, END], ["ZB3"], ["LE0"])
-            act(T.LE[:, 1], T.ZB[:, 3, :, END], ["ZB3"], ["LE1"], F.Identity, scale=-1.0, bias=8.0)
-        ts(T.PH[:, 0], ps(4, 0, 128), MAG64, A.add, ["B4"], ["PH0"], -MAG64, A.add)
-        tt(T.PH[:, 1], ps(4, 0, 128), T.PH[:, 0], A.subtract, ["B4", "PH0"], ["PH1"])
-        act(T.AS[:, :, 8, :], T.PH[:, 0], ["PH0"], ["AS8"])
-        mm([(ps(5, 0, 128), T.E0[:], T.ONE[:], True, False), (ps(5, 0, 128), T.PH[:, 0], I, False, True), (ps(5, 128, 256), T.PH[:, 1], I, True, True)],
-           ["PH0", "PH1", "II", "E0", "ONE"], ["B5"])
-        act(T.AS[:, :, 9, :], T.PH[:, 1], ["PH1"], ["AS9"])
-        if not last:
-            tt(T.EC[:], T.EM[:, 0], T.EM[:, 1], A.add, ["EM"], ["EC"])
-        cp(T.PL[:], ps(5, 0, 256), ["B5"], ["PL"])
-        js = [list(range(1, 5)), list(range(5, 9)), list(range(9, 12)), list(range(12, 15))]
-
-        def zmm(c):
-            it = []
-            for i, j in enumerate(js[c]):
-                o = ps(6 + c % 2, 128 * i, 128 * i + 128)
-                it += [(o, T.ZM[:, j - 1], T.PL[:, 0:128], True, False), (o, T.ZM[:, j - 1], T.PL[:, 128:256], False, True)]
-            mm(it, ["PL"] + ["ZM%d" % j for j in js[c]], ["B%d" % (6 + c % 2)])
-
-        def zcmp(c):
-            j0, n = js[c][0] - 1, len(js[c])
-            ts(T.CZ[:, 128 * j0:128 * (j0 + n)], ps(6 + c % 2, 0, 128 * n), 0.0, A.is_ge, ["B%d" % (6 + c % 2)], ["CZ%d" % c], 128.0, A.mult)
-
-        def zcnt(c):
-            it = []
-            if c == 0:
-                it += [(ps(4, 0, 128), T.IMID[:], T.PP[:], True, False), (ps(4, 0, 128), T.IEND[:], T.ONE[:], False, False)]
-                if not last:
-                    it.append((ps(4, 0, 128), T.ZB[:, 4], I, False, False))
-            it += [(ps(4, 0, 128), T.IMID[:], T.CZ[:, 128 * (j - 1):128 * j], False, j == 14) for j in js[c]]
-            mm(it, ["CZ%d" % c, "IMID", "IEND", "PP", "ONE", "II", "ZB4"], ["B4"])
-
-        def wmm(c):
-            mm([(T.ps[:, 128 * j:128 * j + 128], T.AS[:, :, :, j], I, True, True) for j in range(4 * c, min(4 * c + 4, 15))], ast + ["II"], ["B%d" % c])
-            n = 512 if c < 3 else 384
-            act(T.WE[:, 512 * c:512 * c + n], ps(c, 0, n), ["B%d" % c], ["WE%d" % c])
-        zmm(0), zmm(1)
-        if not last:
-            ts(T.AS[:, :, 6, :], T.EC[:], MAG32, A.add, ["EC"], ["AS6"], -MAG32, A.add)
-        tt(T.AS[:, :, 10, 0:15], T.PH[:, 0, :, 1:16], T.PH[:, 0, :, 0:15], A.subtract, ["PH0"], ["AS10"])
-        if not last:
-            tt(T.AS[:, :, 7, :], T.EC[:], T.AS[:, :, 6, :], A.subtract, ["EC", "AS6"], ["AS7"])
-            act(T.AS[:, :, 4:6, 0:15], T.AS[:, :, 6:8, 1:16], ["AS6", "AS7"], ["AS4"])
-        tt(T.AS[:, :, 11, 0:15], T.PH[:, 1, :, 1:16], T.PH[:, 1, :, 0:15], A.subtract, ["PH1"], ["AS11"])
-        zcmp(0), wmm(0), zmm(2), wmm(1)
-        zcmp(1), zmm(3), wmm(2), wmm(3), zcnt(0), zcnt(1)
-        zcmp(2), zcnt(2), zcmp(3), zcnt(3)
-        ud = T.UD[:, :, :, END]
-        tt(T.SS[:], T.UD[:, 0, :, END], T.UD[:, 1, :, END], A.add, ["UD"], ["SS"])
-        tt(T.PQ[:, :, 0], ud, T.S4[:, 0:3:2, :, END], A.mult, ["UD", "NS", "SAB"], ["PQ0"])
-        tt(T.PQ[:, :, 1], ud, T.S4[:, 1:4:2, :, END], A.mult, ["UD", "NS", "SAB"], ["PQ1"])
-        tt(T.SQ[:, 0], T.SS[:], T.S4[:, 1, :, END], A.mult, ["SS", "SAB"], ["SQ0"])
-        tt(T.SQ[:, 1], T.SS[:], T.S4[:, 2, :, END], A.mult, ["SS", "SAB"], ["SQ1"])
-        cp(lst(LW_), ps(4, 0, 128), ["B4"], ["LW"])
-        for h in range(2):
-            it = [(ps(h), Z128, T.LD[:, 0:512], True, False)]
-            for m in range(8):
-                it += [(ps(h, 64 * m, 64 * m + 64), T.PL[:, 128 * i:128 * i + 128], T.KS[:, :, 8 * h:8 * h + 8], False, False) for i in range(2)]
-            mm(it, ["ZERO", "LD0", "PL", "KS"], ["B%d" % h])
-        gather("a", T.WG, "WG", EW, WEt, LW_, "LW", 2, 4)
-        gather("v", T.WG, "WG", EW, WEt, LW_, "LW", 0, 2)
-        it = []
-        for k in range(16):
-            l_ = T.WG[:, k:2048:16]
-            if k % 15:
-                it.append((ps(2, k, 512, 16), l_, T.X3[:], True, True))
-            else:
-                e, o = k // 15, ps(2, k, 256, 16)
-                it += [(ps(2, k, 512, 16), l_, T.X3E[:], True, False), (o, I, T.S4[:, 1:3, :, k], False, False), (o, T.IM1[:], T.SQ[:, :, :, e], False, False),
-                       (o, I, T.PQ[:, 0, :, :, e], False, False), (o, I, T.PQ[:, 1, :, :, e], False, True)]
-        mm(it, allc("WG") + ["X3", "X3E", "SAB", "SQ0", "SQ1", "PQ0", "PQ1", "II", "IM1"], ["B2"])
-
-        def diffs(h):
-            it = []
-            ks = [k for k in range(8 * h, 8 * h + 8) if k % 15]
-            for k in ks:
-                o = ps(h, k % 8, 512, 8)
-                it += [(o, T.WG[:, k:2048:16], T.XP[:], False, False), (o, T.WG[:, k:2048:16], T.XH[:], False, k == ks[-1])]
-            mm(it, allc("WG") + ["XP", "XH"], ["B%d" % h])
-        if not last:
-            tt(T.DE[:], T.SE[:, 0, :, END], T.SE[:, 1, :, END], A.subtract, ["SE"], ["DE"])
-            tt(T.Q4[:], ud, T.SE[:, :, :, END], A.mult, ["UD", "SE"], ["Q4"])
-            tt(T.Q5[:, 0], T.UD[:, 1, :, END], T.DE[:], A.mult, ["UD", "DE"], ["Q50"])
-            tt(T.EP[:], T.SE[:, :, :, END], T.Q4[:], A.subtract, ["SE", "Q4"], ["EP"])
-        cp(SAB, ps(2, 0, 256), ["B2"], ["SAB"])
-        diffs(0)
-        mm([(ps(5, 0, 128), T.S4[:, 2], I, True, True)], ["SAB", "II"], ["B5"])
-        mm([(ps(4, 0, 128), T.S4[:, 1], I, True, True)], ["SAB", "II"], ["B4"])
-        diffs(1)
-        if not last:
-            tt(T.Q5[:, 1], T.UD[:, 0, :, END], T.DE[:], A.mult, ["UD", "DE"], ["Q51"])
-            tt(T.EP[:, 0], T.EP[:, 0], T.Q5[:, 0], A.subtract, ["EP", "Q50"], ["EP"])
-            act(lst(LA_), ps(5, 0, 128), ["B5"], ["LA"], F.Identity, bias=1280.0)
-            ts(lst(LB_), ps(4, 0, 128), 1280.0, A.add, ["B4"], ["LB"])
-            tt(T.EP[:, 1], T.EP[:, 1], T.Q5[:, 1], A.add, ["EP", "Q51"], ["EP"])
-    act(T.YO[:, 0:128], ps(5, 0, 128), ["B5"], ["YA"], F.Identity, bias=1280.0)
-    ts(T.C2[:, :, 0:8], ps(0), 0.0, A.is_ge, ["B0"], ["C20"])
-    act(T.YO[:, 128:256], ps(4, 0, 128), ["B4"], ["YB"], F.Identity, bias=1280.0)
-    dma("s", T.ya[:], T.YO[:, 0:128], ["YA"], [], ("o1", 32), 2300.0)
-    ts(T.C2[:, :, 8:16], ps(1), 0.0, A.is_ge, ["B1"], ["C21"])
-    dma("s", T.yb[:], T.YO[:, 128:256], ["YB"], [], ("o1", 32), 2300.0)
-    l_sums()
-    act(T.YO[:, 256:384], ps(3, 0, 128), ["B3"], ["YL"])
-    dma("a", T.yl[:], T.YO[:, 256:384], ["YL"], [], ("o2", 16), 2300.0)
+        for s in range(2):
+            lead[0] = s
+            stream(r, s)
     if "o" not in ORDER:
+        ORDER["ops"] = ops
         ORDER["o"] = arrange(ops)
     for i in ORDER["o"]:
         issue(*ops[i][:5])
     for s in ("v", "a", "p", "gq"):
         g.wait_ge(T.sem[s], cnt[s])
-    for s, n in (("snt", 24), ("o1", 32), ("o2", 16)):
+    for s, n in (("snt", 48), ("o1", 64), ("o2", 32)):
         g.wait_ge(T.sem[s], n)

@@ -38,8 +38,8 @@ SCRATCH = {
 SEMAPHORES = ["v", "a", "p", "gq", "dx", "dg", "dn", "de", "dw", "dz", "dpa", "dpb", "dpl", "snt", "o1", "o2"] + [n + str(i) for n in "hw" for i in range(6)]
 MAG = 12582912.0
 END = slice(0, 16, 15)
-CYC, GAM, PCYC, FIX, WAKE = 0.83, 1.56, 0.417, 50.0, 70.0
-OPT = {"lead": 6000.0, "turns": 600, "seed": 2, "ud": 0, "e1": "aa", "radd": "av", "D": 2, "DG": 2, "cz": "aa", "wg": "aa", "ng": "aa", "e0": "aa", "sg": "a", "tail": 5, "ga": "aa", "xu": "aa", "xa": "aa", "dma": 2500.0, "rem": 3500.0}
+CYC, GAM, PCYC, FIX, WAKE = 0.83, 1.56, 0.417, 50.0, 120.0
+OPT = {"lead": 6000.0, "turns": 700, "seed": 4, "flip": 2, "ph": 0, "even": 0.3, "tilt": 0.0, "ud": 0, "e1": "aa", "radd": "av", "D": 2, "DG": 2, "cz": "aa", "wg": "aa", "ng": "aa", "e0": "aa", "sg": "v", "tail": 5, "ga": "aa", "xu": "aa", "xa": "aa", "dma": 2500.0, "rem": 7000.0}
 ORDER = {}
 
 
@@ -67,35 +67,36 @@ def arrange(ops):
     for i in range(n):
         for j in pred[i]:
             succ[j].append(i)
-    needs = [[o[0]] + sorted(set(t[1] for t in o[2] + o[3] if bank(t))) for o in ops]
+    banks = [sorted(set(t[1] for t in o[2] + o[3] if bank(t))) for o in ops]
+    free = [i for i in range(n) if ops[i][8]]
 
-    def place(before, after, key, back):
+    def place(before, after, key, other, back):
         left = [len(p) for p in before]
-        ready = [i for i in range(n) if not left[i]]
+        ready = sorted((key[i], i) for i in range(n) if not left[i])
         busy, start, end = {}, [0.0] * n, [0.0] * n
         while ready:
-            i = max(ready, key=lambda i: key[i])
-            ready.remove(i)
-            q, c, late = ops[i][0], ops[i][5], ops[i][6]
+            i = ready.pop()[1]
+            q, c, late = (ops[i][8][0], ops[i][8][2], 0.0) if i in other else (ops[i][0], ops[i][5], ops[i][6])
             s = max([end[j] + (0.0 if q == "p" == ops[j][0] else WAKE) for j in before[i]], default=0.0) + (late if back else 0.0)
+            needs = [q] + banks[i]
             moved = True
             while moved:
                 moved = False
-                for k, res in enumerate(needs[i]):
+                for k, res in enumerate(needs):
                     l = busy.setdefault(res, [])
-                    for t0, t1, q2 in l[find(l, s - 2500.0):]:
+                    for t0, t1, q2 in l[max(0, find(l, s) - 2):]:
                         gap = WAKE if k and q2 != q else 0.0
                         if t0 - gap >= s + c:
                             break
                         if t1 + gap > s and (k == 0 or q2 != q):
                             s, moved = t1 + gap, True
-            for res in needs[i]:
+            for res in needs:
                 busy[res].insert(find(busy[res], s), (s, s + c, q))
             start[i], end[i] = s, s + c + (0.0 if back else late)
             for j in after[i]:
                 left[j] -= 1
                 if not left[j]:
-                    ready.append(j)
+                    ready.insert(find(ready, key[j]), (key[j], j))
         return start, end
 
     def find(l, t):
@@ -105,22 +106,27 @@ def arrange(ops):
             lo, hi = (m + 1, hi) if l[m][0] < t else (lo, m)
         return lo
 
-    def settle(key):
-        one = place(pred, succ, key, False)
-        two = place(pred, succ, place(succ, pred, one[1], True)[1], False)
-        return min((max(one[1]), one[0]), (max(two[1]), two[0]))
+    def settle(key, other):
+        one = place(pred, succ, key, other, False)
+        two = place(pred, succ, place(succ, pred, one[1], other, True)[1], other, False)
+        one = min(one, two, key=lambda x: max(x[1]))
+        load = sum(ops[i][8][2] * (1 if ops[i][8][0] == "v" else -1) for i in other)
+        return max(one[1]) + OPT["even"] * abs(load + OPT["tilt"]), one[0], other
     key = [0.0] * n
     for i in range(n - 1, -1, -1):
         key[i] = ops[i][5] + ops[i][6] + WAKE + max([key[j] for j in succ[i]], default=OPT["lead"] * (ops[i][7] == 0))
-    best = settle(key)
+    best = settle(key, set())
     rng = np.random.default_rng(OPT["seed"])
-    for _ in range(OPT["turns"]):
+    for turn in range(OPT["turns"]):
         mid, wide, s, by = rng.uniform(0, best[0]), rng.uniform(2000, 10000), int(rng.integers(2)), rng.normal(0, 2500)
-        new = settle([(by if ops[i][7] == s and abs(t - mid) < wide else 0.0) - t for i, t in enumerate(best[1])])
+        other = best[2]
+        if turn % 2:
+            other, by = other ^ set(int(i) for i in rng.choice(free, OPT["flip"])), 0.0
+        new = settle([(by if ops[i][7] == s and abs(t - mid) < wide else 0.0) - t for i, t in enumerate(best[1])], other)
         if new[0] <= best[0]:
             best = new
     ORDER["t"] = best
-    return sorted(range(n), key=lambda i: (best[1][i], i))
+    return [(i, i in best[2]) for i in sorted(range(n), key=lambda i: (best[1][i], i))]
 
 
 def rank_program(g, core, T, topo):
@@ -137,7 +143,13 @@ def rank_program(g, core, T, topo):
     ops, lead = [], [0.0]
 
     def op(q, fn, r=(), w=(), ev=None, cost=100.0, late=0.0):
-        ops.append((q, fn, list(r), list(w), ev, cost, late, lead[0]))
+        ops.append((q, fn, list(r), list(w), ev, cost, late, lead[0], None))
+
+    def either(one, two):
+        one()
+        two()
+        alt = ops.pop()
+        ops.append(ops.pop()[:8] + ((alt[0], alt[1], alt[5]),))
 
     def issue(q, fn, r, w, ev):
         want = {}
@@ -199,6 +211,9 @@ def rank_program(g, core, T, topo):
         op("a", lambda: S.activation(out, a, func, **kw), r, w, cost=cost(out, r, 1.0) + 15.0)
 
     def move(q, out, a, r, w, bias=None):
+        either(lambda: copy(q, out, a, r, w, bias), lambda: copy("av"[q == "a"], out, a, r, w, bias))
+
+    def copy(q, out, a, r, w, bias):
         if q == "a" and bias is None:
             act(out, a, r, w)
         elif q == "a":
@@ -449,7 +464,7 @@ def rank_program(g, core, T, topo):
             for y in range(8):
                 it += [(ps(mb, y, 256, 8), T.AD[:, o + y:o + 1024:8], T.E0[:, 0:4], True, False), (ps(mb, 128 + y, 256, 8), T.WG[:, o + y:o + 1024:8], T.E0[:, 4:6], False, True)]
             mm(it, ["E0"] + both("AD") + both("WG"), [mk(i) for i in range(4)])
-            act(pad("eh", k=4), mi(0, 4), [mk(i) for i in range(4)] + ["PB"], ["e" + x])
+            move("a", pad("eh", k=4), mi(0, 4), [mk(i) for i in range(4)] + ["PB"], ["e" + x])
             energies([], [], [])
         gather(OPT["xa"], T.XA, po, "XA", T.X[:, 0:W], ["X"], "LA")
         gsub(T.D, "D", T.X[:, 0:W], "X", "LB", T.XA, po, "XA")
@@ -465,7 +480,7 @@ def rank_program(g, core, T, topo):
             else:
                 tt(half(T.TT, e), ps(wb[e]), par(T.D, e), A.mult, [wk(e)] + both("D"), ["T" + x + str(e)])
                 grp(ps(wb[e]), [(I, par(T.XA, e, po)), (I, half(T.TT, e))], ["II", "T" + x + str(e)] + both("XA"), [wk(e)])
-                act((RE, RO)[e], ps(wb[e]), [wk(e)], ["R" + x + str(e)])
+                move("a", (RE, RO)[e], ps(wb[e]), [wk(e)], ["R" + x + str(e)])
         if not h:
             spread(nh("LL"), "LL" + x)
             for e in range(2):
@@ -474,16 +489,18 @@ def rank_program(g, core, T, topo):
         ee = "E%d" % first + x
         tt(EE, st(SEA), nf("EM"), A.add, [sk(SEA), "EM" + x], [ee])
         if first:
-            act(T.SN[:, h, 0], RO[:, 7:512:8], ["R" + x + "1"], ["SN0" + hx])
-            act(T.SN[:, h, 2], RE[:, 0:512:8], ["R" + x + "0"], ["SN1" + hx])
+            move("a", T.SN[:, h, 0], RO[:, 7:512:8], ["R" + x + "1"], ["SN0" + hx])
+            move("a", T.SN[:, h, 2], RE[:, 0:512:8], ["R" + x + "0"], ["SN1" + hx])
             send(h, ee)
-        act(nh("M8L"), st(SL), [sk(SL)], ["M8L" + x], F.Relu, scale=8.0, bias=-56.0)
+        either(lambda: act(nh("M8L"), st(SL), [sk(SL)], ["M8L" + x], F.Relu, scale=8.0, bias=-56.0),
+               lambda: ts(nh("M8L"), st(SL), 8.0, A.is_equal, [sk(SL)], ["M8L" + x], 8.0, A.mult))
         tt(nf("ZP"), st(SBA), nh("M8L"), A.mult, [sk(SBA), "M8L" + x], ["ZP" + x])
         grp(mi(6), [(I, nh("A16")), (mf("I32"), nf("ZP"))], ["II", "I32", "A16" + x, "ZP" + x], [mk(6)])
         move("a", lst("LZ"), mi(6), [mk(6)], ["LZ" + x], 1280.0)
         gather(OPT["ng"], T.NG, o, "NG", T.NB[:, 0:W], ["NB"], "LZ", -1280.0)
         mm([(ps(mb, 384 + y, 512, 8), T.NG[:, o + y:o + 1024:8], T.IT[:, y:16:8], True, True) for y in range(8)], ["IT"] + both("NG"), [mk(6), mk(7)])
-        act(pad("n0", 2), mi(6, 2), [mk(6), mk(7), "PB"], ["n" + x], F.Identity, scale=8.0)
+        either(lambda: act(pad("n0", 2), mi(6, 2), [mk(6), mk(7), "PB"], ["n" + x], F.Identity, scale=8.0),
+               lambda: ts(pad("n0", 2), mi(6, 2), 8.0, A.mult, [mk(6), mk(7), "PB"], ["n" + x]))
         grp(st(SN_), turn("n0", I)[0:1] + turn("n1", I)[1:2], ["II", "n" + x], [sk(SN_)])
         grp(mi(4), [(mf("SH"), EE), (mf("H16"), T.RW[:, rw0:rw0 + 64]), (mf("HM1"), T.RW[:, rw0 + 1216:rw0 + 1280])], ["SH", "H16", "HM1", ee, "HALO" + hx], [mk(4)])
         ts(mi(4), mi(4), 0.0, A.is_ge, [mk(4)], [mk(4)])
@@ -505,11 +522,13 @@ def rank_program(g, core, T, topo):
             tt(par(T.PR1, e), ps(wb[e]), half(T.TT, e), A.mult, [wk(e), "T" + x + str(e)], ["P1" + x + str(e)])
         for i, j in enumerate((0, 3, 2, 1)):
             for e in range(2):
-                mm([(ps(mb, 64 * i + y, 64 * i + 64, 8), T["PR%d" % j][:, o + y:o + 1024:8], T.BO[:], True, True) for y in range(e, 8, 2)],
-                   ["BO", "P%d" % j + x + str(e), mk(i)], [mk(i) + str(e)])
-        act(nf("GM0", 2), mi(0, 2), [mk(i) + y for i in (0, 1) for y in ("0", "1", "")], ["GM" + x])
-        tt(mi(2), mi(2), nf("GM0"), A.mult, [mk(2) + "0", mk(2) + "1", "GM" + x], [mk(2)])
-        tt(nf("BV"), mi(3), nf("GM1"), A.mult, [mk(3) + "0", mk(3) + "1", mk(3), "GM" + x], ["BV" + x])
+                at, tok = (mi(i), mk(i)) if i < 3 else (st(SLR), sk(SLR))
+                mm([(at[:, y:64:8], T["PR%d" % j][:, o + y:o + 1024:8], T.BO[:], True, True) for y in range(e, 8, 2)],
+                   ["BO", "P%d" % j + x + str(e), tok], [tok + str(e)])
+        for i in range(2):
+            move("a", nf("GM%d" % i), mi(i), [mk(i) + y for y in ("0", "1", "")], ["GM%d" % i + x])
+        tt(mi(2), mi(2), nf("GM0"), A.mult, [mk(2) + "0", mk(2) + "1", "GM0" + x], [mk(2)])
+        tt(nf("BV"), st(SLR), nf("GM1"), A.mult, [sk(SLR) + "0", sk(SLR) + "1", sk(SLR), "GM1" + x], ["BV" + x])
         if OPT["sg"] == "a":
             tt(mi(2), mi(2), nf("BV"), A.subtract, [mk(2), "BV" + x], [mk(2)])
             act(pad("c0"), mi(2), [mk(2), "PB"], ["c0" + x], F.Sign)
@@ -527,8 +546,10 @@ def rank_program(g, core, T, topo):
             grp(mi(3), lr + [(mc("N2"), nh("UP")), (I, nh("DN"))], ["II", "IM1", "N2", "LL" + x, "c0" + x, "UP" + x, "DN" + x], [mk(3)])
             move("a", nh("LP", 2), mi(2, 2), [mk(2), mk(3)], ["LP" + x, "L2L" + x])
         else:
-            act(nh("UP"), st(SLR), [sk(SLR)], ["UP" + x], F.Relu, bias=-8.0)
-            act(nh("DN"), st(SLR), [sk(SLR)], ["DN" + x], F.Relu, scale=-1.0)
+            either(lambda: act(nh("UP"), st(SLR), [sk(SLR)], ["UP" + x], F.Relu, bias=-8.0),
+                   lambda: ts(nh("UP"), st(SLR), 9.0, A.is_equal, [sk(SLR)], ["UP" + x]))
+            either(lambda: act(nh("DN"), st(SLR), [sk(SLR)], ["DN" + x], F.Relu, scale=-1.0),
+                   lambda: ts(nh("DN"), st(SLR), -1.0, A.is_equal, [sk(SLR)], ["DN" + x]))
             act(nh("W8"), st(SLR), [sk(SLR)], ["W8" + x], F.Abs, scale=-1.0, bias=8.0)
             act(nh("L2L"), nh("W8"), ["W8" + x], ["L2L" + x], F.Relu, scale=-1.0, bias=8.0)
             grp(mi(2), [(I, nh("L2L")), (mc("EM6"), nh("UP")), (mc("E7"), nh("DN"))], ["II", "EM6", "E7", "L2L" + x, "UP" + x, "DN" + x], [mk(2)])
@@ -569,7 +590,7 @@ def rank_program(g, core, T, topo):
             for i, k in ((0, 15), (1, 0)):
                 grp(mi(i), [(mc("I7"), T.XA[:, po + k:po + 1024:16]), (I, L2[k % 2][:, k // 2:512:8]), (mc("P8"), T.XU[:, po + k:po + 1024:16])],
                     both("XA") + both("XU") + both("L2") + ["II", "I7", "P8"], [mk(i)])
-            act(T.SN[:, h + 2, 0:3:2], mi(0, 2), [mk(0), mk(1)], ["SN0" + h1, "SN1" + h1])
+            move("a", T.SN[:, h + 2, 0:3:2], mi(0, 2), [mk(0), mk(1)], ["SN0" + h1, "SN1" + h1])
             grp(ps(mb, 192, 208), [(T.CK[:, j % 2, 15 - j:143 - j], nh("AE", 2)[:, 64 * (j // 2 % 2) + j // 4:64 * (j // 2 % 2) + 64:4]) for j in range(16)],
                 ["CK0", "CK1", "AE" + x], [mk(3)])
             move("a", lst("LE", 0, 16), ps(mb, 192, 208), [mk(3)], ["LE" + x], 1280.0)
@@ -579,12 +600,20 @@ def rank_program(g, core, T, topo):
             tt(nf("ME"), mi(6), nh("LP"), A.mult, [mk(6), "LP" + x], ["ME" + x])
             tt(T.SN[:, h + 2, 1], mi(5), nf("ME"), A.add, [mk(5), "ME" + x], ["SN2" + h1])
             send(h + 2, "SN2" + h1)
-        grp(mi(7), [(T.SM[:, k], T.AD[:, o + 512 * (k % 2) + k // 2:o + 512 * (k % 2) + 512:8]) for k in range(15)],
-            ["SM%d" % k for k in range(15)] + both("AD"), [mk(7)])
+        pp = ps(wb[0], 0, 64)
+        for e in range(2):
+            grp(pp, [(T.SM[:, k], T.AD[:, o + 512 * e + k // 2:o + 512 * e + 512:8]) for k in range(e, 15, 2)],
+                ["SM%d" % k for k in range(e, 15, 2)] + ["AD" + x + str(e)], [wk(0)], start=e == 0, stop=e == 1)
         ph = [T.PH[:, 2 * s + i, 1:129:2] for i in range(2)]
-        ts(nf("SPH"), mi(7), MAG, A.add, [mk(7)], ["SPH" + x], -MAG, A.add)
-        tt(nf("SPL"), mi(7), nf("SPH"), A.subtract, [mk(7), "SPH" + x], ["SPL" + x])
-        move("a", T.PH[:, 2 * s:2 * s + 2, 1:129:2], nf("SPH", 2), ["SPH" + x, "SPL" + x, "PH"], ["PH0" + x, "PH1" + x])
+        if OPT["ph"]:
+            ts(ph[0], pp, MAG, A.add, [wk(0), "PH"], ["PH0" + x], -MAG, A.add)
+            tt(ph[1], pp, ph[0], A.subtract, [wk(0), "PH0" + x, "PH"], ["PH1" + x])
+            move("a", nf("SPH"), ph[0], ["PH0" + x], ["SPH" + x])
+            move("a", nf("SPL"), ph[1], ["PH1" + x], ["SPL" + x])
+        else:
+            ts(nf("SPH"), pp, MAG, A.add, [wk(0)], ["SPH" + x], -MAG, A.add)
+            tt(nf("SPL"), pp, nf("SPH"), A.subtract, [wk(0), "SPH" + x], ["SPL" + x])
+            move("a", T.PH[:, 2 * s:2 * s + 2, 1:129:2], nf("SPH", 2), ["SPH" + x, "SPL" + x, "PH"], ["PH0" + x, "PH1" + x])
         rowdma("SPH", 6, 7)
         rowdma("SPL", 8, 9)
         for e in range(2):
@@ -598,26 +627,26 @@ def rank_program(g, core, T, topo):
             else:
                 ts(cz, ps(wb[e], 0, 448), 0.0, A.is_ge, [wk(e)], ["CZ" + x + str(e)], 2.0, A.mult)
         cd = "CD" if opt("cz") == "aa" else "CD1"
-        grp(mi(7), [(mc("IMID"), T.PP[:]), (mc(cd), T.ONE[:, 0:64])] + [(mc("MID32"), T.CZ[:, 896 * s + 64 * j:896 * s + 64 * j + 64]) for j in range(14)],
-            ["IMID", cd, "MID32", "PP", "ONE"] + both("CZ"), [mk(7)])
-        move("a", lst("LW"), mi(7), [mk(7)], ["LW" + x])
+        for e in range(2):
+            grp(pp, [(mc("IMID"), T.PP[:]), (mc(cd), T.ONE[:, 0:64])][2 * e:] + [(mc("MID32"), T.CZ[:, 896 * s + 64 * j:896 * s + 64 * j + 64]) for j in range(7 * e, 7 * e + 7)],
+                ["IMID", cd, "MID32", "PP", "ONE", "CZ" + x + str(e)], [wk(0)], start=e == 0, stop=e == 1)
+        move("a", lst("LW"), pp, [wk(0)], ["LW" + x])
         gather(opt("wg"), T.WG, o, "WG", T.WE[:, we0 + 64:we0 + WEN], ["WR%d" % i + x for i in range(16) if not (last and 2 <= i < 6)], "LW")
-        xb = wb[0]
-        it = [(ps(xb), Z128, T.ZERO[:], True, False)]
-        it += [(ps(xb, 384, 448), T.PH[:, 2 * s + i, 1 - y:129 - y], T.KS[:, y], False, False) for i in range(2) for y in range(2)]
-        mm(it, ["ZERO", "KS", "PH0" + x, "PH1" + x], [wk(0)])
-        it = [(ps(xb, y, 512, 8), T.WG[:, o + y:o + 1024:8], T.XH[:], False, False) for y in range(8)]
-        it += [(ps(xb, 384 + y, 512, 8), T.WG[:, o + y:o + 1024:8], T.XL[:], False, False) for y in range(8)]
-        it.append((ps(xb, 384, 512), T.ONE[:], T.CR[:], False, True))
-        mm(it, ["XH", "XL", "ONE", "CR"] + both("WG"), [wk(0)])
-        act(pad("a", k=2), ps(xb, 0, 128), [wk(0), "PB"], ["ab" + x])
-        op("v", lambda: V.reciprocal(nf("RC"), ps(xb, 448, 512)), [wk(0)], ["RC" + x], cost=190 + 384 * CYC)
+        xb, yb = wb
+        it = [(ps(yb, 0, 128), Z128, Z128, True, False)]
+        it += [(ps(yb, 0, 64), T.PH[:, 2 * s + i, 1 - y:129 - y], T.KS[:, y], False, False) for i in range(2) for y in range(2)]
+        mm(it, ["ZERO", "KS", "PH0" + x, "PH1" + x], [wk(1)])
+        mm([(ps(xb, y, 384, 8), T.WG[:, o + y:o + 1024:8], T.XH[:, 0:6], True, True) for y in range(8)], ["XH"] + both("WG"), [wk(0)])
+        it = [(ps(yb, y, 128, 8), T.WG[:, o + y:o + 1024:8], w, False, False) for w in (T.XH[:, 6:8], T.XL[:]) for y in range(8)]
+        mm(it + [(ps(yb, 0, 128), T.ONE[:], T.CR[:], False, True)], ["XH", "XL", "ONE", "CR"] + both("WG"), [wk(1)])
+        move("a", pad("a", k=2), ps(xb, 0, 128), [wk(0), "PB"], ["ab" + x])
+        op("v", lambda: V.reciprocal(nf("RC"), ps(yb, 64, 128)), [wk(1)], ["RC" + x], cost=190 + 384 * CYC)
         for i, n, e in ((SA, "a", "AE"), (SB, "b", "BE")):
             grp(st(i), turn(n, I) + [(mc("IEND"), nh(e))], ["II", "IEND", "ab" + x, "AE" + x], [sk(i)])
-        tt(nf("XX"), ps(xb, 384, 448), nf("RC"), A.mult, [wk(0), "RC" + x], ["XX" + x])
+        tt(nf("XX"), ps(yb, 0, 64), nf("RC"), A.mult, [wk(1), "RC" + x], ["XX" + x])
         ts(pad("l0"), nf("XX"), MAG, A.add, ["XX" + x, "PB"], ["l0" + x], -MAG, A.add)
-        tt(nf("YY"), ps(xb, 448, 512), pad("l0"), A.mult, [wk(0), "l0" + x], ["YY" + x])
-        tt(pad("cm"), ps(xb, 384, 448), nf("YY"), A.is_lt, [wk(0), "YY" + x, "PB"], ["cm" + x])
+        tt(nf("YY"), ps(yb, 64, 128), pad("l0"), A.mult, [wk(1), "l0" + x], ["YY" + x])
+        tt(pad("cm"), ps(yb, 0, 64), nf("YY"), A.is_lt, [wk(1), "YY" + x, "PB"], ["cm" + x])
         grp(st(SL), [(mc("IEND"), nh("LP")), (mc("EN8"), T.ONE[:, 0:64])] + turn("l0", I) + turn("cm", M1),
             ["II", "IM1", "IEND", "EN8", "ONE", "LP" + x, "l0" + x, "cm" + x], [sk(SL)])
         if last:
@@ -630,7 +659,7 @@ def rank_program(g, core, T, topo):
         move("a", nh("A16", 2), st(SA, 2), [sk(SA), sk(SB)], ["A16" + x, "B16" + x])
         move("a", nh("LL"), st(SL), [sk(SL)], ["LL" + x])
         grp(st(SBA), turn("b", mc("P8")) + turn("a", mc("M8")) + [(mc("EP8"), nh("BE")), (mc("EM8"), nh("AE"))], ["P8", "M8", "EP8", "EM8", "ab" + x, "AE" + x], [sk(SBA)])
-        act(pad("eh", k=4), ps(xb, 128, 384), [wk(0), "PB"], ["e" + x])
+        move("a", pad("eh", k=4), ps(xb, 128, 384), [wk(0), "PB"], ["e" + x])
         energies(ends(0, 0), ends(1, 0) + ends(2, 1), ["EK0", "EK1", "EK2", "EG" + x])
 
     for r in range(3):
@@ -640,8 +669,8 @@ def rank_program(g, core, T, topo):
     if "o" not in ORDER:
         ORDER["ops"] = ops
         ORDER["o"] = arrange(ops)
-    for i in ORDER["o"]:
-        issue(*ops[i][:5])
+    for i, other in ORDER["o"]:
+        issue(*((ops[i][8] if other else ops[i])[:2] + ops[i][2:5]))
     for s in ("v", "a", "p", "gq"):
         g.wait_ge(T.sem[s], cnt[s])
     for s, n in (("snt", 48), ("o1", 64), ("o2", 32)):

import numpy as np
from concourse.bass import DstId, RemoteDMATransfer
from concourse.mybir import AluOpType, ActivationFunctionType
A = AluOpType
F = ActivationFunctionType
W = 2560
f32, f16, b16, i32, u16 = "float32", "float16", "bfloat16", "int32", "uint16"
RWN, SNN, WEN, PAD = 1280, 192, 1152, 1040


def _sb(shape, dt):
    return ("sbuf", [128] + shape, dt)


MC = ["IEND", "EP8", "EM8", "EM6", "E7", "EN8", "DLM", "DAE", "IM1", "I7", "IM7", "P8", "M8", "IMID", "MID32", "CD", "CD1", "DLA", "DME", "DAF", "DK", "I16", "I64", "N8", "I8", "N2"]
MF = ["H16", "HM1", "I32", "SH"]
LISTS = ["LA", "LB", "LZ", "LN", "LU", "LW", "LE"]
NF = ["EM", "EE", "ME", "ZP", "Z2", "GM0", "GM1", "BV", "CP", "EP", "EC", "RC", "XX", "YY", "SC", "SEH", "SEL", "SPH", "SPL"]
NH = ["A16", "B16", "AE", "BE", "LL", "LP", "L2L", "M8L", "FD", "UP", "DN", "W8", "S8", "UA", "UB", "UN", "DA", "DB", "DNN"]
PADS = ["a", "b", "eh", "el", "dh", "dl", "l0", "cm", "c0", "c1", "n0", "n1"]
SCRATCH = {
    "ps": ("psum", [128, 4096], f32),
    "X": _sb([W], b16), "G": _sb([W], b16), "NB": _sb([W], i32), "ET": _sb([W], i32),
    "RW": _sb([6 * RWN], f32), "SN": _sb([6, 3, 64], f32), "WE": _sb([2 * WEN], f32),
    "XA": _sb([2 * PAD], b16), "XU": _sb([2 * PAD], b16), "L2": _sb([2 * PAD], f16),
    "D": _sb([2048], b16), "GA": _sb([2048], b16), "DG": _sb([2048], b16), "LG": _sb([2048], f16),
    "TT": _sb([2048], f16), "NG": _sb([2048], f16), "AD": _sb([2048], f16), "WG": _sb([2048], f16), "CZ": _sb([1792], b16),
    "PR0": _sb([2048], f32), "PR1": _sb([2048], f32), "PR2": _sb([2048], f32), "PR3": _sb([2048], f32), "EG": _sb([512], f16),
    "LST": _sb([128 * len(LISTS)], u16), "NFB": _sb([128 * len(NF)], f32), "NHB": _sb([128 * len(NH)], f16),
    "PB": _sb([2 * len(PADS), 18, 8], f16), "PH": _sb([4, 130], f16), "IT": _sb([16, 8], b16), "BOX": _sb([128], b16),
    "PI": _sb([384], i32), "EI": _sb([3, 160], i32), "YO": _sb([384], f32),
    "II": _sb([8, 16], b16), "MCB": _sb([len(MC), 8, 16], b16), "MFB": _sb([len(MF), 8, 16], f32),
    "BK": _sb([16, 8, 16], b16), "ZM": _sb([14, 128], b16), "ZK": _sb([128], b16),
    "ZERO": _sb([512], b16), "ONE": _sb([128], b16), "PP": _sb([64], b16), "KI": _sb([128], b16), "BO": _sb([8], f32),
    "PM": _sb([2, 18, 8], f16), "CK": _sb([2, 144], f16), "EK": _sb([3, 144], f16), "E0": _sb([6, 8], f16), "SM": _sb([15, 128], b16),
    "XH": _sb([8, 8], b16), "XL": _sb([2, 8], b16), "KS": _sb([2, 64], b16), "CR": _sb([128], b16), "DL": _sb([128], f16),
}
SEMAPHORES = ["v", "a", "p", "gq", "dx", "dg", "dn", "de", "dw", "dz", "dpa", "dpb", "dpl", "snt", "o1", "o2"] + [n + str(i) for n in "hw" for i in range(6)]
MAG = 12582912.0
END = slice(0, 16, 15)
CYC, GAM, PCYC, FIX, WAKE = 0.83, 1.56, 0.417, 50.0, 120.0
OPT = {"lead": 6000.0, "turns": 700, "seed": 4, "flip": 2, "ph": 0, "even": 0.3, "tilt": 0.0, "ud": 0, "e1": "aa", "radd": "av", "D": 2, "DG": 2, "cz": "aa", "wg": "aa", "ng": "aa", "e0": "aa", "sg": "v", "tail": 5, "ga": "aa", "xu": "aa", "xa": "aa", "dma": 2500.0, "rem": 7000.0}
ORDER = {}


def bank(t):
    return t[0] == "b" and t[2] == "."


def arrange(ops):
    n = len(ops)
    pred = [set() for _ in range(n)]
    lw, rd = {}, {}
    for i, o in enumerate(ops):
        for t in o[2] + o[3]:
            if t in lw:
                pred[i].add(lw[t])
            if t in o[3]:
                pred[i].update(rd.get(t, ()))
        for t in o[2]:
            rd.setdefault(t, []).append(i)
        for t in o[3]:
            lw[t] = i
            rd[t] = []
        pred[i].discard(i)
    succ = [[] for _ in range(n)]
    for i in range(n):
        for j in pred[i]:
            succ[j].append(i)
    banks = [sorted(set(t[1] for t in o[2] + o[3] if bank(t))) for o in ops]
    free = [i for i in range(n) if ops[i][8]]

    def place(before, after, key, other, back):
        left = [len(p) for p in before]
        ready = sorted((key[i], i) for i in range(n) if not left[i])
        busy, start, end = {}, [0.0] * n, [0.0] * n
        while ready:
            i = ready.pop()[1]
            q, c, late = (ops[i][8][0], ops[i][8][2], 0.0) if i in other else (ops[i][0], ops[i][5], ops[i][6])
            s = max([end[j] + (0.0 if q == "p" == ops[j][0] else WAKE) for j in before[i]], default=0.0) + (late if back else 0.0)
            needs = [q] + banks[i]
            moved = True
            while moved:
                moved = False
                for k, res in enumerate(needs):
                    l = busy.setdefault(res, [])
                    for t0, t1, q2 in l[max(0, find(l, s) - 2):]:
                        gap = WAKE if k and q2 != q else 0.0
                        if t0 - gap >= s + c:
                            break
                        if t1 + gap > s and (k == 0 or q2 != q):
                            s, moved = t1 + gap, True
            for res in needs:
                busy[res].insert(find(busy[res], s), (s, s + c, q))
            start[i], end[i] = s, s + c + (0.0 if back else late)
            for j in after[i]:
                left[j] -= 1
                if not left[j]:
                    ready.insert(find(ready, key[j]), (key[j], j))
        return start, end

    def find(l, t):
        lo, hi = 0, len(l)
        while lo < hi:
            m = (lo + hi) // 2
            lo, hi = (m + 1, hi) if l[m][0] < t else (lo, m)
        return lo

    def settle(key, other):
        one = place(pred, succ, key, other, False)
        two = place(pred, succ, place(succ, pred, one[1], other, True)[1], other, False)
        one = min(one, two, key=lambda x: max(x[1]))
        load = sum(ops[i][8][2] * (1 if ops[i][8][0] == "v" else -1) for i in other)
        return max(one[1]) + OPT["even"] * abs(load + OPT["tilt"]), one[0], other
    key = [0.0] * n
    for i in range(n - 1, -1, -1):
        key[i] = ops[i][5] + ops[i][6] + WAKE + max([key[j] for j in succ[i]], default=OPT["lead"] * (ops[i][7] == 0))
    best = settle(key, set())
    rng = np.random.default_rng(OPT["seed"])
    for turn in range(OPT["turns"]):
        mid, wide, s, by = rng.uniform(0, best[0]), rng.uniform(2000, 10000), int(rng.integers(2)), rng.normal(0, 2500)
        other = best[2]
        if turn % 2:
            other, by = other ^ set(int(i) for i in rng.choice(free, OPT["flip"])), 0.0
        new = settle([(by if ops[i][7] == s and abs(t - mid) < wide else 0.0) - t for i, t in enumerate(best[1])], other)
        if new[0] <= best[0]:
            best = new
    ORDER["t"] = best
    return [(i, i in best[2]) for i in sorted(range(n), key=lambda i: (best[1][i], i))]


def rank_program(g, core, T, topo):
    rank = T.rank_of(core)
    if rank is None:
        return
    N = len(T.cores)
    prv, nxt = T.cores[(rank - 1) % N], T.cores[(rank + 1) % N]
    Q = {"v": g.vector, "a": g.scalar, "p": g.tensor, "gq": g, "s": g.sync}
    V, S, P = g.vector, g.scalar, g.tensor
    cnt = {"v": 0, "a": 0, "p": 0, "gq": 0}
    seen = {q: {} for q in Q}
    lastw, readers, users = {}, {}, {}
    ops, lead = [], [0.0]

    def op(q, fn, r=(), w=(), ev=None, cost=100.0, late=0.0):
        ops.append((q, fn, list(r), list(w), ev, cost, late, lead[0], None))

    def either(one, two):
        one()
        two()
        alt = ops.pop()
        ops.append(ops.pop()[:8] + ((alt[0], alt[1], alt[5]),))

    def issue(q, fn, r, w, ev):
        want = {}
        for t in r + w:
            evs = [lastw.get(t)]
            if t in w:
                evs += readers.get(t, {}).items()
            if bank(t):
                evs += [e for e in users.get(t[1], {}).items() if e[0] != q]
            for e in evs:
                if e is not None:
                    want[e[0]] = max(want.get(e[0], 0), e[1])
        for s, n in want.items():
            if not s == "p" == q and seen[q].get(s, 0) < n:
                seen[q][s] = n
                Q[q].wait_ge(T.sem[s], n)
        ins = fn()
        if ev is None:
            cnt[q] += 1
            ev = (q, cnt[q])
            ins.then_inc(T.sem[q], 1)
        elif ev[0] != "snt":
            ins.then_inc(T.sem[ev[0]], 16)
        for t in r:
            readers.setdefault(t, {})[ev[0]] = ev[1]
        for t in w:
            lastw[t] = ("h" + t[4:], 8) if t[:4] == "HALO" else ev
            readers[t] = {}
        for t in r + w:
            if bank(t):
                users.setdefault(t[1], {})[q] = ev[1]

    def nel(ap):
        n = 1
        for x in ap.shape[1:]:
            n *= x
        return n

    def short(*aps):
        return all("16" in str(x.dtype) for x in aps)

    def cost(out, r, k):
        return FIX + nel(out) * GAM * CYC if any(t[:2] in LISTS for t in r) else FIX + max(64, nel(out) * k) * CYC

    def tt(out, a, b, o, r, w):
        op("v", lambda: V.tensor_tensor(out, a, b, o), r, w, cost=cost(out, r, 1.0 if any(bank(t) for t in r) else 2.0))

    def ts(out, a, s1, o1, r, w, s2=None, o2=None):
        c = cost(out, r, 0.5 if short(out, a) else 1.0)
        if o2 is None:
            op("v", lambda: V.tensor_scalar(out, a, s1, None, o1), r, w, cost=c)
        else:
            op("v", lambda: V.tensor_scalar(out, a, s1, s2, o1, o2), r, w, cost=c)

    def fill(out, w, v=0.0):
        op("v", lambda: V.memset(out, v), (), w, cost=cost(out, (), 0.5 if short(out) else 1.0))

    def act(out, a, r, w, func=F.Copy, **kw):
        op("a", lambda: S.activation(out, a, func, **kw), r, w, cost=cost(out, r, 1.0) + 15.0)

    def move(q, out, a, r, w, bias=None):
        either(lambda: copy(q, out, a, r, w, bias), lambda: copy("av"[q == "a"], out, a, r, w, bias))

    def copy(q, out, a, r, w, bias):
        if q == "a" and bias is None:
            act(out, a, r, w)
        elif q == "a":
            act(out, a, r, w, F.Identity, bias=bias)
        elif bias is None:
            op("v", lambda: V.tensor_copy(out, a), r, w, cost=cost(out, r, 0.5 if short(out, a) else 1.0))
        else:
            ts(out, a, bias, A.add, r, w)

    def mm(items, r, w):
        def fn():
            for o, l, rh, st, sp in items:
                ins = P.matmul(o, l, rh, st, sp)
            return ins
        op("p", fn, r, w, cost=sum(max(64, nel(x[2])) * (1 if short(x[1]) else 4) * PCYC for x in items))

    def grp(out, pairs, r, w, start=True, stop=True):
        mm([(out, l, rh, start and i == 0, stop and i == len(pairs) - 1) for i, (l, rh) in enumerate(pairs)], r, w)

    def dma(q, out, in_, r, w, ev, late):
        op(q, lambda: Q[q].dma_start(out, in_), r, w, ev, 100.0, late)

    def ps(b, c0=0, c1=512, st=1):
        return T.ps[:, 512 * b + c0:512 * b + c1:st]

    def mc(n):
        return T.MCB[:, MC.index(n)]

    def mf(n):
        return T.MFB[:, MF.index(n)]
    I = T.II[:]

    dma("a", T.EI[:, 0], T.erec[:], [], ["EI"], ("de", 16), 2300.0)
    dma("s", T.X[:], T.xrec[:], [], ["X"], ("dx", 16), 4600.0)
    dma("a", T.PI[:, 0:128], T.pa[:], [], ["PIa"], ("dpa", 16), 2300.0)
    dma("a", T.PI[:, 128:256], T.pb[:], [], ["PIb"], ("dpb", 16), 2300.0)
    dma("a", T.PI[:, 256:384], T.lam[:], [], ["PIl"], ("dpl", 16), 2300.0)
    op("v", lambda: V.memset(T.ET[:], 0), (), ["ET"], cost=W * CYC)
    ts(T.EI[:, 1], T.EI[:, 0], 10, A.arith_shift_right, ["EI"], ["EI1"])
    ts(T.EI[:, 2], T.EI[:, 0], 1023, A.bitwise_and, ["EI"], ["EI2"])
    for i in range(2):
        dma("s", T.ET[i:128:16, :], T.EI[:, 1 + i], ["EI%d" % (1 + i), "ET"], ["ET%d" % i], ("dw", 32), 2300.0)
    ETt = ["ET0", "ET1"]
    dma("s", T.G[:], T.grec[:], ["X"], ["G"], ("dg", 16), 4600.0)
    dma("s", T.NB[:], T.nbr[:], ["X"], ["NB"], ("dn", 16), 9000.0)

    def iota(n, pat, base=0, cm=0, ap=None):
        o = T[n][:] if ap is None else ap
        op("gq", lambda: g.iota(o, pat, base, cm, allow_small_or_imprecise_dtypes=True), w=[n], cost=130 + 2 * CYC * nel(o))

    def sel(n, src, pat, cmp, v, base=0, cm=1, ap=None, sap=None):
        o = T[n][:] if ap is None else ap
        op("gq", lambda: g.affine_select(o, T[src][:] if sap is None else sap, pat, cmp, v, base, cm), [src], [n], cost=170 + 2 * CYC * nel(o))

    def rows(n, lo, hi, lead=(), tail=()):
        sel(n, n, list(lead) + [[-16, 8]] + list(tail), A.is_ge, 0.0, -lo, 1)
        sel(n, n, list(lead) + [[16, 8]] + list(tail), A.is_ge, 0.0, hi, -1)

    def put(out, src, v, w, r=()):
        act(out, src, ["II"] + list(r), [w], F.Identity, scale=float(v))
    Z128 = T.ZERO[:, 0:128]
    iota("KI", [[0, 128]])
    sel("II", "KI", [[-1, 128]], A.not_equal, 1.0)
    sel("IT", "KI", [[-1, 16], [-16, 8]], A.not_equal, 0.125)
    iota("KI", [[0, 8], [1, 16]])
    iota("PP", [[1, 64]])
    iota("ONE", [[0, 128]], 1)
    iota("BO", [[0, 8]], 1)
    rows("BO", 0, 15)
    for n in ("PM", "CK", "EK", "PB", "PH", "ZERO"):
        fill(T[n][:], [n])
    for n, k in (("XH", 64), ("XL", 16), ("CR", 128)):
        iota(n, [[0, k]])
    for s in range(2):
        fill(T.WE[:, WEN * s + 1024:WEN * s + WEN], ["WE%d" % s])
        for row in range(10, 16):
            dma("s", T.WE[row:128:16, WEN * s:WEN * s + 1024], T.WE[:, 1088:WEN], ["WE0", "G"], ["WR%d%d" % (row, s)], ("dz", 192), 2500.0)
    fill(T.L2[:, 512:513 + PAD:PAD], ["L2p"])
    for n in ("XA", "XU"):
        iota(n + "p", [[0, 2]], ap=T[n][:, 1024:1025 + PAD:PAD])
        iota(n + "p", [[0, 2]], ap=T[n][:, 1025:1026 + PAD:PAD])
    for i in range(16):
        act(T.BK[:, :, :, i], T.IT[:], ["IT"], ["BK%d" % i])
    BKt = ["BK%d" % i for i in range(16)]

    fill(T.MCB[:, 0:8], ["MC0"])
    fill(T.MFB[:, 0:2], ["MC0"])

    def diag(n, v, single=(), buf=T.MCB, names=MC, step=0):
        i = names.index(n)
        if v:
            sel(n, "ZERO", [[-1, 128]], A.not_equal, float(v), -step, ap=buf[:, i], sap=Z128)
        for k, d, row, u in single:
            o = buf[:, i, :, k:16:d]
            sel(n, n if v else "MC0", [[-16, 8], [-d, o.shape[2]]], A.not_equal, float(u), -row, ap=o, sap=o)
    for n, v in (("P8", 0.125), ("M8", -0.125), ("IM1", -1), ("I16", 16), ("I64", 64), ("I7", 0.875), ("IM7", -0.875), ("N8", -8), ("I8", 8), ("N2", -2)):
        diag(n, v)
    for n, v, e in (("IEND", 0, 1), ("EP8", 0, 0.125), ("EM8", 0, -0.125), ("EM6", 0, -6), ("E7", 0, 7), ("EN8", 0, -8),
                    ("IMID", 1, 0), ("MID32", 32, 0), ("CD", 448, 1024), ("CD1", 224, 1024)):
        diag(n, v, [(0, 15, 0, e)])
    diag("DLM", 0, [(0, 16, 0, 7), (15, 16, 15, -7)])
    diag("DLA", 1, [(0, 16, 0, -512), (15, 16, 15, -71)])
    diag("DME", 16, [(0, 8, 0, 2)])
    diag("DAE", 0, [(0, 8, 0, 512)])
    diag("DAF", -1, [(0, 16, 0, 0), (8, 16, 8, -7)])
    tt(mc("DK"), I, T.KI[:], A.mult, ["II", "KI"], ["DK"])
    diag("I32", 1, buf=T.MFB, names=MF)
    diag("SH", 1, [(15, 16, 16, 0)], T.MFB, MF, 1)
    sel("SH", "SH", [[-1, 128]], A.not_equal, -1.0, 1, ap=mf("SH"), sap=mf("SH"))
    sel("SH", "SH", [[-16, 8]], A.not_equal, 0.0, 1, ap=T.MFB[:, MF.index("SH"), :, 0], sap=T.MFB[:, MF.index("SH"), :, 0])
    diag("H16", 0, [(15, 16, 0, 1)], T.MFB, MF)
    diag("HM1", 0, [(0, 16, 15, -1)], T.MFB, MF)
    for e in range(2):
        put(T.PM[:, e, 1:16:2], T.II[:, :, e:16:2], 1, "PM%d" % e, ["PM"])
        put(T.CK[:, e, 15:143:16], T.II[:, :, 15 * e], 1, "CK%d" % e, ["CK"])
    for i, (row, v) in enumerate(((0, 1), (1, 1 / 1024), (0, -1), (1, -1 / 1024), (0, 1), (1, 1 / 1024))):
        put(T.E0[:, i], T.II[:, :, row], v, "E0")
    tt(T.EK[:, 0, 15:143:16], T.E0[:, 0], T.E0[:, 1], A.add, ["E0", "EK"], ["EK0"])
    put(T.EK[:, 1, 15:143:16], T.EK[:, 0, 15:143:16], -0.125, "EK1", ["EK0"])
    put(T.EK[:, 2, 15:143:16], T.EK[:, 0, 15:143:16], 0.125, "EK2", ["EK0"])
    grp(ps(1, 384, 448), [(mc("DLM"), T.PP[:]), (mc("DLA"), T.ONE[:, 0:64])], ["DLM", "DLA", "PP", "ONE"], ["b1.6"])
    grp(ps(1, 448, 480), [(mc("DME"), T.PP[:, 0:32]), (mc("DK"), T.ONE[:, 0:32]), (mc("DAE"), T.ONE[:, 0:32]), (mc("DAF"), T.ONE[:, 0:32])], ["DME", "DK", "DAE", "DAF", "PP", "ONE"], ["b1.7"])
    grp(ps(1, 480, 512), [(mc("I16"), T.PP[:, 0:32]), (mc("DK"), T.ONE[:, 0:32]), (mc("I64"), T.ONE[:, 0:32])], ["I16", "DK", "I64", "PP", "ONE"], ["b1.7"])
    act(T.DL[:], ps(1, 384, 512), ["b1.6", "b1.7"], ["DL"])
    sel("BOX", "ONE", [[0, 128]], A.is_gt, 1 / 32, 0, 0)
    rows("BOX", 0, 15, tail=[[0, 16]])
    for k in range(15):
        sel("SM%d" % k, "BOX", [[0, 8], [1, 16]], A.is_gt, 0.0, -k, 0, ap=T.SM[:, k])
    iota("ZK", [[0, 8], [1, 16]])
    sel("ZK", "ZK", [[-16, 8], [0, 16]], A.is_equal, 0.0, -15)
    for j in range(1, 15):
        sel("ZM%d" % j, "ZK", [[-16, 8], [0, 16]], A.not_equal, -15.0, -j, ap=T.ZM[:, j - 1])
    iota("KS", [[128, 2], [0, 8], [16, 8]])
    sel("KS", "KS", [[0, 2], [-16, 8], [0, 8]], A.is_equal, 0.0, -15)
    sel("KS", "KS", [[8, 2], [0, 8], [1, 8]], A.not_equal, 0.0, -15, 0)
    for n, q, row, v in [("XH", 0, 0, 1), ("XH", 1, 1, 1), ("XH", 2, 2, 1), ("XH", 3, 3, 1), ("XH", 4, 4, 1), ("XH", 4, 2, -1), ("XH", 5, 5, 1), ("XH", 5, 3, -1),
                         ("XH", 6, 6, -255), ("XH", 6, 7, 15), ("XH", 7, 6, -30), ("XH", 7, 7, 30),
                         ("XL", 0, 8, -255), ("XL", 0, 9, 15), ("XL", 1, 8, -30), ("XL", 1, 9, 30)]:
        sel(n, n, [[-16, 8]], A.not_equal, float(v), -row, ap=T[n][:, q], sap=T[n][:, q])
    for c, v in ((0, 1 / 1024), (64, 1 / 8192)):
        sel("CR", "CR", [[0, 64]], A.not_equal, v, ap=T.CR[:, c:c + 64], sap=T.CR[:, c:c + 64])

    def send(h, tok):
        rw0 = RWN * h
        e0, e1 = topo.engines(core, prv), topo.engines(core, nxt)
        m0 = sum(1 << e for e in e0[0:4])
        m1 = sum(1 << e for e in [y for y in e1 if not m0 >> y & 1][0:4])
        a0, a1 = topo.addr(prv), topo.addr(nxt)
        trs = [RemoteDMATransfer(dst_ids=[DstId(rid=a0[0], pnc=a0[1])], dma_engine_mask=m0, remote_sem=T.sem["h%d" % h],
                                 src=T.SN[:, h, 1:3], dst=T.RW[:, rw0:rw0 + 128]),
               RemoteDMATransfer(dst_ids=[DstId(rid=a1[0], pnc=a1[1])], dma_engine_mask=m1, remote_sem=T.sem["h%d" % h],
                                 src=T.SN[:, h, 0:2], dst=T.RW[:, rw0 + 1152:rw0 + 1280])]
        op("gq", lambda: g.remote_dma_fused(trs, local_sem=T.sem.snt), ["SN0%d" % h, "SN1%d" % h, tok], ["HALO%d" % h], ("snt", 48), 300.0, OPT["rem"])

    def stream(r, s):
        first, last = r == 0, r == 2
        sb, wb, mb = s, (2 + 2 * s, 3 + 2 * s), 6 + s
        x = str(s)
        o, po = 1024 * s, PAD * s

        def opt(n):
            return "av" if 2 * r + s >= OPT["tail"] else OPT[n]

        def st(i, n=1):
            return ps(sb, 64 * i, 64 * (i + n))

        def mi(i, n=1):
            return ps(mb, 64 * i, 64 * (i + n))

        def sk(i):
            return "b%d.%d" % (sb, i)

        def mk(i):
            return "b%d.%d" % (mb, i)

        def wk(e):
            return "b%d.w" % wb[e]

        def nf(n, k=1):
            c = 64 * (len(NF) * s + NF.index(n))
            return T.NFB[:, c:c + 64 * k]

        def nh(n, k=1):
            c = 64 * (len(NH) * s + NH.index(n))
            return T.NHB[:, c:c + 64 * k]

        def lst(n, c0=0, c1=64):
            c = 64 * (len(LISTS) * s + LISTS.index(n))
            return T.LST[:, c + c0:c + c1]

        def pad(n, k=1):
            i = len(PADS) * s + PADS.index(n)
            return T.PB[:, i:i + k, 1:16:2]

        def turn(n, rhs):
            i = len(PADS) * s + PADS.index(n)
            return [(T.PB[:, i, 1:17], rhs[:, :, 0:16:2]), (T.PB[:, i, 0:16], rhs[:, :, 1:16:2])]

        def half(t, c, base=o):
            return t[:, base + 512 * c:base + 512 * c + 512]

        def par(t, e, base=o, sh=0):
            return t[:, base + e + sh:base + 1024 + sh:2]

        def both(n):
            return [n + x + "0", n + x + "1"]

        def gather(q, dst, base, tok, win, wtok, ln, bias=None):
            if len(q) == 1:
                return move(q, dst[:, base:base + 1024], win.indirect(lst(ln)), wtok + [ln + x], both(tok), bias)
            for c in range(2):
                move(q[c], half(dst, c, base), win.indirect(lst(ln, 32 * c, 32 * c + 32)), wtok + [ln + x], [tok + x + str(c)], bias)

        def gsub(dst, tok, win, wtok, ln, src, base, stok):
            if OPT[tok] == 1:
                return tt(dst[:, o:o + 1024], win.indirect(lst(ln)), src[:, base:base + 1024], A.subtract, [wtok, ln + x] + both(stok), both(tok))
            for c in range(2):
                tt(half(dst, c), win.indirect(lst(ln, 32 * c, 32 * c + 32)), half(src, c, base), A.subtract, [wtok, ln + x, stok + x + str(c)], [tok + x + str(c)])

        def spread(src, tok):
            for e in range(2):
                mm([(ps(wb[e], kk, 512, 8), T.BK[:, 2 * kk + e], src, True, True) for kk in range(8)], BKt + [tok], [wk(e)])

        def ends(i, q):
            return [(T.EK[:, i, 15 - 15 * e:143 - 15 * e], T.EG[:, 256 * s + 2 * q + e:256 * s + 256:4]) for e in range(2)]

        def energies(ea, de, r_):
            grp(st(SEA), turn("eh", I) + turn("el", I) + ea, ["II", "e" + x] + r_, [sk(SEA)])
            grp(st(SDE), turn("dh", mc("P8")) + turn("dl", mc("P8")) + de, ["P8", "e" + x] + r_, [sk(SDE)])
        SA, SB, SBA, SEA, SDE, SL, SN_, SLR = range(8)
        h = 2 * r + s
        rw0, we0 = RWN * h, WEN * s
        RE, RO = T.RW[:, rw0 + 128:rw0 + 640], T.RW[:, rw0 + 640:rw0 + 1152]
        EE = T.SN[:, h, 1] if first else nf("EE")
        hx = str(h)
        M1 = mc("IM1")

        if first:
            for n, i in (("LA", 0), ("LB", 1)):
                move("v", lst(n), T.PI[:, 128 * i + 64 * s:128 * i + 64 * s + 64], ["PI" + "ab"[i]], [n + x])
                ts(nh("AB"[i] + "16"), T.PI[:, 128 * i + 64 * s:128 * i + 64 * s + 64], -1280.0, A.add, ["PI" + "ab"[i]], ["AB"[i] + "16" + x])
            move("v", nh("LL"), T.PI[:, 256 + 64 * s:320 + 64 * s], ["PIl"], ["LL" + x])
            mm([(st(SA, 2), I, nh("A16", 2), True, True), (st(SL), I, nh("LL"), True, True)], ["II", "A16" + x, "B16" + x, "LL" + x], [sk(SA), sk(SB), sk(SL)])
            grp(st(SBA), [(mc("P8"), nh("B16")), (mc("M8"), nh("A16"))], ["P8", "M8", "A16" + x, "B16" + x], [sk(SBA)])
            gather(OPT["e" + x][0], T.AD, o, "AD", T.ET[:, 0:W], ETt, "LA")
            gather(OPT["e" + x][1], T.WG, o, "WG", T.ET[:, 0:W], ETt, "LB")
            it = []
            for y in range(8):
                it += [(ps(mb, y, 256, 8), T.AD[:, o + y:o + 1024:8], T.E0[:, 0:4], True, False), (ps(mb, 128 + y, 256, 8), T.WG[:, o + y:o + 1024:8], T.E0[:, 4:6], False, True)]
            mm(it, ["E0"] + both("AD") + both("WG"), [mk(i) for i in range(4)])
            move("a", pad("eh", k=4), mi(0, 4), [mk(i) for i in range(4)] + ["PB"], ["e" + x])
            energies([], [], [])
        gather(OPT["xa"], T.XA, po, "XA", T.X[:, 0:W], ["X"], "LA")
        gsub(T.D, "D", T.X[:, 0:W], "X", "LB", T.XA, po, "XA")
        gather(OPT["ga"], T.GA, o, "GA", T.G[:, 0:W], ["G"], "LA")
        gsub(T.DG, "DG", T.G[:, 0:W], "G", "LB", T.GA, o, "GA")
        spread(nh("LL"), "LL" + x)
        for e in range(2):
            if h:
                tt(half(T.LG, e), ps(wb[e]), par(T.DG, e), A.mult, [wk(e)] + both("DG"), ["LG" + x + str(e)])
            if OPT["radd"][e] == "v":
                tt(ps(wb[e]), ps(wb[e]), par(T.D, e), A.mult, [wk(e)] + both("D"), [wk(e)])
                tt((RE, RO)[e], ps(wb[e]), par(T.XA, e, po), A.add, [wk(e)] + both("XA"), ["R" + x + str(e)])
            else:
                tt(half(T.TT, e), ps(wb[e]), par(T.D, e), A.mult, [wk(e)] + both("D"), ["T" + x + str(e)])
                grp(ps(wb[e]), [(I, par(T.XA, e, po)), (I, half(T.TT, e))], ["II", "T" + x + str(e)] + both("XA"), [wk(e)])
                move("a", (RE, RO)[e], ps(wb[e]), [wk(e)], ["R" + x + str(e)])
        if not h:
            spread(nh("LL"), "LL" + x)
            for e in range(2):
                tt(half(T.LG, e), ps(wb[e]), par(T.DG, e), A.mult, [wk(e)] + both("DG"), ["LG" + x + str(e)])
        tt(nf("EM"), st(SDE), nh("LL"), A.mult, [sk(SDE), "LL" + x], ["EM" + x])
        ee = "E%d" % first + x
        tt(EE, st(SEA), nf("EM"), A.add, [sk(SEA), "EM" + x], [ee])
        if first:
            move("a", T.SN[:, h, 0], RO[:, 7:512:8], ["R" + x + "1"], ["SN0" + hx])
            move("a", T.SN[:, h, 2], RE[:, 0:512:8], ["R" + x + "0"], ["SN1" + hx])
            send(h, ee)
        either(lambda: act(nh("M8L"), st(SL), [sk(SL)], ["M8L" + x], F.Relu, scale=8.0, bias=-56.0),
               lambda: ts(nh("M8L"), st(SL), 8.0, A.is_equal, [sk(SL)], ["M8L" + x], 8.0, A.mult))
        tt(nf("ZP"), st(SBA), nh("M8L"), A.mult, [sk(SBA), "M8L" + x], ["ZP" + x])
        grp(mi(6), [(I, nh("A16")), (mf("I32"), nf("ZP"))], ["II", "I32", "A16" + x, "ZP" + x], [mk(6)])
        move("a", lst("LZ"), mi(6), [mk(6)], ["LZ" + x], 1280.0)
        gather(OPT["ng"], T.NG, o, "NG", T.NB[:, 0:W], ["NB"], "LZ", -1280.0)
        mm([(ps(mb, 384 + y, 512, 8), T.NG[:, o + y:o + 1024:8], T.IT[:, y:16:8], True, True) for y in range(8)], ["IT"] + both("NG"), [mk(6), mk(7)])
        either(lambda: act(pad("n0", 2), mi(6, 2), [mk(6), mk(7), "PB"], ["n" + x], F.Identity, scale=8.0),
               lambda: ts(pad("n0", 2), mi(6, 2), 8.0, A.mult, [mk(6), mk(7), "PB"], ["n" + x]))
        grp(st(SN_), turn("n0", I)[0:1] + turn("n1", I)[1:2], ["II", "n" + x], [sk(SN_)])
        grp(mi(4), [(mf("SH"), EE), (mf("H16"), T.RW[:, rw0:rw0 + 64]), (mf("HM1"), T.RW[:, rw0 + 1216:rw0 + 1280])], ["SH", "H16", "HM1", ee, "HALO" + hx], [mk(4)])
        ts(mi(4), mi(4), 0.0, A.is_ge, [mk(4)], [mk(4)])
        tt(nh("FD"), mi(4), T.DL[:, 0:64], A.mult, [mk(4), "DL"], ["FD" + x])
        it = [(mi(5), I, T.DL[:, 64:128], True, False)]
        for e in range(2):
            for pp in range(2):
                it.append((ps(mb, 320 + 32 * e, 352 + 32 * e), T.PM[:, e, 1 - pp:17 - pp], nh("FD")[:, pp:64:2], False, e + pp == 2))
        mm(it, ["II", "DL", "PM0", "PM1", "FD" + x], [mk(5)])
        move("a", lst("LN"), mi(5), [mk(5)], ["LN" + x])
        wins = (T.RW[:, rw0 + 640:rw0 + 1216], T.RW[:, rw0 + 64:rw0 + 640])
        for e in range(2):
            tt(half(T.TT, e), wins[e].indirect(lst("LN", 32 * e, 32 * e + 32)), (RE, RO)[e], A.subtract, both("R") + ["HALO" + hx, "LN" + x], ["T" + x + str(e)])
            act(par(T.PR2, e), half(T.TT, e), ["T" + x + str(e)], ["P2" + x + str(e)], F.Square)
            grp(ps(wb[e]), [(I, par(T.GA, e)), (I, half(T.LG, e))], ["II", "LG" + x + str(e)] + both("GA"), [wk(e)])
            tt(par(T.PR0, e), ps(wb[e]), par(T.D, e), A.mult, [wk(e)] + both("D"), ["P0" + x + str(e)])
            tt(par(T.PR3, e), ps(wb[e]), half(T.TT, e), A.mult, [wk(e), "T" + x + str(e)], ["P3" + x + str(e)])
            mm([(ps(wb[e]), I, par(T.D, e), True, True)], ["II"] + both("D"), [wk(e)])
            tt(par(T.PR1, e), ps(wb[e]), half(T.TT, e), A.mult, [wk(e), "T" + x + str(e)], ["P1" + x + str(e)])
        for i, j in enumerate((0, 3, 2, 1)):
            for e in range(2):
                at, tok = (mi(i), mk(i)) if i < 3 else (st(SLR), sk(SLR))
                mm([(at[:, y:64:8], T["PR%d" % j][:, o + y:o + 1024:8], T.BO[:], True, True) for y in range(e, 8, 2)],
                   ["BO", "P%d" % j + x + str(e), tok], [tok + str(e)])
        for i in range(2):
            move("a", nf("GM%d" % i), mi(i), [mk(i) + y for y in ("0", "1", "")], ["GM%d" % i + x])
        tt(mi(2), mi(2), nf("GM0"), A.mult, [mk(2) + "0", mk(2) + "1", "GM0" + x], [mk(2)])
        tt(nf("BV"), st(SLR), nf("GM1"), A.mult, [sk(SLR) + "0", sk(SLR) + "1", sk(SLR), "GM1" + x], ["BV" + x])
        if OPT["sg"] == "a":
            tt(mi(2), mi(2), nf("BV"), A.subtract, [mk(2), "BV" + x], [mk(2)])
            act(pad("c0"), mi(2), [mk(2), "PB"], ["c0" + x], F.Sign)
            grp(st(SLR), [(I, nh("LL"))] + turn("c0", M1), ["II", "IM1", "LL" + x, "c0" + x], [sk(SLR)])
        else:
            tt(pad("c0"), mi(2), nf("BV"), A.is_lt, [mk(2), "BV" + x, "PB"], ["c0" + x])
            tt(pad("c1"), mi(2), nf("BV"), A.is_gt, [mk(2), "BV" + x, "PB"], ["c1" + x])
            grp(st(SLR), [(I, nh("LL"))] + turn("c0", I) + turn("c1", M1), ["II", "IM1", "LL" + x, "c0" + x, "c1" + x], [sk(SLR)])
        if OPT["ud"]:
            grp(mi(0), [(I, nh("LL")), (mc("N8"), T.ONE[:, 0:64])] + turn("c0", M1), ["II", "IM1", "N8", "ONE", "LL" + x, "c0" + x], [mk(0)])
            grp(mi(1), [(M1, nh("LL"))] + turn("c0", I), ["II", "IM1", "LL" + x, "c0" + x], [mk(1)])
            act(nh("UP", 2), mi(0, 2), [mk(0), mk(1)], ["UP" + x, "DN" + x], F.Relu)
            lr = [(I, nh("LL"))] + turn("c0", M1)
            grp(mi(2), lr + [(mc("N8"), nh("UP")), (mc("I8"), nh("DN"))], ["II", "IM1", "N8", "I8", "LL" + x, "c0" + x, "UP" + x, "DN" + x], [mk(2)])
            grp(mi(3), lr + [(mc("N2"), nh("UP")), (I, nh("DN"))], ["II", "IM1", "N2", "LL" + x, "c0" + x, "UP" + x, "DN" + x], [mk(3)])
            move("a", nh("LP", 2), mi(2, 2), [mk(2), mk(3)], ["LP" + x, "L2L" + x])
        else:
            either(lambda: act(nh("UP"), st(SLR), [sk(SLR)], ["UP" + x], F.Relu, bias=-8.0),
                   lambda: ts(nh("UP"), st(SLR), 9.0, A.is_equal, [sk(SLR)], ["UP" + x]))
            either(lambda: act(nh("DN"), st(SLR), [sk(SLR)], ["DN" + x], F.Relu, scale=-1.0),
                   lambda: ts(nh("DN"), st(SLR), -1.0, A.is_equal, [sk(SLR)], ["DN" + x]))
            act(nh("W8"), st(SLR), [sk(SLR)], ["W8" + x], F.Abs, scale=-1.0, bias=8.0)
            act(nh("L2L"), nh("W8"), ["W8" + x], ["L2L" + x], F.Relu, scale=-1.0, bias=8.0)
            grp(mi(2), [(I, nh("L2L")), (mc("EM6"), nh("UP")), (mc("E7"), nh("DN"))], ["II", "EM6", "E7", "L2L" + x, "UP" + x, "DN" + x], [mk(2)])
            move("a", nh("LP"), mi(2), [mk(2)], ["LP" + x])
        for n, m, i in (("UN", "UP", SN_), ("DNN", "DN", SN_), ("UA", "UP", SA), ("DA", "DN", SA), ("UB", "UP", SB), ("DB", "DN", SB)):
            tt(nh(n), st(i), nh(m), A.mult, [sk(i), m + x], [n + x])
        for i, terms in ((4, ("A16", "UN", "DNN", "-UA", "-DA")), (5, ("A16", "-UA", "-DA", "UB", "DNN")), (6, ("B16", "-UB", "-DB", "UN", "DA"))):
            grp(mi(i), [(M1, nh(t[1:])) if t[0] == "-" else (I, nh(t)) for t in terms], ["II", "IM1"] + [t.strip("-") + x for t in terms], [mk(i)])
        move("a", lst("LU"), mi(4), [mk(4)], ["LU" + x], 1280.0)
        move("a", nh("AE", 2), mi(5, 2), [mk(5), mk(6)], ["AE" + x])
        gather(opt("xu"), T.XU, po, "XU", T.X[:, 0:W], ["X"], "LU")
        spread(nh("L2L"), "L2L" + x)
        L2 = (T.L2[:, po:po + 512], T.L2[:, po + 528:po + 1040])
        for e in range(2):
            tt(L2[e], ps(wb[e]), par(T.D, e), A.mult, [wk(e)] + both("D"), ["L2" + x + str(e)])
        for e in range(2):
            grp(ps(wb[e]), [(mc("I7"), par(T.XA, 1 - e, po, 2 * e)), (mc("IM7"), par(T.XA, e, po))], both("XA") + ["I7", "IM7", "XAp"], [wk(e)], stop=False)
            grp(ps(wb[e]), [(I, (L2[1], T.L2[:, po + 1:po + 513])[e]), (M1, L2[e])], both("L2") + ["II", "IM1", "L2p"], [wk(e)], start=False, stop=False)
            grp(ps(wb[e]), [(mc("P8"), par(T.XU, 1 - e, po, 2 * e)), (mc("M8"), par(T.XU, e, po))], both("XU") + ["P8", "M8", "XUp"], [wk(e)], start=False)
            act(half(T.AD, e), ps(wb[e]), [wk(e)], ["AD" + x + str(e)], F.Abs)
        ts(nh("S8"), st(SLR), 4.0, A.is_gt, [sk(SLR)], ["S8" + x], 8.0, A.mult)
        tt(nf("CP"), st(SBA), nh("S8"), A.mult, [sk(SBA), "S8" + x], ["CP" + x])
        tt(nf("SC"), st(SA), nf("CP"), A.add, [sk(SA), "CP" + x], ["SC" + x])
        nd = 96 if last else 160

        def rowdma(n, here, before):
            for row, c in ((here, 64), (before, 0)):
                dma("s", T.WE[row:128:16, we0 + c:we0 + c + 1024], nf(n), [n + x, "WE" + x], ["WR%d" % row + x], ("w" + hx, nd), OPT["dma"])
        rowdma("SC", 0, 1)
        if not last:
            tt(nf("EP"), st(SDE), nh("S8"), A.mult, [sk(SDE), "S8" + x], ["EP" + x])
            tt(nf("EC"), st(SEA), nf("EP"), A.add, [sk(SEA), "EP" + x], ["EC" + x])
            ts(nf("SEH"), nf("EC"), MAG, A.add, ["EC" + x], ["SEH" + x], -MAG, A.add)
            tt(nf("SEL"), nf("EC"), nf("SEH"), A.subtract, ["EC" + x, "SEH" + x], ["SEL" + x])
            rowdma("SEH", 2, 4)
            rowdma("SEL", 3, 5)
            h1 = str(h + 2)
            for i, k in ((0, 15), (1, 0)):
                grp(mi(i), [(mc("I7"), T.XA[:, po + k:po + 1024:16]), (I, L2[k % 2][:, k // 2:512:8]), (mc("P8"), T.XU[:, po + k:po + 1024:16])],
                    both("XA") + both("XU") + both("L2") + ["II", "I7", "P8"], [mk(i)])
            move("a", T.SN[:, h + 2, 0:3:2], mi(0, 2), [mk(0), mk(1)], ["SN0" + h1, "SN1" + h1])
            grp(ps(mb, 192, 208), [(T.CK[:, j % 2, 15 - j:143 - j], nh("AE", 2)[:, 64 * (j // 2 % 2) + j // 4:64 * (j // 2 % 2) + 64:4]) for j in range(16)],
                ["CK0", "CK1", "AE" + x], [mk(3)])
            move("a", lst("LE", 0, 16), ps(mb, 192, 208), [mk(3)], ["LE" + x], 1280.0)
            move("a", T.EG[:, 256 * s:256 * s + 256], T.ET[:, 0:W].indirect(lst("LE", 0, 16)), ETt + ["LE" + x], ["EG" + x])
            grp(mi(5), ends(0, 0), ["EK0", "EG" + x], [mk(5)])
            grp(mi(6), ends(1, 0) + ends(2, 1), ["EK1", "EK2", "EG" + x], [mk(6)])
            tt(nf("ME"), mi(6), nh("LP"), A.mult, [mk(6), "LP" + x], ["ME" + x])
            tt(T.SN[:, h + 2, 1], mi(5), nf("ME"), A.add, [mk(5), "ME" + x], ["SN2" + h1])
            send(h + 2, "SN2" + h1)
        pp = ps(wb[0], 0, 64)
        for e in range(2):
            grp(pp, [(T.SM[:, k], T.AD[:, o + 512 * e + k // 2:o + 512 * e + 512:8]) for k in range(e, 15, 2)],
                ["SM%d" % k for k in range(e, 15, 2)] + ["AD" + x + str(e)], [wk(0)], start=e == 0, stop=e == 1)
        ph = [T.PH[:, 2 * s + i, 1:129:2] for i in range(2)]
        if OPT["ph"]:
            ts(ph[0], pp, MAG, A.add, [wk(0), "PH"], ["PH0" + x], -MAG, A.add)
            tt(ph[1], pp, ph[0], A.subtract, [wk(0), "PH0" + x, "PH"], ["PH1" + x])
            move("a", nf("SPH"), ph[0], ["PH0" + x], ["SPH" + x])
            move("a", nf("SPL"), ph[1], ["PH1" + x], ["SPL" + x])
        else:
            ts(nf("SPH"), pp, MAG, A.add, [wk(0)], ["SPH" + x], -MAG, A.add)
            tt(nf("SPL"), pp, nf("SPH"), A.subtract, [wk(0), "SPH" + x], ["SPL" + x])
            move("a", T.PH[:, 2 * s:2 * s + 2, 1:129:2], nf("SPH", 2), ["SPH" + x, "SPL" + x, "PH"], ["PH0" + x, "PH1" + x])
        rowdma("SPH", 6, 7)
        rowdma("SPL", 8, 9)
        for e in range(2):
            it = []
            for j in range(7):
                it += [(ps(wb[e], 64 * j, 64 * j + 64), T.ZM[:, 7 * e + j], ph[i], i == 0, i == 1) for i in range(2)]
            mm(it, ["PH0" + x, "PH1" + x] + ["ZM%d" % (7 * e + j + 1) for j in range(7)], [wk(e)])
            cz = T.CZ[:, 896 * s + 448 * e:896 * s + 448 * e + 448]
            if opt("cz")[e] == "a":
                act(cz, ps(wb[e], 0, 448), [wk(e)], ["CZ" + x + str(e)], F.Sign, bias=1 / 1024)
            else:
                ts(cz, ps(wb[e], 0, 448), 0.0, A.is_ge, [wk(e)], ["CZ" + x + str(e)], 2.0, A.mult)
        cd = "CD" if opt("cz") == "aa" else "CD1"
        for e in range(2):
            grp(pp, [(mc("IMID"), T.PP[:]), (mc(cd), T.ONE[:, 0:64])][2 * e:] + [(mc("MID32"), T.CZ[:, 896 * s + 64 * j:896 * s + 64 * j + 64]) for j in range(7 * e, 7 * e + 7)],
                ["IMID", cd, "MID32", "PP", "ONE", "CZ" + x + str(e)], [wk(0)], start=e == 0, stop=e == 1)
        move("a", lst("LW"), pp, [wk(0)], ["LW" + x])
        gather(opt("wg"), T.WG, o, "WG", T.WE[:, we0 + 64:we0 + WEN], ["WR%d" % i + x for i in range(16) if not (last and 2 <= i < 6)], "LW")
        xb, yb = wb
        it = [(ps(yb, 0, 128), Z128, Z128, True, False)]
        it += [(ps(yb, 0, 64), T.PH[:, 2 * s + i, 1 - y:129 - y], T.KS[:, y], False, False) for i in range(2) for y in range(2)]
        mm(it, ["ZERO", "KS", "PH0" + x, "PH1" + x], [wk(1)])
        mm([(ps(xb, y, 384, 8), T.WG[:, o + y:o + 1024:8], T.XH[:, 0:6], True, True) for y in range(8)], ["XH"] + both("WG"), [wk(0)])
        it = [(ps(yb, y, 128, 8), T.WG[:, o + y:o + 1024:8], w, False, False) for w in (T.XH[:, 6:8], T.XL[:]) for y in range(8)]
        mm(it + [(ps(yb, 0, 128), T.ONE[:], T.CR[:], False, True)], ["XH", "XL", "ONE", "CR"] + both("WG"), [wk(1)])
        move("a", pad("a", k=2), ps(xb, 0, 128), [wk(0), "PB"], ["ab" + x])
        op("v", lambda: V.reciprocal(nf("RC"), ps(yb, 64, 128)), [wk(1)], ["RC" + x], cost=190 + 384 * CYC)
        for i, n, e in ((SA, "a", "AE"), (SB, "b", "BE")):
            grp(st(i), turn(n, I) + [(mc("IEND"), nh(e))], ["II", "IEND", "ab" + x, "AE" + x], [sk(i)])
        tt(nf("XX"), ps(yb, 0, 64), nf("RC"), A.mult, [wk(1), "RC" + x], ["XX" + x])
        ts(pad("l0"), nf("XX"), MAG, A.add, ["XX" + x, "PB"], ["l0" + x], -MAG, A.add)
        tt(nf("YY"), ps(yb, 64, 128), pad("l0"), A.mult, [wk(1), "l0" + x], ["YY" + x])
        tt(pad("cm"), ps(yb, 0, 64), nf("YY"), A.is_lt, [wk(1), "YY" + x, "PB"], ["cm" + x])
        grp(st(SL), [(mc("IEND"), nh("LP")), (mc("EN8"), T.ONE[:, 0:64])] + turn("l0", I) + turn("cm", M1),
            ["II", "IM1", "IEND", "EN8", "ONE", "LP" + x, "l0" + x, "cm" + x], [sk(SL)])
        if last:
            for i, (n, q, bias) in enumerate((("ya", "a", 1280.0), ("yb", "a", 1280.0), ("yl", "v", None))):
                yo = T.YO[:, 192 * s + 64 * i:192 * s + 64 * i + 64]
                move(q, yo, st((SA, SB, SL)[i]), [sk((SA, SB, SL)[i])], [n + x], bias)
                dma("sa"[i == 1], T[n][:, 64 * s:64 * s + 64], yo, [n + x], [], ("o2", 32) if i == 1 else ("o1", 64), 2300.0)
            return
        move("a", lst("LA", 0, 128), st(SA, 2), [sk(SA), sk(SB)], ["LA" + x, "LB" + x], 1280.0)
        move("a", nh("A16", 2), st(SA, 2), [sk(SA), sk(SB)], ["A16" + x, "B16" + x])
        move("a", nh("LL"), st(SL), [sk(SL)], ["LL" + x])
        grp(st(SBA), turn("b", mc("P8")) + turn("a", mc("M8")) + [(mc("EP8"), nh("BE")), (mc("EM8"), nh("AE"))], ["P8", "M8", "EP8", "EM8", "ab" + x, "AE" + x], [sk(SBA)])
        move("a", pad("eh", k=4), ps(xb, 128, 384), [wk(0), "PB"], ["e" + x])
        energies(ends(0, 0), ends(1, 0) + ends(2, 1), ["EK0", "EK1", "EK2", "EG" + x])

    for r in range(3):
        for s in range(2):
            lead[0] = s
            stream(r, s)
    if "o" not in ORDER:
        ORDER["ops"] = ops
        ORDER["o"] = arrange(ops)
    for i, other in ORDER["o"]:
        issue(*((ops[i][8] if other else ops[i])[:2] + ops[i][2:5]))
    for s in ("v", "a", "p", "gq"):
        g.wait_ge(T.sem[s], cnt[s])
    for s, n in (("snt", 48), ("o1", 64), ("o2", 32)):
        g.wait_ge(T.sem[s], n)
